import numpy as np, ml_dtypes
CORES = [51,54,179,182]
N = 4
BF = ml_dtypes.bfloat16
def gentries(a):
    return np.ascontiguousarray(a.reshape(8, 16, -1).transpose(0, 2, 1)).reshape(8, -1)
def gtable(e):
    e = np.asarray(e); return np.ascontiguousarray(e.reshape(8, -1, 16).transpose(0, 2, 1)).reshape(128, -1).astype(np.int32)
NV, S, TOP, G = 1024, 256, 128, 64
K, K2, LIM, ST, RO = 256, 96, 520, 144, 5
M = NV - S - TOP; W = NV + (N - 1) * G
FANS = np.array([1, 2, 2, 2, 3, 3, 4, 6, 16])
def twin(d):
    g = np.arange(8)
    return (7 - g, (8 - g) % 8, g)[(d - 1) % 3]
def wire(rng, cut):
    p = np.zeros((16, NV), np.int64)
    for c, im, f in cut:
        b = np.stack([rng.permutation(im) for _ in range(f)])
        p[:, c] = b[rng.permutation(np.concatenate([np.arange(f), rng.integers(0, f, 16 - f)]))]
    return p
def layered(rng, fans):
    pool = np.argsort(np.concatenate([np.arange(NV), rng.integers(0, NV, W - NV)]) + rng.random(W))
    lag = int(rng.choice(np.array([0, 32, 64, 128]))); cut = []
    for a in range(0, NV - S, 128):
        o = S + a + rng.permutation(128); im = rng.permutation(pool[lag + a:lag + a + 128])
        for i in range(0, 128, 32): cut.append((o[i:i + 32], im[i:i + 32], int(rng.choice(fans))))
    rest = rng.permutation(np.concatenate([pool[:lag], pool[lag + NV - S:]])); o = rng.permutation(S)
    for i in range(0, S, 64): cut.append((o[i:i + 64], rest[i:i + 64], int(rng.choice(fans))))
    return wire(rng, cut)
def flat(rng, pool):
    p = np.zeros((16, NV), np.int64)
    for k in range(16):
        o = rng.permutation(pool)[:TOP]; p[k, NV - TOP:] = o
        p[k, :NV - TOP] = rng.permutation(np.setdiff1d(np.arange(W), o))[:NV - TOP]
    return p
def aim(p, k, v, u):
    w = np.nonzero(p[k] == u)[0]
    if len(w): p[k, w[0]] = p[k, v]
    p[k, v] = u
def sweep(rng, miss):
    o = rng.permutation(NV); p = np.zeros((16, NV), np.int64); x = S + int(rng.integers(0, M))
    for k in range(16):
        a = o[k::16]; v = NV - TOP + rng.permutation(TOP - 3)[:len(a)]
        p[k, v] = a; p[k, np.setdiff1d(np.arange(NV), v)] = rng.permutation(np.setdiff1d(np.arange(W), a))[:NV - len(a)]
        if miss: aim(p, k, S, x)
    return p
def back(rng, p, share):
    c = np.full((16, W), NV); np.put_along_axis(c, p, np.broadcast_to(np.arange(NV), (16, NV)), 1); mix = rng.random((16, NV))
    return np.where(mix < share, c[:, :NV], np.where(mix < share + 0.03, rng.integers(0, NV, (16, NV)), NV))
def presence(rng, extra):
    h = np.ones(NV, bool); h[:S] = rng.random(S) > 0.01; h[NV - TOP:] = rng.random(TOP) < 0.2; h[S:NV - TOP] = False
    h[S:NV - TOP] = rng.permutation(M) < LIM + extra - int(np.sum(h))
    return h
def parity(rng):
    return 2 * rng.integers(0, 8, (16, NV)) + rng.integers(0, 2, (1, NV))
def start(rng):
    y = rng.integers(0, 16, (N, 8, 16, NV)); m = rng.integers(0, 2, (N, 8, NV)); b = np.argsort(rng.random((N, 8, NV)), axis=-1)[..., :(N - 1) * G].copy()
    y = np.where(rng.random((N, 8, 1, NV)) < 0.15, 2 * (y >> 1) + rng.integers(0, 2, (N, 8, 1, NV)), y)
    p = np.zeros((N, 8, 16, NV), np.int64); c = p.copy(); h = np.zeros((N, 8, NV), bool)
    for q in range(N):
        for g in range(8):
            p[q, g] = layered(rng, FANS); c[q, g] = back(rng, p[q, g], float(rng.choice(np.array([0.5, 0.8, 0.95]))))
            h[q, g] = presence(rng, int(rng.choice(np.array([-60, 0, 40, 120, K2, 2 * K2]))))
    return y, p, c, m, b, h
def pack(y, p, c, m, b, h):
    y = np.where(h[:, :, None, :], y, -1)
    return {"y0": np.ascontiguousarray(y.reshape(N, 128, NV)).astype(np.float32).astype(BF), "pr": np.ascontiguousarray(p.reshape(N, 128, NV)).astype(np.int32), "co": np.ascontiguousarray(c.reshape(N, 128, NV)).astype(np.int32),
            "mo": np.ascontiguousarray(m).astype(np.int32), "bd": np.stack([gtable(a) for a in b])}
def setup_inputs(rng):
    return pack(*start(rng))
def setup_inputs_spread(rng):
    y, p, c, m, b, h = start(rng)
    y = (rng.random((N, 8, 16, NV)) * rng.choice(np.array([1, 2, 3, 8, 16]), (N, 8, 1, NV))).astype(np.int64); y = np.where(rng.random((N, 8, 1, NV)) < 0.5, 15 - y, y)
    m = (rng.random((N, 8, NV)) < rng.choice(np.array([0.03, 0.5, 0.97]), (N, 8, 1))).astype(np.int64)
    for q in range(N):
        for g in range(1, 8, 2):
            o = rng.permutation(NV); im = rng.permutation(W)[:NV]
            p[q, g] = wire(rng, [(o[i:i + 64], im[i:i + 64], int(rng.choice(np.array([2, 2, 3, 5, 16])))) for i in range(0, NV, 64)])
            c[q, g] = np.where(rng.random((16, NV)) < rng.random((1, NV)) * 0.4, rng.integers(0, NV, (16, NV)), NV)
            h[q, g] = rng.random(NV) < float(rng.choice(np.array([0.1, 0.5, 0.8, 0.95])))
    return pack(y, p, c, m, b, h)
def setup_inputs_ends(rng):
    y, p, c, m, b, h = start(rng)
    kind = rng.integers(0, 5, (N, 8, 1, NV)); one = np.arange(16)[:, None] == rng.integers(0, 16, (N, 8, 1, NV)); rnd = rng.random((N, 8, 16, NV)) < 0.75
    odd = np.where(kind == 0, True, np.where(kind == 1, ~one, np.where(kind == 2, one, rnd)))
    y = np.where(odd, 15, 0); y[:, :, :, 1] = 15; y[:, :, :, 2] = 0
    B = (N - 1) * G // 2; both = np.concatenate([np.arange(B), np.arange(NV - B, NV)])
    for q in range(N):
        for g in range(8):
            pp, hh = p[q, g], h[q, g]; b[q, g] = rng.permutation(both)
            if g == 6: hh[:] = True
            if g == 4:
                hh[:] = True; hh[S:NV - TOP] = rng.permutation(M) < LIM + K2 * RO - 1 - S - TOP
                own = [S + int(v) for v in np.nonzero(hh[S:NV - TOP])[0][:8]]
                for i in range(8):
                    v = own[i]; m[q, g, v] = 1; y[q, g, :, v] = np.where(np.arange(16) <= i, 15, 0)
                    for k in range(16): aim(pp, k, v, v if k == (2 * i + 1) % 16 else 16 + i + 8 * (k % 2))
            if g == 2:
                hh[:] = False; hh[:S] = q % 2 == 0
                if q % 2 == 1: pp[:] = sweep(rng, q % 4 == 3)
            if g not in (2, 4, 6): hh[1] = True; hh[2] = True; hh[NV - 1] = False
            if g % 2 == 1: hh[0] = False; hh[NV - 2] = False; aim(pp, 0, 0, 0); aim(pp, 1, NV - 2, 0)
            for k in range(16): aim(pp, k, NV - 1, 1 + k % 2)
            aim(pp, 15, NV - 3, W - 1)
            z = rng.random((1, NV)); mix = np.where(rng.random((16, NV)) < 0.5, 0, NV)
            c[q, g] = np.where(z < 0.5, NV, np.where(z < 0.75, mix, np.where(z < 0.8, 0, back(rng, pp, 0.95))))
            c[q, g, :, 0] = NV; c[q, g, :, NV - 1] = 0
    return pack(y, p, c, m, b, h)
def setup_inputs_corners(rng):
    y, p, c, m, b, h = start(rng); fixed = np.concatenate([np.arange(S), np.arange(NV - TOP, NV)])
    for q in range(N):
        for g in range(8):
            pp, hh = p[q, g], h[q, g]
            if g < 3:
                dl = (g + q) % 3 - 1; hh[:] = True; m[q, g] = 0
                ta = NV - TOP + 1 + rng.permutation(TOP - 2)[:TOP - 18]; nb = K + dl - (TOP - 17); bs = S + rng.permutation(M)[:nb]; na = len(ta)
                hh[ta] = False; hh[bs] = False; hh[NV - TOP] = False; hh[NV - 1] = False
                for j in range(max(na, nb)): aim(pp, j // min(na, nb), int(ta[j % na]), int(bs[j % nb]))
                for k in range(16):
                    aim(pp, k, NV - TOP, 16 + k); aim(pp, k, NV - 1, NV - TOP if k == 0 else k)
                c[q, g] = back(rng, pp, 0.1); c[q, g, 15] = np.where(rng.random(NV) < 0.5, NV - 1, NV)
            if g == 3:
                y[q, g] = parity(rng); hh[:] = True; hh[S:NV - TOP] = rng.permutation(M) < LIM + K2 * RO - 1 + q % 2 - S - TOP
                c[q, g] = NV; b[q, g] = rng.permutation(fixed)[:(N - 1) * G]
            if g == 4:
                y[q, g] = parity(rng); hh[:] = True; hh[S:NV - TOP] = rng.permutation(M) < LIM + q % 4 - S - TOP
                b[q, g] = rng.permutation(fixed)[:(N - 1) * G]
            if g == 5: hh[:] = False; hh[:S] = q % 2 == 1
            if g == 6:
                for i in range(8): aim(pp, i, NV - 1 - i, NV - 1 - i); hh[NV - 1 - i] = False
                z = rng.integers(0, 4, (1, NV)); last = np.where(np.arange(16)[:, None] == 15, NV - 1, NV)
                c[q, g] = np.where(z == 0, NV - 1, np.where(z == 1, last, np.where(z == 2, np.arange(NV)[None, :], NV)))
            if g == 7:
                p[q, g] = layered(rng, np.array([1, 16])); c[q, g] = back(rng, p[q, g], 0.9); h[q, g] = presence(rng, 0)
    return pack(y, p, c, m, b, h)
def setup_inputs_calm(rng):
    y, p, c, m, b, h = start(rng)
    for q in range(N):
        for g in range(6):
            few = (g + q) % 4; pp, hh = p[q, g], h[q, g]; y[q, g] = parity(rng); hh[:] = True
            for t in range(RO):
                for i in range(few):
                    v = NV - 1 - (4 * t + i); hh[v] = False
                    for k in range(16): aim(pp, k, v, v + 4 if k == 0 and t > 0 else 16 + 4 * t + i + 32 * (k % 2))
            hh[S:NV - TOP] = rng.permutation(M) < LIM - S - (TOP - few * RO)
            c[q, g] = NV; c[q, g, 15] = np.where(rng.random(NV) < 0.3, NV - 1 - 4 * (RO - 1), NV); c[q, g, 0] = np.where(rng.random(NV) < 0.2, NV - 5, NV)
            b[q, g] = rng.permutation(np.concatenate([np.arange(S), np.arange(NV - TOP, NV - 4 * RO)]))[:(N - 1) * G]
        pp, hh = p[q, 6], h[q, 6]; y[q, 6] = parity(rng); u = S + (ST * (RO - 1)) % M; x = NV - RO
        o = np.setdiff1d(np.arange(S, NV - TOP), np.array([u])); hh[:] = True; hh[x:] = False; hh[S:NV - TOP] = False
        hh[rng.permutation(o)[:LIM - S - (TOP - RO)]] = True
        for i in range(RO + 1):
            v = NV - 1 - i if i < RO else u
            for k in range(16):
                a = 16 + i + 32 * (k % 2)
                if k == 0 and 0 < i < RO - 1: a = NV - i
                if k == 0 and i == RO - 1: a = u
                if k == 1 and i == RO - 1: a = NV + 2 * G
                if k == 0 and i == RO: a = NV - RO + 1
                aim(pp, k, v, a)
        c[q, 6] = NV; c[q, 6, 3] = np.where(rng.random(NV) < 0.3, x, NV); c[q, 6, :, u] = NV
        b[q, 6] = rng.permutation(np.concatenate([np.arange(S), np.arange(NV - TOP, x)]))[:(N - 1) * G]; b[q, 6, 2 * G] = u
    return pack(y, p, c, m, b, h)
def setup_inputs_crowd(rng):
    y, p, c, m, b, h = start(rng)
    for q in range(N):
        for g in range(8):
            if g % 4 == 0: p[q, g] = layered(rng, np.array([1]))
            if g % 4 == 1: p[q, g] = layered(rng, np.array([16])); h[q, g] = presence(rng, -60); h[q, g, :S] = True
            if g % 4 > 1:
                h[q, g] = rng.random(NV) < 0.8; h[q, g, :S] = True; h[q, g, NV - TOP:] = False; bs = S + rng.permutation(M)[:2 * TOP]
            if g % 4 == 2:
                p[q, g] = flat(rng, np.arange(S)); h[q, g, bs[:TOP]] = False
                for i in range(TOP): aim(p[q, g], i % 16, NV - TOP + i, int(bs[i]))
            if g % 4 == 3:
                p[q, g] = flat(rng, bs); h[q, g, bs] = False
                for i in range(0, TOP, 2): aim(p[q, g], (i >> 1) % 16, NV - TOP + i, i)
            z = rng.random((1, NV)); last = np.where(np.arange(16)[:, None] == 15, NV - 1, NV)
            c[q, g] = np.where(z < 0.2, NV - 1, np.where(z < 0.4, last, back(rng, p[q, g], 0.6)))
    return pack(y, p, c, m, b, h)
def check_inputs(d):
    bad = []
    for k, lo, hi in (("y0", -1, 15), ("pr", 0, W - 1), ("co", 0, NV), ("mo", 0, 1), ("bd", 0, NV - 1)):
        a = np.asarray(d[k]).astype(np.float64)
        if not (np.min(a) >= lo and np.max(a) <= hi): bad.append("range of " + k)
    y = np.asarray(d["y0"]).astype(np.float32).reshape(N, 8, 16, NV); h = y < 0
    if np.any(y != np.floor(y)): bad.append("whole numbers of y0")
    if np.any(np.any(h, axis=2) != np.all(h, axis=2)): bad.append("absent in all 16 branches or in none, of y0")
    s = np.sort(np.asarray(d["pr"]), axis=2)
    if np.any(s[:, :, 1:] == s[:, :, :-1]): bad.append("different numbers in a row of pr")
    s = np.sort(np.stack([gentries(a) for a in np.asarray(d["bd"])]), axis=2)
    if np.any(s[:, :, 1:] == s[:, :, :-1]): bad.append("different entries of a group of bd")
    return bad
def ghosts(y, bl):
    s = np.zeros((N, 8, 16, (N - 1) * G), np.int64)
    for r in range(N):
        for d in range(1, N):
            q = r ^ d; h = twin(d)
            s[r, :, :, (d - 1) * G:d * G] = np.take_along_axis(y[q][h], bl[q][h, d - 1][:, None, :], 2)
    return s
def reference(y0, pr, co, mo, bd):
    y = y0.astype(np.float32).astype(np.int64).reshape(N, 8, 16, NV); ph = np.zeros((N, 8, 16, NV), np.int64)
    p = pr.astype(np.int64).reshape(N, 8, 16, NV); c = co.astype(np.int64).reshape(N, 8, 16, NV); m = mo.astype(np.int64)
    bl = np.stack([gentries(a) for a in bd]).astype(np.int64).reshape(N, 8, N - 1, G)
    want = (y[:, :, 0] < 0) & (np.arange(NV) >= NV - TOP)
    for t in range(RO):
        gh = ghosts(y, bl); a = np.concatenate([y, gh], axis=3)
        tl = np.argsort(~want, axis=2, kind="stable")[..., :K]; live = np.take_along_axis(want, tl, 2)
        pt = np.take_along_axis(p, tl[:, :, None, :], 3)
        v = np.take_along_axis(a, pt.reshape(N, 8, 1, 16 * K), 3).reshape(N, 8, 16, 16, K)
        gone = v[:, :, 0] < 0; diff = np.max(v, axis=3) - np.min(v, axis=3); named = np.zeros((N, 8, W), bool)
        i, j, k, s = np.nonzero(gone & live[:, :, None, :]); named[i, j, pt[i, j, k, s]] = True
        i, j, s = np.nonzero(live & ~np.any(gone, axis=2)); u = tl[i, j, s]
        y[i, j, :, u] = diff[i, j, :, s]; ph[i, j, :, u] = 0
        want = want | named[:, :, :NV]; want[i, j, u] = False
        here = y[:, :, 0] >= 0; e = np.clip(np.add.reduce(here.astype(np.int64), axis=2) - LIM, 0, K2)
        ring = S + (np.arange(M) + ST * t) % M
        rl = ring[np.argsort(~here[:, :, ring], axis=2, kind="stable")[..., :K2]]; live = np.take_along_axis(here, rl, 2)
        wx = np.concatenate([want, np.zeros((N, 8, 1), bool)], axis=2)
        ct = np.take_along_axis(c, rl[:, :, None, :], 3).reshape(N, 8, 16 * K2)
        held = np.any(np.take_along_axis(wx, ct, 2).reshape(N, 8, 16, K2), axis=2)
        fr = (live & ~held).astype(np.int64); go = (fr == 1) & (np.add.accumulate(fr, axis=2) - fr < e[:, :, None])
        has = np.concatenate([here, gh[:, :, 0] >= 0], axis=2); pt = np.take_along_axis(p, rl[:, :, None, :], 3).reshape(N, 8, 16 * K2)
        dirty = ~np.all(np.take_along_axis(has, pt, 2).reshape(N, 8, 16, K2), axis=2)
        old = np.take_along_axis(y, rl[:, :, None, :], 3)
        f = np.where(dirty[:, :, None, :], (old & 1) * np.take_along_axis(m, rl, 2)[:, :, None, :], 0); cnt = np.add.reduce(f, axis=2)
        i, j, s = np.nonzero(go); u = rl[i, j, s]
        ph[i, j, :, u] = f[i, j, :, s]; y[i, j, :, u] = -1
        want[i, j, u] = (cnt[i, j, s] >= 1) & (cnt[i, j, s] <= 15)
        lost = y[:, :, 0] < 0
        for r in range(N):
            for d in range(1, N):
                q = r ^ d; h = twin(d)[:, None]; ix = bl[q][twin(d), d - 1]
                want[q, h, ix] = want[q, h, ix] | (named[r, :, NV + (d - 1) * G:NV + d * G] & lost[q][h, ix])
    return {"yy": y.reshape(N, 128, NV).astype(np.float32).astype(BF), "yf": ph.reshape(N, 128, NV).astype(np.float32).astype(BF), "yw": want.astype(np.float32).astype(BF)}

@@ -1,0 +1,469 @@
+from concourse.bass import DstId, RemoteDMATransfer
+from concourse.mybir import AluOpType as A, ActivationFunctionType as F
+
+NV, NG, RO, K2 = 1024, 192, 5, 96
+DUMP = NV + NG
+YW_ = DUMP + 256
+OFF = 32
+SILU_ONE = 1.278464542761074
+S_COLS = 176
+S_CUTS = (128, 192)
+V_FIRST = 80
+H_V = 40
+D_S = (64, 0)
+T0_K, T0_S = 3, 48
+ABSENT = 1.0 - 2.0 ** -8
+TAG = 3.0 * 2.0 ** -10
+V_K = (1, 1, 1)
+ENG = (4, 4, 4)
+
+
+def _sb(n, d):
+    return ("sbuf", [128, n], d)
+
+
+SCRATCH = {
+    "Y": _sb(YW_, "bfloat16"), "Y0": _sb(NV, "bfloat16"), "Y2": _sb(896, "bfloat16"),
+    "PR": _sb(1312, "int32"), "CO": _sb(1312, "int32"), "MO": _sb(1312, "int32"), "PRF": _sb(NV, "float32"),
+    "BDI": _sb(12, "int32"), "BD": _sb(12, "uint16"), "AB": _sb(NG, "bfloat16"), "NN": _sb(NG, "bfloat16"),
+    "BW": _sb(NG, "bfloat16"),
+    "WV": _sb(3104, "float32"), "WS": _sb(3104, "float32"), "RW": _sb(2720, "float32"),
+    "C": _sb(256, "float16"), "CT": _sb(256, "float16"), "LS": _sb(256, "uint16"), "L": _sb(256, "uint16"),
+    "C0": _sb(128, "float32"), "C1": _sb(128, "float32"), "DS": _sb(128, "float32"),
+    "G": _sb(4096, "bfloat16"), "MX": _sb(4096, "bfloat16"), "MN": _sb(4096, "bfloat16"),
+    "K2": _sb(1024, "bfloat16"), "K3": _sb(1024, "bfloat16"),
+    "R1": _sb(256, "bfloat16"), "R3": _sb(256, "bfloat16"), "RES": _sb(272, "bfloat16"),
+    "W": _sb(64, "float16"), "E": _sb(64, "float16"), "WT": _sb(64, "float16"), "TT": _sb(64, "float16"),
+    "NT": _sb(64, "float16"), "TF": _sb(64, "float32"),
+    "RK": _sb(64, "uint16"), "RK2": _sb(64, "uint16"), "RR": _sb(40, "uint16"),
+    "IDS": _sb(640, "float32"), "SIL": _sb(256, "float32"),
+    "PI": _sb(1, "int32"), "PI2": _sb(1, "int32"), "CC": _sb(1, "float32"), "SC": _sb(1, "float32"), "E1": _sb(1, "float32"),
+    "I16": _sb(K2, "float32"), "KA": _sb(K2, "float32"), "KB": _sb(K2, "float32"), "KC": _sb(K2, "float32"),
+    "KD": _sb(K2, "float32"),
+    "DG1": _sb(K2, "float32"), "CL": _sb(6, "uint16"), "COL": _sb(K2, "uint16"), "PRL": _sb(K2, "uint16"),
+    "DG": _sb(1536, "bfloat16"), "HG": _sb(1536, "bfloat16"), "HS": _sb(1536, "bfloat16"),
+    "ALF": _sb(K2, "bfloat16"), "TAG": _sb(256, "bfloat16"), "MV": _sb(YW_, "bfloat16"),
+    "OI": _sb(K2, "int32"), "OD": _sb(K2, "int32"), "OM": _sb(K2, "bfloat16"),
+    "FF": _sb(K2, "bfloat16"), "T1": _sb(K2, "bfloat16"), "CD": _sb(K2, "bfloat16"), "OC": _sb(K2, "bfloat16"),
+    "EL": _sb(K2, "float32"), "EF": _sb(K2, "float32"), "CF": _sb(K2, "float32"),
+    "KP": _sb(K2, "bfloat16"), "KO": _sb(K2, "bfloat16"),
+    "PH": _sb(1312, "bfloat16"), "OY": _sb(NV, "bfloat16"), "OZ": _sb(NV, "bfloat16"), "OF": _sb(NV, "bfloat16"),
+    "OW": _sb(NV, "bfloat16"),
+    "ONE": _sb(160, "bfloat16"), "ONF": _sb(128, "float32"),
+    "Z0": _sb(160, "bfloat16"), "Z1": _sb(160, "bfloat16"), "ZS": _sb(160, "bfloat16"), "ID": _sb(128, "bfloat16"),
+    "B1": _sb(128, "bfloat16"), "NB": _sb(128, "bfloat16"), "NU": _sb(128, "bfloat16"), "NI": _sb(128, "bfloat16"),
+    "P1": _sb(128, "float32"), "P2": _sb(128, "float32"), "P3": _sb(128, "float32"),
+}
+for _t in range(RO):
+    SCRATCH["M%d" % _t] = _sb(YW_, "float32")
+    for _n in ("BN", "LG", "LN", "BV"):
+        SCRATCH["%s%d" % (_n, _t)] = _sb(NG, "float32")
+SCRATCH["BN%d" % RO] = _sb(NG, "float32")
+for _n in ("PD", "PK", "PL", "PG", "PN", "PS", "PY0", "PY1"):
+    SCRATCH[_n] = ("psum", [128, 512], "float32")
+
+SEMAPHORES = (["v", "s", "p", "g", "sent", "d_y", "d_bd", "d_pt", "d_pr", "d_co", "d_mo", "o_y", "o_f", "o_w"]
+              + ["gh%d" % t for t in range(RO)] + ["nt%d" % t for t in range(RO)])
+
+
+def rank_program(g, core, T, topo):
+    rank = T.rank_of(core)
+    if rank is None:
+        return
+    V, S, P, Q = g.vector, g.scalar, g.tensor, g.sync
+    eng = {"v": V, "s": S, "p": P, "g": g, "q": Q}
+    count = {"v": 0, "s": 0, "p": 0, "g": 0}
+    known = {e: {} for e in eng}
+    clock = {}
+    wrote, read = {}, {}
+
+    def need(e, mark):
+        sem, val = mark
+        if known[e].get(sem, 0) >= val:
+            return
+        eng[e].wait_ge(T.sem[sem], val)
+        known[e][sem] = val
+        for k, x in clock.get(mark, {}).items():
+            if known[e].get(k, 0) < x:
+                known[e][k] = x
+
+    def order(e, r, w):
+        marks = {}
+        for m in [m for x in r for m in wrote.get(x, [])] + [m for x in w for m in wrote.get(x, []) + read.get(x, [])]:
+            marks[m[0]] = max(marks.get(m[0], 0), m[1])
+        for m in marks.items():
+            need(e, m)
+
+    def done(e, mark, r, w):
+        clock[mark] = dict(known[e])
+        for x in w:
+            wrote[x] = [mark]
+            read[x] = []
+        for x in r:
+            read[x] = [m for m in read.get(x, []) if m[0] != mark[0]] + [mark]
+
+    def op(e, r, w, call):
+        r, w = r.split(), w.split()
+        order(e, r, w)
+        count[e] += 1
+        call().then_inc(T.sem[e], 1)
+        done(e, (e, count[e]), r, w)
+
+    def mm(r, w, items):
+        def call():
+            for it in items[:-1]:
+                P.matmul(*it)
+            return P.matmul(*items[-1])
+        op("p", r, w, call)
+
+    dmas = {}
+
+    def dma(e, sem, r, w, pairs):
+        r, w = r.split(), w.split()
+        order(e, r, w)
+        for o, i in pairs:
+            eng[e].dma_start(o, i).then_inc(T.sem[sem], 16)
+        dmas[sem] = 16 * len(pairs)
+        done(e, (sem, dmas[sem]), r, w)
+
+    peers = [T.cores[rank ^ d] for d in (1, 2, 3)]
+    masks, used = [0, 0, 0], []
+    for j in sorted(range(3), key=lambda j: len(topo.engines(core, peers[j]))):
+        free = [x for x in topo.engines(core, peers[j]) if x not in used][:ENG[j]]
+        used.extend(free)
+        masks[j] = sum(1 << x for x in free)
+    sent = [0]
+
+    def exchange(r, src, base, land, sem, more=None):
+        order("g", r.split(), [])
+        tr = []
+        for j in range(3):
+            rid, pid = topo.addr(peers[j], core)
+            srcs = [src[:, base + 64 * j:base + 64 * j + 64]] + ([] if more is None else [more[:, 64 * j:64 * j + 64]])
+            tr.append(RemoteDMATransfer(dst_ids=[DstId(rid=rid, pnc=pid)], dma_engine_mask=masks[j], remote_sem=T.sem[sem],
+                                        srcs=srcs, dsts=[T[land][:, 64 * j:64 * j + 64]], alu_op=0 if more is None else 2))
+        g.remote_dma_fused(tr, local_sem=T.sem.sent)
+        sent[0] += sum(ENG)
+        wrote[land] = [(sem, sum(ENG))]
+
+    def ts(r, w, out, in0, s1, o1, s2=None, o2=None):
+        if o2 is None:
+            op("v", r, w, lambda: V.tensor_scalar(out, in0, s1, None, o1))
+        else:
+            op("v", r, w, lambda: V.tensor_scalar(out, in0, s1, s2, o1, o2))
+
+    def tt(r, w, out, a, b, o):
+        op("v", r, w, lambda: V.tensor_tensor(out, a, b, o))
+
+    def cp(r, w, out, a):
+        op("v", r, w, lambda: V.tensor_copy(out, a))
+
+    def fill(w, out, c):
+        op("v", "", w, lambda: V.memset(out, c))
+
+    def scan(r, w, out, a, b, o0, o1):
+        op("v", r, w, lambda: V.tensor_tensor_scan(out, a, b, 0.0, o0, o1))
+
+    def act(r, w, out, a, f, bias=None, scale=None):
+        if bias is None and scale is None:
+            op("s", r, w, lambda: S.activation(out, a, f))
+        else:
+            op("s", r, w, lambda: S.activation(out, a, f, bias=bias, scale=scale))
+
+    def iota(w, out, pat, base, cm=0, flag=True):
+        if flag:
+            op("g", "", w, lambda: g.iota(out, pat, base, cm, allow_small_or_imprecise_dtypes=True))
+        else:
+            op("g", "", w, lambda: g.iota(out, pat, base, cm))
+
+    def sel(r, w, out, a, pat, cmp, base, cm):
+        op("g", r, w, lambda: g.affine_select(out, a, pat, cmp, 0.0, base, cm))
+
+    Y = T.Y
+    YA = "Yo Yt Yg Yd"
+    Ywin = Y[:, 0:YW_]
+    perm = [T.P1, T.P2, T.P3]
+    PC = T.PG[:, 256:256 + K2]
+    CL = T.CL[:, :]
+
+    def turn(lands, ps):
+        lands = lands.split()
+        mm(" ".join(lands) + " P1 P2a P2b P3", ps,
+           [(T[ps][:, 64 * j:64 * j + 64], perm[j][:, :], T[x][:, 64 * j:64 * j + 64], x == lands[0], x == lands[-1])
+            for j in range(3) for x in lands])
+
+    def diagonal():
+        mm("Yo Yt ZS", "PD", [(T.PD[:, 0:64], T.ZS[:, 16 - c:144 - c], Y[:, c:NV:16], c == 0, c == 15) for c in range(16)])
+
+    def places(parts, extra):
+        scan("W", "E", T.E[:, :], T.W[:, :], T.W[:, :], A.add, A.max)
+        for j, (a, b, x) in enumerate(parts):
+            tt("W TT", "WT%d" % j, T.WT[:, a:b], T.W[:, a:b], T.TT[:, x:x + b - a], A.mult)
+        items = []
+        for a, b, x in parts:
+            o = T.PK[:, a:b]
+            items += [(o, T.NI[:, :], T.NT[:, x:x + b - a], True, False), (o, T.NU[:, :], T.W[:, a:b], False, False),
+                      (o, T.B1[:, :], T.E[:, a:b], False, False), (o, T.NI[:, :], T.WT[:, a:b], False, True)]
+        mm("W E WT0 WT1 NT B1 NB NU NI", "PK", extra + items)
+
+    def phases():
+        tt("FF CL", "PH", T.PH[:, :].indirect(CL), T.FF[:, :], T.FF[:, :], A.add)
+
+    dma("q", "d_y", "", "Y0", [(T.Y0[:, :], T.y0[:, :])])
+    dma("s", "d_bd", "", "BDI", [(T.BDI[:, :], T.bd[:, :])])
+    dma("s", "d_pt", "", "PRt", [(T.PR[:, 896:NV], T.pr[:, 896:NV])])
+    dma("q", "d_pr", "", "PRb", [(T.PR[:, 0:896], T.pr[:, 0:896])])
+    dma("q", "d_co", "", "COa", [(T.CO[:, 0:NV], T.co[:, :])])
+    dma("q", "d_mo", "", "MOa", [(T.MO[i:128:16, 0:NV], T.mo[:, :]) for i in range(16)])
+
+    fill("ONE", T.ONE[:, :], 1.0)
+    fill("ONF", T.ONF[:, :], 1.0)
+    sel("ONE", "ID", T.ID[:, :], T.ONE[:, 0:128], [[-1, 128]], A.is_equal, 0, 1)
+    iota("DS", T.DS[:, :], [[1, 128]], DUMP)
+    for h, z in ((0, "Z0"), (1, "Z1")):
+        sel("ONE", z, T[z][:, :], T.ONE[:, :], [[-32, 5], [984, 2], [-1, 16]], A.is_equal, 16 - 1000 * (1 - h), 1)
+    sel("ONF", "P1", T.P1[:, :], T.ONF[:, :], [[16, 8], [-1, 16]], A.is_equal, -112, 1)
+    sel("ONF", "P2b", T.P2[:, 16:128], T.ONF[:, 16:128], [[16, 7], [-1, 16]], A.is_equal, -112, 1)
+    fill("K2", T.K2[:, :], -32.0)
+    fill("K3", T.K3[:, :], 32.0)
+    fill("M0", T.M0[:, :], 0.0)
+    fill("K2", T.K2[:, 0:1024:16], 32.0)
+    fill("K3", T.K3[:, 0:1024:16], -32.0)
+    ts("ID", "NI", T.NI[:, :], T.ID[:, :], -1.0, A.mult)
+    cp("BDI", "BD", T.BD[:, :], T.BDI[:, :])
+    ts("Y0 BD", "BN0", T.BN0[:, :], T.Y0[:, 0:NV].indirect(T.BD[:, :]), 2.0, A.add)
+    exchange("BN0", T.BN0, 0, "LG0", "gh0")
+    sel("ONF", "P2a", T.P2[:, 0:16], T.ONF[:, 0:16], [[-1, 16]], A.is_equal, 0, 1)
+    sel("ONF", "P3", T.P3[:, :], T.ONF[:, :], [[-1, 128]], A.is_equal, 0, 1)
+    iota("PI", T.PI[:, :], [[0, 1]], 0, 1, False)
+    iota("TF", T.TF[:, :], [[16, 64]], NV)
+    iota("I16", T.I16[:, :], [[0, 6], [1, 16]], 0)
+    sel("ONE", "B1", T.B1[:, :], T.ONE[:, 0:128], [[-16, 8], [0, 16]], A.is_ge, 0, 1)
+    sel("ONE", "ZS", T.ZS[:, :], T.ONE[:, :], [[-16, 10], [999, 16]], A.is_equal, 16, 1)
+    sel("B1", "B1", T.B1[:, :], T.B1[:, :], [[16, 8], [0, 16]], A.is_ge, 15, -1)
+
+    act("Y0", "Y2", T.Y2[:, :], T.Y0[:, 0:896], F.Relu, 0.0, ABSENT - 1.0)
+    mm("Y0 Y2 ID NI", "PY0 PY1",
+       [(T.PY0[:, :], T.ID[:, :], T.Y0[:, 0:512], True, False), (T.PY0[:, :], T.NI[:, :], T.Y2[:, 0:512], False, True),
+        (T.PY1[:, 0:384], T.ID[:, :], T.Y0[:, 512:896], True, False), (T.PY1[:, 0:384], T.NI[:, :], T.Y2[:, 512:896], False, True)])
+    act("PY0", "Ya", Y[:, 0:512], T.PY0[:, :], F.Identity, 2.0, 1.0)
+    act("PY1 Ya", "Yo", Y[:, 512:896], T.PY1[:, 0:384], F.Identity, 2.0, 1.0)
+
+    for t in range(RO):
+        M, Mn = T["M%d" % t], "M%d" % t
+        last = t == RO - 1
+        ns = 128 if t == 0 else 256
+        off = 0.0 if t == 0 else float(OFF)
+        if t == 0:
+            ts("Y0", "C0", T.C0[:, :], T.Y0[:, 896:NV], 0.0, A.is_ge, 2000.0, A.mult)
+            fill("SIL", T.SIL[:, :], SILU_ONE)
+            tt("C0 PRt", "C1", T.C1[:, :], T.C0[:, :], T.PR[:, 896:NV], A.max)
+            fill("Yd", Y[:, DUMP:YW_], 0.0)
+            tt("C1 DS", "C", T.C[:, 0:128], T.C1[:, :], T.DS[:, :], A.min)
+            ts("Y0", "Yt", Y[:, 896:NV], T.Y0[:, 896:NV], 2.0, A.add)
+        else:
+            ts("PD", "W", T.W[:, :], T.PD[:, 0:64], 1.0, A.is_equal)
+            places([(0, 64, 0)], [])
+            ts("BN%d" % t, "AB", T.AB[:, :], T["BN%d" % t][:, :], 2.0, A.is_lt)
+            ts("PK", "RK", T.RK[:, :], T.PK[:, 0:64], -1.0, A.add)
+            act("PRF RK", "WS", T.WS[:, :].indirect(T.RK[:, 32:64]), T.PRF[:, 512:NV], F.Silu)
+            cp("PRF RK", "WV", T.WV[:, :].indirect(T.RK[:, 0:32]), T.PRF[:, 0:512])
+            turn("LG%d" % t, "PG")
+            ts("PG", "Yg", Y[:, NV:DUMP], T.PG[:, 0:NG], 1.5, A.max)
+            tt("WV WS", "C", T.C[:, :], T.WV[:, 0:256], T.WS[:, 0:256], A.min)
+        if t == 0:
+            op("v", "C", "CT", lambda: V.transpose(T.CT[:, 0:ns], T.C[:, 0:ns]))
+            ts("C", "LS", T.LS[:, 0:ns], T.C[:, 0:ns], -off, A.add)
+        else:
+            ts("C", "LS", T.LS[:, 0:ns], T.C[:, 0:ns], -off, A.add)
+            op("v", "C", "CT", lambda: V.transpose(T.CT[:, 0:ns], T.C[:, 0:ns]))
+        kc = ns // 16
+        items = []
+        for b in range(ns // 32):
+            for h in (0, 1):
+                for gg in (0, 1):
+                    x = 16 - 16 * (gg - h)
+                    items.append((T.PL[:, 2 * b + h:ns:kc], T["Z%d" % h][:, x:x + 128],
+                                  T.CT[:, 32 * b + 16 * gg:32 * b + 16 * gg + 16], gg == 0, gg == 1))
+        mm("CT Z0 Z1", "PL", items)
+
+        def gather(e, a, b):
+            names = " ".join("G%d" % j for j in range(a // 16, (b + 15) // 16))
+            o, i = T.G[:, 16 * a:16 * b], Ywin.indirect(T.LS[:, a:b])
+            if e == "v":
+                ts(YA + " LS", names, o, i, -1.75, A.add)
+            else:
+                act(YA + " LS", names, o, i, F.Identity, -1.75, 1.0)
+
+        def naming(a, b):
+            for k in range(a, b):
+                act("L SIL", Mn, M[:, :].indirect(T.L[:, kc * k:kc * k + kc]), T.SIL[:, 0:ns], F.Silu)
+
+        def naming_v(j):
+            for k in range(16 - sum(V_K[j:]), 16 - sum(V_K[j + 1:])):
+                cp("L TAG", "MV", T.MV[:, :].indirect(T.L[:, 16 * k:16 * k + 16]), T.TAG[:, :])
+
+        if t == 0:
+            fill("ALF", T.ALF[:, :], ABSENT)
+            fill("RESz", T.RES[:, 256:272], 0.0)
+            ts("BN0", "AB", T.AB[:, :], T.BN0[:, :], 2.0, A.is_lt)
+            ts("PL", "L", T.L[:, 0:ns], T.PL[:, 0:ns], 0.0, A.add)
+            naming(0, T0_K)
+            ts("PI", "PI2", T.PI2[:, :], T.PI[:, :], 15, A.bitwise_and)
+            turn("LG0", "PG")
+            cp("PI2", "CC", T.CC[:, :], T.PI2[:, :])
+            ts("B1", "NB", T.NB[:, :], T.B1[:, :], -1.0, A.mult)
+            sel("NB", "NU", T.NU[:, :], T.NB[:, :], [[-1, 128]], A.is_gt, 0, 1)
+            iota("IDS", T.IDS[:, :], [[1, 640]], 256)
+            iota("RW", T.RW[:, 0:K2], [[1, K2]], DUMP)
+            for n in ("PR", "CO", "MO"):
+                iota(n + "z", T[n][:, NV:1312], [[0, 288]], 0, 0, False)
+            ts("TF CC", "TT", T.TT[:, :], T.TF[:, :], T.CC[:, :], A.add)
+            ts("TF CC", "NT", T.NT[:, :], T.TF[:, :], T.CC[:, :], A.add, -1.0, A.mult)
+            ts("I16 CC", "KB", T.KB[:, :], T.I16[:, :], T.CC[:, :], A.subtract, 1.0, A.is_equal)
+            ts("I16 CC", "KA", T.KA[:, :], T.I16[:, :], T.CC[:, :], A.not_equal)
+            ts("PG", "Yg", Y[:, NV:DUMP], T.PG[:, 0:NG], 1.5, A.max)
+            if T0_S:
+                gather("s", ns - T0_S, ns)
+            naming(T0_K, 16)
+            gather("v", 0, ns - T0_S)
+        else:
+            cuts = [ns - S_COLS] + [x for x in S_CUTS if x > ns - S_COLS] + [ns]
+            for a, b in zip(cuts, cuts[1:]):
+                gather("s", a, b)
+            gather("v", 0, V_FIRST)
+            ts("PK", "RK2", T.RK2[:, :], T.PK[:, 0:64], -1.0, A.add, 256.0, A.min)
+            ts("PL", "L", T.L[:, 0:ns], T.PL[:, 0:ns], -off, A.add)
+            naming(0, 16 - sum(V_K))
+            naming_v(0)
+            if V_FIRST < ns - S_COLS:
+                gather("v", V_FIRST, ns - S_COLS)
+        if not last:
+            iota("WV", T.WV[:, 0:256], [[1, 256]], DUMP + OFF)
+            iota("WS", T.WS[:, 0:256], [[1, 256]], DUMP + OFF)
+            if t == 0:
+                iota("PH", T.PH[:, 256:896], [[0, 640]], 0)
+            else:
+                iota("M%d" % (t + 1), T["M%d" % (t + 1)][:, :], [[0, YW_]], 0)
+        else:
+            iota("OFz", T.OF[:, 0:256], [[0, 256]], 0)
+            iota("OFy", T.OF[:, 896:NV], [[0, 128]], 0)
+        if t == 0:
+            exchange(Mn, M, NV, "LN%d" % t, "nt%d" % t)
+            iota("M1", T.M1[:, :], [[0, YW_]], 0)
+
+        for j in range(ns // 64):
+            gs = " ".join("G%d" % x for x in range(4 * j, 4 * j + 4))
+            sl = slice(1024 * j, 1024 * j + 1024)
+            scan(gs + " K2", "MN%d" % j, T.MN[:, sl], T.K2[:, :], T.G[:, sl], A.max, A.min)
+            scan(gs + " K3", "MX%d" % j, T.MX[:, sl], T.K3[:, :], T.G[:, sl], A.min, A.max)
+            o, ends = T.PS[:, 128 + 64 * j:192 + 64 * j], slice(1024 * j + 15, 1024 * j + 1024, 16)
+            mm("MN%d MX%d ID NI" % (j, j), "PS", [(o, T.NI[:, :], T.MN[:, ends], True, False), (o, T.ID[:, :], T.MX[:, ends], False, True)])
+        ts(" ".join("MN%d" % j for j in range(ns // 64)), "R1", T.R1[:, 0:ns], T.MN[:, 15:16 * ns:16], 128.0, A.mult, 2.0, A.min)
+        tt("R1 PS", "RES", T.RES[:, 0:ns], T.PS[:, 128:128 + ns], T.R1[:, 0:ns], A.add)
+        if t == 0:
+            tt("RES Yt", "Yt", Y[:, 896:NV], T.RES[:, 0:128], Y[:, 896:NV], A.max)
+        else:
+            tt("RES RESz RK2 Yo Yt", "Yo Yt", Y[:, 0:NV], T.RES[:, :].indirect(T.RK2[:, :]), Y[:, 0:NV], A.max)
+
+        diagonal()
+        if t == 0:
+            ts("KB", "KC", T.KC[:, :], T.KB[:, :], 65536.0, A.mult)
+            ts("CC", "SC", T.SC[:, :], T.CC[:, :], 15.0, A.is_equal, 1.0 / 65536, A.max)
+            ts("PRb", "PRF", T.PRF[:, 0:512], T.PR[:, 0:512], OFF + 0.125, A.add)
+            tt("KA KC", "KD", T.KD[:, :], T.KA[:, :], T.KC[:, :], A.max)
+            fill("TAG", T.TAG[:, :], TAG)
+        else:
+            naming_v(1)
+        ts("PD", "W", T.W[:, :], T.PD[:, 0:64], 2.0, A.is_ge)
+        s0 = 16 + (9 * t) % 40
+        col = lambda j: T.PK[:, j:j + 1]
+        e_ = lambda j: T.E[:, j:j + 1]
+        extra = [(col(64), T.NB[:, :], e_(s0 - 1), True, True), (col(66), T.B1[:, :], e_(63), True, True)]
+        if s0 > 16:
+            extra += [(col(65), T.NB[:, :], e_(15), True, False), (col(65), T.B1[:, :], e_(55), False, False),
+                      (col(65), T.NB[:, :], e_(s0 - 1), False, True)]
+        places([(s0, 56, 0)] + ([(16, s0, 56 - s0)] if s0 > 16 else []), extra)
+        if t > 0:
+            naming_v(2)
+            mm("Yo Yt ID MV", "PY0 PY1",
+               [(T.PY0[:, :], T.ID[:, :], Y[:, 0:512], True, False), (T.PY0[:, :], T.ID[:, :], T.MV[:, 0:512], False, True),
+                (T.PY1[:, :], T.ID[:, :], Y[:, 512:NV], True, False), (T.PY1[:, :], T.ID[:, :], T.MV[:, 512:NV], False, True)])
+        else:
+            mm("Yo Yt ID", "PY0 PY1", [(T.PY0[:, :], T.ID[:, :], Y[:, 0:512], True, True),
+                                       (T.PY1[:, :], T.ID[:, :], Y[:, 512:NV], True, True)])
+            ts("PRt PRb PRF", "PRF", T.PRF[:, 512:NV], T.PR[:, 512:NV], OFF + 0.125, A.add)
+        ts("PK", "RR", T.RR[:, s0 - 16:40], T.PK[:, s0:56], col(64), A.add, -1.0, A.add)
+        if s0 > 16:
+            ts("PK", "RRb", T.RR[:, 0:s0 - 16], T.PK[:, 16:s0], col(65), A.add, -1.0, A.add)
+        ts("PK", "E1", T.E1[:, :], col(66), -519.0, A.add, 1.0, A.max)
+        cp("RR RRb IDS", "RW", T.RW[:, :].indirect(T.RR[:, :]), T.IDS[:, :])
+        scan("RW KD", "DG1", T.DG1[:, :], T.KD[:, :], T.RW[:, 0:K2], A.mult, A.add)
+        ts("RW E1", "EL", T.EL[:, :], T.RW[:, 0:K2], float(NV), A.is_lt, T.E1[:, :], A.mult)
+        if t > 0:
+            ts("MV", "BV%d" % t, T["BV%d" % t][:, :], T.MV[:, NV:DUMP], 0.0, A.is_gt)
+        ts("DG1 SC", "CL", CL, T.DG1[:, 15:K2:16], T.SC[:, :], A.mult)
+        cp("PRt PRb PRz CL", "PRL", T.PRL[:, :], T.PR[:, :].indirect(CL))
+        cp(YA + " CL", "OI", T.OI[:, :], Ywin.indirect(CL))
+        dv = K2 - D_S[min(t, 1)]
+        if dv < K2:
+            act(YA + " PRL", "DGs", T.DG[:, 16 * dv:1536], Ywin.indirect(T.PRL[:, dv:K2]), F.Relu, 4.0, -2.0)
+        ts(YA + " PRL", "DGv", T.DG[:, 0:16 * dv], Ywin.indirect(T.PRL[:, 0:dv]), 2.0, A.is_lt)
+        mm("DGv DGs ID", "PS", [(T.PS[:, 0:K2], T.ID[:, :], T.DG[:, k:1536:16], k == 0, k == 15) for k in range(16)])
+        if not last:
+            iota("RW", T.RW[:, 0:K2], [[1, K2]], DUMP)
+            if t > 0:
+                iota("MV", T.MV[:, :], [[0, YW_]], 0)
+        if t > 0:
+            exchange(Mn + " BV%d" % t, M, NV, "LN%d" % t, "nt%d" % t, T["BV%d" % t])
+        ts("OI", "OD", T.OD[:, :], T.OI[:, :], 1, A.bitwise_and)
+        cp("COa COz CL", "COL", T.COL[:, :], T.CO[:, :].indirect(CL))
+        tt("MOa MOz CL OD", "OM", T.OM[:, :], T.MO[:, :].indirect(CL), T.OD[:, :], A.mult)
+        ts("OI", "OC", T.OC[:, :], T.OI[:, :], -1.0, A.add)
+
+        tt("PY0 " + Mn, "Ya Yo", Y[:, 0:512], T.PY0[:, :], M[:, 0:512], A.max)
+        tt("PY1 " + Mn, "Yb Yt", Y[:, 512:NV], T.PY1[:, :], M[:, 512:NV], A.max)
+        wrote["Yo"] = wrote["Yt"]
+        act(YA + " COL", "HGs", T.HG[:, 16 * H_V:1536], Ywin.indirect(T.COL[:, H_V:K2]), F.Abs, -8192.0, 8192.0)
+        ts(YA + " COL", "HGv", T.HG[:, 0:16 * H_V], Ywin.indirect(T.COL[:, 0:H_V]), 1.0, A.not_equal, 32.0, A.mult)
+        tt("PS OM", "FF", T.FF[:, :], T.PS[:, 0:K2], T.OM[:, :], A.min)
+        mm("FF B1 ID ALF", "PG", [(PC, T.ID[:, :], T.ALF[:, :], True, False), (PC, T.B1[:, :], T.FF[:, :], False, True)])
+        scan("K2 HGv", "HSv", T.HS[:, 0:16 * H_V], T.K2[:, 0:16 * H_V], T.HG[:, 0:16 * H_V], A.max, A.min)
+        ts("PG", "T1", T.T1[:, :], PC, 16.5, A.is_lt, ABSENT, A.max)
+        scan("K2 HGs", "HSs", T.HS[:, 16 * H_V:1536], T.K2[:, 0:1536 - 16 * H_V], T.HG[:, 16 * H_V:1536], A.max, A.min)
+        tt("PG T1", "CD", T.CD[:, :], PC, T.T1[:, :], A.min)
+        hs = T.HS[:, 15:1536:16]
+        scan("HSv HSs", "CF", T.CF[:, :], hs, hs, A.add, A.max)
+        tt("HSv HSs EL", "EF", T.EF[:, :], hs, T.EL[:, :], A.mult)
+        turn("LN%d" % t, "PN")
+        tt("CF EF", "KP", T.KP[:, :], T.CF[:, :], T.EF[:, :], A.is_ge)
+        tt("KP OC", "KO", T.KO[:, :], T.KP[:, :], T.OC[:, :], A.mult)
+        tt("KO CD CL", YA, Ywin.indirect(CL), T.KO[:, :], T.CD[:, :], A.add)
+        tt("PN AB", "NN", T.NN[:, :], T.PN[:, 0:NG], T.AB[:, :], A.min)
+
+        bn = "BN%d" % (t + 1)
+        tt("Yo Yt BD NN", bn, T[bn][:, :], Y[:, 0:NV].indirect(T.BD[:, :]), T.NN[:, :], A.max)
+        if not last:
+            exchange(bn, T[bn], 0, "LG%d" % (t + 1), "gh%d" % (t + 1))
+            cp(bn + " BD", "Yo Yt", Y[:, 0:NV].indirect(T.BD[:, :]), T[bn][:, :])
+            diagonal()
+            if t == 0:
+                iota("MV", T.MV[:, :], [[0, YW_]], 0)
+        phases()
+        if last:
+            mm("PH ID", "PY0 PY1", [(T.PY0[:, :], T.ID[:, :], T.PH[:, 256:768], True, True),
+                                    (T.PY1[:, 0:128], T.ID[:, :], T.PH[:, 768:896], True, True)])
+
+    act("Yo Yt", "OZ", T.OZ[:, :], Y[:, 0:NV], F.Relu, -1.0, 1.0)
+    act("OZ", "OY", T.OY[:, :], T.OZ[:, :], F.Identity, -1.0, 1.0)
+    dma("s", "o_y", "OY", "", [(T.yy[:, :], T.OY[:, :])])
+    ts("Yo Yt", "OW", T.OW[:, :], Y[:, 0:NV], 1.0, A.is_equal)
+    ts(bn, "BW", T.BW[:, :], T[bn][:, :], 1.0, A.is_equal)
+    tt("PY0 Yo Yt", "OFa", T.OF[:, 256:768], T.PY0[:, :], Y[:, 256:768], A.is_gt)
+    tt("PY1 Yo Yt", "OFb", T.OF[:, 768:896], T.PY1[:, 0:128], Y[:, 768:896], A.is_gt)
+    cp("BW BD", "OW", T.OW[:, :].indirect(T.BD[:, :]), T.BW[:, :])
+    dma("q", "o_f", "OFa OFb OFz OFy", "", [(T.yf[:, :], T.OF[:, :])])
+    dma("q", "o_w", "OW", "", [(T.yw[:, :], T.OW[0:128:16, :])])
+    g.wait_ge(T.sem.sent, sent[0])
+    for sem, n in list(count.items()) + list(dmas.items()):
+        need("q", (sem, n))

@@ -4,17 +4,21 @@ from concourse.mybir import AluOpType as A, ActivationFunctionType as F
 NV, NG, RO, K2 = 1024, 192, 5, 96
 DUMP = NV + NG
 YW_ = DUMP + 256
+RING0, RINGN = 256, 640
+TW = DUMP + K2 - RING0
+SEG = 47
 OFF = 32
 SILU_ONE = 1.278464542761074
-S_COLS = 176
-S_CUTS = (128, 192)
-V_FIRST = 80
-H_V = 40
-D_S = (64, 0)
-T0_K, T0_S = 3, 48
-ABSENT = 1.0 - 2.0 ** -8
-TAG = 3.0 * 2.0 ** -10
-V_K = (1, 1, 1)
+ROUND = 65536.0 + 2.0 ** -7
+STEP = 20
+PIECE = 96
+S_SLOTS = (0, 112)
+V_FIRST = 64
+V_NAME = ((0, 0, 0, 0, 0), (16, 16, 16, 16, 0))
+T0_K = 2
+D_V = (16, 24)
+H_V = (((0, 48, 96),),) * 2
+FAR = NV + 256
 ENG = (4, 4, 4)
 
 
@@ -23,46 +27,46 @@ def _sb(n, d):
 
 
 SCRATCH = {
-    "Y": _sb(YW_, "bfloat16"), "Y0": _sb(NV, "bfloat16"), "Y2": _sb(896, "bfloat16"),
-    "PR": _sb(1312, "int32"), "CO": _sb(1312, "int32"), "MO": _sb(1312, "int32"), "PRF": _sb(NV, "float32"),
+    "YA": _sb(YW_, "bfloat16"), "YB": _sb(YW_, "bfloat16"), "Y0": _sb(NV, "bfloat16"),
+    "PR": _sb(DUMP + K2, "int32"), "CO": _sb(TW, "int32"), "MO": _sb(TW, "int32"), "PRF": _sb(NV, "float32"),
     "BDI": _sb(12, "int32"), "BD": _sb(12, "uint16"), "AB": _sb(NG, "bfloat16"), "NN": _sb(NG, "bfloat16"),
-    "BW": _sb(NG, "bfloat16"),
-    "WV": _sb(3104, "float32"), "WS": _sb(3104, "float32"), "RW": _sb(2720, "float32"),
+    "WV": _sb(FAR, "float32"), "WS": _sb(FAR, "float32"),
     "C": _sb(256, "float16"), "CT": _sb(256, "float16"), "LS": _sb(256, "uint16"), "L": _sb(256, "uint16"),
     "C0": _sb(128, "float32"), "C1": _sb(128, "float32"), "DS": _sb(128, "float32"),
-    "G": _sb(4096, "bfloat16"), "MX": _sb(4096, "bfloat16"), "MN": _sb(4096, "bfloat16"),
-    "K2": _sb(1024, "bfloat16"), "K3": _sb(1024, "bfloat16"),
-    "R1": _sb(256, "bfloat16"), "R3": _sb(256, "bfloat16"), "RES": _sb(272, "bfloat16"),
+    "G": _sb(4096, "float16"), "GS": _sb(4096, "bfloat16"), "MX": _sb(2048, "float16"), "MN": _sb(2048, "float16"),
+    "MXS": _sb(4096, "bfloat16"), "MNS": _sb(4096, "bfloat16"),
+    "K2": _sb(1024, "bfloat16"), "K3": _sb(1024, "bfloat16"), "R0": _sb(16 * PIECE, "float16"), "RA": _sb(16 * PIECE, "float16"),
+    "FL": _sb(256, "bfloat16"), "RES": _sb(FAR, "bfloat16"), "TWO": _sb(256, "bfloat16"),
     "W": _sb(64, "float16"), "E": _sb(64, "float16"), "WT": _sb(64, "float16"), "TT": _sb(64, "float16"),
-    "NT": _sb(64, "float16"), "TF": _sb(64, "float32"),
-    "RK": _sb(64, "uint16"), "RK2": _sb(64, "uint16"), "RR": _sb(40, "uint16"),
-    "IDS": _sb(640, "float32"), "SIL": _sb(256, "float32"),
-    "PI": _sb(1, "int32"), "PI2": _sb(1, "int32"), "CC": _sb(1, "float32"), "SC": _sb(1, "float32"), "E1": _sb(1, "float32"),
-    "I16": _sb(K2, "float32"), "KA": _sb(K2, "float32"), "KB": _sb(K2, "float32"), "KC": _sb(K2, "float32"),
-    "KD": _sb(K2, "float32"),
-    "DG1": _sb(K2, "float32"), "CL": _sb(6, "uint16"), "COL": _sb(K2, "uint16"), "PRL": _sb(K2, "uint16"),
-    "DG": _sb(1536, "bfloat16"), "HG": _sb(1536, "bfloat16"), "HS": _sb(1536, "bfloat16"),
-    "ALF": _sb(K2, "bfloat16"), "TAG": _sb(256, "bfloat16"), "MV": _sb(YW_, "bfloat16"),
-    "OI": _sb(K2, "int32"), "OD": _sb(K2, "int32"), "OM": _sb(K2, "bfloat16"),
-    "FF": _sb(K2, "bfloat16"), "T1": _sb(K2, "bfloat16"), "CD": _sb(K2, "bfloat16"), "OC": _sb(K2, "bfloat16"),
-    "EL": _sb(K2, "float32"), "EF": _sb(K2, "float32"), "CF": _sb(K2, "float32"),
-    "KP": _sb(K2, "bfloat16"), "KO": _sb(K2, "bfloat16"),
-    "PH": _sb(1312, "bfloat16"), "OY": _sb(NV, "bfloat16"), "OZ": _sb(NV, "bfloat16"), "OF": _sb(NV, "bfloat16"),
-    "OW": _sb(NV, "bfloat16"),
-    "ONE": _sb(160, "bfloat16"), "ONF": _sb(128, "float32"),
-    "Z0": _sb(160, "bfloat16"), "Z1": _sb(160, "bfloat16"), "ZS": _sb(160, "bfloat16"), "ID": _sb(128, "bfloat16"),
-    "B1": _sb(128, "bfloat16"), "NB": _sb(128, "bfloat16"), "NU": _sb(128, "bfloat16"), "NI": _sb(128, "bfloat16"),
-    "P1": _sb(128, "float32"), "P2": _sb(128, "float32"), "P3": _sb(128, "float32"),
+    "TF": _sb(64, "float32"), "RK": _sb(64, "uint16"), "OC": _sb(K2, "bfloat16"),
+    "WR": _sb(48, "bfloat16"), "ER": _sb(48, "bfloat16"), "SI": _sb(6 * SEG, "bfloat16"), "SG": _sb(6 * SEG, "bfloat16"),
+    "GT": _sb(6 * SEG, "bfloat16"), "D0": _sb(6 * SEG, "bfloat16"), "D1": _sb(6 * SEG, "bfloat16"), "D": _sb(6 * SEG, "bfloat16"),
+    "BS": _sb(6 * SEG, "bfloat16"), "BL": _sb(6, "uint16"), "RT": _sb(80, "bfloat16"), "SF": _sb(K2, "bfloat16"),
+    "X1": _sb(K2, "bfloat16"), "SIL": _sb(256, "float32"), "SN": _sb(64, "bfloat16"), "CN": _sb(1, "float32"),
+    "PI": _sb(1, "int32"), "PI2": _sb(1, "int32"), "CC": _sb(1, "float32"), "CX": _sb(1, "float32"),
+    "CL": _sb(6, "uint16"), "COL": _sb(K2, "uint16"), "PRL": _sb(K2, "uint16"),
+    "DG": _sb(1536, "bfloat16"), "HG": _sb(1536, "bfloat16"), "TAG": _sb(256, "bfloat16"),
+    "OI": _sb(K2, "int32"), "OD": _sb(K2, "int32"), "OM": _sb(K2, "bfloat16"), "FF": _sb(K2, "bfloat16"),
+    "A8": _sb(K2, "float32"), "CD": _sb(K2, "bfloat16"), "FR": _sb(K2, "bfloat16"), "CF": _sb(K2, "bfloat16"),
+    "U": _sb(K2, "bfloat16"), "KO": _sb(K2, "bfloat16"),
+    "PH": _sb(TW, "bfloat16"), "OY": _sb(NV, "bfloat16"), "OF": _sb(NV, "bfloat16"), "OW": _sb(64, "bfloat16"),
+    "ONE": _sb(288, "bfloat16"),
+    "Z0": _sb(160, "bfloat16"), "Z1": _sb(160, "bfloat16"), "ZS": _sb(160, "bfloat16"), "ZA": _sb(160, "bfloat16"),
+    "ZB": _sb(160, "bfloat16"), "ID": _sb(128, "bfloat16"), "I16": _sb(128, "bfloat16"), "IH": _sb(128, "bfloat16"),
+    "B0": _sb(128, "bfloat16"), "B1": _sb(128, "bfloat16"), "NB": _sb(128, "bfloat16"), "NU": _sb(128, "bfloat16"),
+    "NI": _sb(128, "bfloat16"), "BF": _sb(128, "float32"), "P1": _sb(128, "bfloat16"), "P2": _sb(128, "bfloat16"),
 }
 for _t in range(RO):
     SCRATCH["M%d" % _t] = _sb(YW_, "float32")
-    for _n in ("BN", "LG", "LN", "BV"):
-        SCRATCH["%s%d" % (_n, _t)] = _sb(NG, "float32")
-SCRATCH["BN%d" % RO] = _sb(NG, "float32")
-for _n in ("PD", "PK", "PL", "PG", "PN", "PS", "PY0", "PY1"):
+for _n in ("BN", "LG", "LN", "NM"):
+    SCRATCH[_n] = _sb(RO * NG, "bfloat16")
+for _t in range(RO + 1):
+    SCRATCH["MV%d" % _t] = _sb(YW_, "bfloat16")
+PSUM = ("PD", "PK", "PL", "PG", "PN", "PS", "PY0", "PY1")
+for _n in PSUM:
     SCRATCH[_n] = ("psum", [128, 512], "float32")
 
-SEMAPHORES = (["v", "s", "p", "g", "sent", "d_y", "d_bd", "d_pt", "d_pr", "d_co", "d_mo", "o_y", "o_f", "o_w"]
+SEMAPHORES = (["v", "s", "p", "g", "first", "sent", "d_y", "d_bd", "d_pt", "d_pr", "d_pa", "d_co", "d_mo", "o_a", "o_y", "o_f", "o_w"]
               + ["gh%d" % t for t in range(RO)] + ["nt%d" % t for t in range(RO)])
 
 
@@ -75,7 +79,16 @@ def rank_program(g, core, T, topo):
     count = {"v": 0, "s": 0, "p": 0, "g": 0}
     known = {e: {} for e in eng}
     clock = {}
-    wrote, read = {}, {}
+    log = {}
+
+    def c(name, a=0, b=None, step=1):
+        b = SCRATCH[name][1][1] if b is None else b
+        if step > 0:
+            return {"ap": T[name][:, a:b:step] if step > 1 else T[name][:, a:b], "at": (name, a, b)}
+        return {"ap": T[name][:, a:(b if b >= 0 else None):step], "at": (name, b + 1, a + 1)}
+
+    def ind(win, off):
+        return {"ap": win["ap"].indirect(off["ap"]), "at": win["at"], "off": off["at"]}
 
     def need(e, mark):
         sem, val = mark
@@ -87,44 +100,56 @@ def rank_program(g, core, T, topo):
             if known[e].get(k, 0) < x:
                 known[e][k] = x
 
-    def order(e, r, w):
+    def spans(outs, ins):
+        ins = [x for x in ins if isinstance(x, dict)]
+        return ([x["at"] for x in outs], [x["at"] for x in ins] + [x["off"] for x in outs + ins if "off" in x])
+
+    def order(e, w, r, more=False):
         marks = {}
-        for m in [m for x in r for m in wrote.get(x, [])] + [m for x in w for m in wrote.get(x, []) + read.get(x, [])]:
-            marks[m[0]] = max(marks.get(m[0], 0), m[1])
+        for (name, a, b), writes in [(x, True) for x in w] + [(x, False) for x in r]:
+            for lo, hi, m, wrote, q in log.get(name, []):
+                meet = lo < b and a < hi and (writes or wrote) and not (more and q == e and name in PSUM)
+                if meet or (name in PSUM and q != e):
+                    marks[m[0]] = max(marks.get(m[0], 0), m[1])
         for m in marks.items():
             need(e, m)
 
-    def done(e, mark, r, w):
+    def done(e, mark, w, r):
         clock[mark] = dict(known[e])
-        for x in w:
-            wrote[x] = [mark]
-            read[x] = []
-        for x in r:
-            read[x] = [m for m in read.get(x, []) if m[0] != mark[0]] + [mark]
+        for (name, a, b), writes in [(x, False) for x in r] + [(x, True) for x in w]:
+            old = log.get(name, [])
+            if name in PSUM:
+                old = [x for x in old if x[4] == e]
+            old = [x for x in old if not (a <= x[0] and x[1] <= b and (writes or (x[4] == e and not x[3] and x[2][0] == mark[0])))]
+            log[name] = old + [[a, b, mark, writes, e]]
 
-    def op(e, r, w, call):
-        r, w = r.split(), w.split()
-        order(e, r, w)
+    def op(e, outs, ins, call, more=False):
+        w, r = spans(outs, ins)
+        order(e, w, r, more)
         count[e] += 1
         call().then_inc(T.sem[e], 1)
-        done(e, (e, count[e]), r, w)
+        done(e, (e, count[e]), w, r)
 
-    def mm(r, w, items):
+    def raw(x):
+        return x["ap"] if isinstance(x, dict) else x
+
+    def mm(items, more=False):
         def call():
-            for it in items[:-1]:
-                P.matmul(*it)
-            return P.matmul(*items[-1])
-        op("p", r, w, call)
+            for o, l, r, a, b in items[:-1]:
+                P.matmul(o["ap"], l["ap"], r["ap"], a, b)
+            o, l, r, a, b = items[-1]
+            return P.matmul(o["ap"], l["ap"], r["ap"], a, b)
+        op("p", [x[0] for x in items], [x[1] for x in items] + [x[2] for x in items], call, more)
 
     dmas = {}
 
-    def dma(e, sem, r, w, pairs):
-        r, w = r.split(), w.split()
-        order(e, r, w)
+    def dma(e, sem, outs, ins, pairs):
+        w, r = spans(outs, ins)
+        order(e, w, r)
         for o, i in pairs:
             eng[e].dma_start(o, i).then_inc(T.sem[sem], 16)
         dmas[sem] = 16 * len(pairs)
-        done(e, (sem, dmas[sem]), r, w)
+        done(e, (sem, dmas[sem]), w, r)
 
     peers = [T.cores[rank ^ d] for d in (1, 2, 3)]
     masks, used = [0, 0, 0], []
@@ -134,336 +159,372 @@ def rank_program(g, core, T, topo):
         masks[j] = sum(1 << x for x in free)
     sent = [0]
 
-    def exchange(r, src, base, land, sem, more=None):
-        order("g", r.split(), [])
+    def exchange(src, land, t, sem):
+        order("g", [], [(src, NG * t, NG * t + NG)])
         tr = []
         for j in range(3):
             rid, pid = topo.addr(peers[j], core)
-            srcs = [src[:, base + 64 * j:base + 64 * j + 64]] + ([] if more is None else [more[:, 64 * j:64 * j + 64]])
-            tr.append(RemoteDMATransfer(dst_ids=[DstId(rid=rid, pnc=pid)], dma_engine_mask=masks[j], remote_sem=T.sem[sem],
-                                        srcs=srcs, dsts=[T[land][:, 64 * j:64 * j + 64]], alu_op=0 if more is None else 2))
-        g.remote_dma_fused(tr, local_sem=T.sem.sent)
-        sent[0] += sum(ENG)
-        wrote[land] = [(sem, sum(ENG))]
+            third = slice(NG * t + 64 * j, NG * t + 64 * j + 64)
+            tr.append(RemoteDMATransfer(dst_ids=[DstId(rid=rid, pnc=pid)], dma_engine_mask=masks[j], remote_sem=T.sem[sem + str(t)],
+                                        srcs=[T[src][:, third]], dsts=[T[land][:, third]], alu_op=0))
+        g.remote_dma_fused(tr, local_sem=T.sem["sent" if sent[0] else "first"])
+        sent[0] += 1
+        log[land] = [[NG * t, NG * t + NG, (sem + str(t), sum(ENG)), True, "far"]]
 
-    def ts(r, w, out, in0, s1, o1, s2=None, o2=None):
+    def ts(out, in0, s1, o1, s2=None, o2=None):
         if o2 is None:
-            op("v", r, w, lambda: V.tensor_scalar(out, in0, s1, None, o1))
+            op("v", [out], [in0, s1], lambda: V.tensor_scalar(out["ap"], in0["ap"], raw(s1), None, o1))
         else:
-            op("v", r, w, lambda: V.tensor_scalar(out, in0, s1, s2, o1, o2))
+            op("v", [out], [in0, s1, s2], lambda: V.tensor_scalar(out["ap"], in0["ap"], raw(s1), raw(s2), o1, o2))
 
-    def tt(r, w, out, a, b, o):
-        op("v", r, w, lambda: V.tensor_tensor(out, a, b, o))
+    def tt(out, a, b, o):
+        op("v", [out], [a, b], lambda: V.tensor_tensor(out["ap"], a["ap"], b["ap"], o))
 
-    def cp(r, w, out, a):
-        op("v", r, w, lambda: V.tensor_copy(out, a))
+    def cp(out, a):
+        op("v", [out], [a], lambda: V.tensor_copy(out["ap"], a["ap"]))
 
-    def fill(w, out, c):
-        op("v", "", w, lambda: V.memset(out, c))
+    def fill(out, x):
+        op("v", [out], [], lambda: V.memset(out["ap"], x))
 
-    def scan(r, w, out, a, b, o0, o1):
-        op("v", r, w, lambda: V.tensor_tensor_scan(out, a, b, 0.0, o0, o1))
+    def scan(out, a, b, o0, o1, first=0.0):
+        op("v", [out], [a, b, first], lambda: V.tensor_tensor_scan(out["ap"], a["ap"], b["ap"], raw(first), o0, o1))
 
-    def act(r, w, out, a, f, bias=None, scale=None):
-        if bias is None and scale is None:
-            op("s", r, w, lambda: S.activation(out, a, f))
+    def act(out, a, f, bias=None, scale=None, total=None):
+        if total is not None:
+            op("s", [out, total], [a], lambda: S.activation(out["ap"], a["ap"], f, bias=bias, scale=scale, accum_out=total["ap"]))
+        elif bias is None:
+            op("s", [out], [a], lambda: S.activation(out["ap"], a["ap"], f))
         else:
-            op("s", r, w, lambda: S.activation(out, a, f, bias=bias, scale=scale))
+            op("s", [out], [a], lambda: S.activation(out["ap"], a["ap"], f, bias=bias, scale=scale))
 
-    def iota(w, out, pat, base, cm=0, flag=True):
-        if flag:
-            op("g", "", w, lambda: g.iota(out, pat, base, cm, allow_small_or_imprecise_dtypes=True))
+    def iota(out, pat, base, cm=0):
+        if SCRATCH[out["at"][0]][2] == "int32":
+            op("g", [out], [], lambda: g.iota(out["ap"], pat, base, cm))
         else:
-            op("g", "", w, lambda: g.iota(out, pat, base, cm))
+            op("g", [out], [], lambda: g.iota(out["ap"], pat, base, cm, allow_small_or_imprecise_dtypes=True))
 
-    def sel(r, w, out, a, pat, cmp, base, cm):
-        op("g", r, w, lambda: g.affine_select(out, a, pat, cmp, 0.0, base, cm))
+    def sel(out, a, pat, cmp, base, cm, other=0.0):
+        op("g", [out], [a], lambda: g.affine_select(out["ap"], a["ap"], pat, cmp, other, base, cm))
 
-    Y = T.Y
-    YA = "Yo Yt Yg Yd"
-    Ywin = Y[:, 0:YW_]
-    perm = [T.P1, T.P2, T.P3]
-    PC = T.PG[:, 256:256 + K2]
-    CL = T.CL[:, :]
+    CL, BD = c("CL"), c("BD")
+    ID, NI, B1, NU = c("ID"), c("NI"), c("B1"), c("NU")
 
-    def turn(lands, ps):
-        lands = lands.split()
-        mm(" ".join(lands) + " P1 P2a P2b P3", ps,
-           [(T[ps][:, 64 * j:64 * j + 64], perm[j][:, :], T[x][:, 64 * j:64 * j + 64], x == lands[0], x == lands[-1])
-            for j in range(3) for x in lands])
+    def block(name, t):
+        return c(name, NG * t, NG * t + NG)
 
-    def diagonal():
-        mm("Yo Yt ZS", "PD", [(T.PD[:, 0:64], T.ZS[:, 16 - c:144 - c], Y[:, c:NV:16], c == 0, c == 15) for c in range(16)])
+    def turn(srcs, ps):
+        mm([(c(ps, 64 * j, 64 * j + 64), c(("P1", "P2", "ID")[j]), c(n, a + 64 * j, a + 64 * j + 64), i == 0, i == len(srcs) - 1)
+            for j in range(3) for i, (n, a) in enumerate(srcs)])
 
-    def places(parts, extra):
-        scan("W", "E", T.E[:, :], T.W[:, :], T.W[:, :], A.add, A.max)
-        for j, (a, b, x) in enumerate(parts):
-            tt("W TT", "WT%d" % j, T.WT[:, a:b], T.W[:, a:b], T.TT[:, x:x + b - a], A.mult)
-        items = []
-        for a, b, x in parts:
-            o = T.PK[:, a:b]
-            items += [(o, T.NI[:, :], T.NT[:, x:x + b - a], True, False), (o, T.NU[:, :], T.W[:, a:b], False, False),
-                      (o, T.B1[:, :], T.E[:, a:b], False, False), (o, T.NI[:, :], T.WT[:, a:b], False, True)]
-        mm("W E WT0 WT1 NT B1 NB NU NI", "PK", extra + items)
+    def border(name, t, shift):
+        act(block("BN", t), ind(c(name, 0, NV), BD), F.Relu, shift, 1.0)
+        exchange("BN", "LG", t, "gh")
+        act(c("AB"), block("BN", t), F.Relu, 0.003, -0.012)
 
-    def phases():
-        tt("FF CL", "PH", T.PH[:, :].indirect(CL), T.FF[:, :], T.FF[:, :], A.add)
+    def ghosts(name, t):
+        turn([("LG", NG * t)], "PG")
+        act(c(name, NV, DUMP), c("PG", 0, NG), F.Identity, 1.5, 1.0)
 
-    dma("q", "d_y", "", "Y0", [(T.Y0[:, :], T.y0[:, :])])
-    dma("s", "d_bd", "", "BDI", [(T.BDI[:, :], T.bd[:, :])])
-    dma("s", "d_pt", "", "PRt", [(T.PR[:, 896:NV], T.pr[:, 896:NV])])
-    dma("q", "d_pr", "", "PRb", [(T.PR[:, 0:896], T.pr[:, 0:896])])
-    dma("q", "d_co", "", "COa", [(T.CO[:, 0:NV], T.co[:, :])])
-    dma("q", "d_mo", "", "MOa", [(T.MO[i:128:16, 0:NV], T.mo[:, :]) for i in range(16)])
+    def diagonal(name, first, final, blocks=False):
+        mm([(c("PD", 0, 64), c("ZS", 16 - i, 144 - i), c(name, 64 * i, 64 * i + 64) if blocks else c(name, i, NV, 16),
+             first and i == 0, final and i == 15) for i in range(16)], not first)
 
-    fill("ONE", T.ONE[:, :], 1.0)
-    fill("ONF", T.ONF[:, :], 1.0)
-    sel("ONE", "ID", T.ID[:, :], T.ONE[:, 0:128], [[-1, 128]], A.is_equal, 0, 1)
-    iota("DS", T.DS[:, :], [[1, 128]], DUMP)
+    def wanted(out):
+        ts(out, c("PD", 0, 64), ROUND, A.add, ROUND + 1.0, A.is_equal)
+
+    def sums(out, name, a, b, lhs, first):
+        return [(out, lhs, c(name, 16 * a + k, 16 * b, 16), first and k == 0, k == 15) for k in range(16)]
+
+    def ring_table(t):
+        s0 = (9 * t) % 40
+        src = "D0"
+        if s0:
+            sel(c("D1"), c("D0"), [[0, 6], [1, SEG]], A.not_equal, -(39 - s0), 0, 39.0)
+            src = "D1"
+        sel(c("D"), c(src), [[0, 6], [1, SEG]], A.not_equal, -39, 0, float((s0 - 1) % 40 - 60))
+
+    dma("q", "d_y", [c("Y0")], [], [(T.Y0[:, :], T.y0[:, :])])
+    dma("s", "d_bd", [c("BDI")], [], [(T.BDI[:, :], T.bd[:, :])])
+    dma("s", "d_pt", [c("PR", 896, NV)], [], [(T.PR[:, 896:NV], T.pr[:, 896:NV])])
+
+    fill(c("ONE"), 1.0)
+    act(c("TAG"), c("ONE", 0, 256), F.Silu, 0.0, 0.00586)
+    sel(ID, c("ONE", 0, 128), [[-1, 128]], A.is_equal, 0, 1)
+    iota(c("DS"), [[1, 128]], DUMP)
     for h, z in ((0, "Z0"), (1, "Z1")):
-        sel("ONE", z, T[z][:, :], T.ONE[:, :], [[-32, 5], [984, 2], [-1, 16]], A.is_equal, 16 - 1000 * (1 - h), 1)
-    sel("ONF", "P1", T.P1[:, :], T.ONF[:, :], [[16, 8], [-1, 16]], A.is_equal, -112, 1)
-    sel("ONF", "P2b", T.P2[:, 16:128], T.ONF[:, 16:128], [[16, 7], [-1, 16]], A.is_equal, -112, 1)
-    fill("K2", T.K2[:, :], -32.0)
-    fill("K3", T.K3[:, :], 32.0)
-    fill("M0", T.M0[:, :], 0.0)
-    fill("K2", T.K2[:, 0:1024:16], 32.0)
-    fill("K3", T.K3[:, 0:1024:16], -32.0)
-    ts("ID", "NI", T.NI[:, :], T.ID[:, :], -1.0, A.mult)
-    cp("BDI", "BD", T.BD[:, :], T.BDI[:, :])
-    ts("Y0 BD", "BN0", T.BN0[:, :], T.Y0[:, 0:NV].indirect(T.BD[:, :]), 2.0, A.add)
-    exchange("BN0", T.BN0, 0, "LG0", "gh0")
-    sel("ONF", "P2a", T.P2[:, 0:16], T.ONF[:, 0:16], [[-1, 16]], A.is_equal, 0, 1)
-    sel("ONF", "P3", T.P3[:, :], T.ONF[:, :], [[-1, 128]], A.is_equal, 0, 1)
-    iota("PI", T.PI[:, :], [[0, 1]], 0, 1, False)
-    iota("TF", T.TF[:, :], [[16, 64]], NV)
-    iota("I16", T.I16[:, :], [[0, 6], [1, 16]], 0)
-    sel("ONE", "B1", T.B1[:, :], T.ONE[:, 0:128], [[-16, 8], [0, 16]], A.is_ge, 0, 1)
-    sel("ONE", "ZS", T.ZS[:, :], T.ONE[:, :], [[-16, 10], [999, 16]], A.is_equal, 16, 1)
-    sel("B1", "B1", T.B1[:, :], T.B1[:, :], [[16, 8], [0, 16]], A.is_ge, 15, -1)
-
-    act("Y0", "Y2", T.Y2[:, :], T.Y0[:, 0:896], F.Relu, 0.0, ABSENT - 1.0)
-    mm("Y0 Y2 ID NI", "PY0 PY1",
-       [(T.PY0[:, :], T.ID[:, :], T.Y0[:, 0:512], True, False), (T.PY0[:, :], T.NI[:, :], T.Y2[:, 0:512], False, True),
-        (T.PY1[:, 0:384], T.ID[:, :], T.Y0[:, 512:896], True, False), (T.PY1[:, 0:384], T.NI[:, :], T.Y2[:, 512:896], False, True)])
-    act("PY0", "Ya", Y[:, 0:512], T.PY0[:, :], F.Identity, 2.0, 1.0)
-    act("PY1 Ya", "Yo", Y[:, 512:896], T.PY1[:, 0:384], F.Identity, 2.0, 1.0)
+        sel(c(z), c("ONE", 0, 160), [[-32, 5], [984, 2], [-1, 16]], A.is_equal, 16 - 1000 * (1 - h), 1)
+    fill(c("M0", 0, DUMP), 0.0)
+    fill(c("SIL"), SILU_ONE)
+    cp(BD, c("BDI"))
+    fill(c("R0"), 0.0)
+    border("Y0", 0, 0.5)
+    need("q", ("first", sum(ENG)))
+    dma("q", "d_pr", [c("PR", RING0, 896)], [], [(T.PR[:, RING0:896], T.pr[:, RING0:896])])
+    dma("q", "d_co", [c("CO", 0, RINGN)], [], [(T.CO[:, 0:RINGN], T.co[:, RING0:896])])
+    dma("q", "d_mo", [c("MO", 0, RINGN)], [], [(T.MO[i:128:16, 0:RINGN], T.mo[:, RING0:896]) for i in range(16)])
+    dma("q", "d_pa", [c("PR", 0, RING0)], [], [(T.PR[:, 0:RING0], T.pr[:, 0:RING0])])
+    sel(c("P1"), c("ONE", 0, 128), [[16, 8], [-1, 16]], A.is_equal, -112, 1)
+    sel(c("P2", 16, 128), c("ONE", 16, 128), [[16, 7], [-1, 16]], A.is_equal, -112, 1)
+    sel(c("P2", 0, 16), c("ONE", 0, 16), [[-1, 16]], A.is_equal, 0, 1)
+    iota(c("PI"), [[0, 1]], 0, 1)
+    sel(c("ZS"), c("ONE", 0, 160), [[-16, 10], [999, 16]], A.is_equal, 16, 1)
+    sel(c("B0"), c("ONE", 0, 128), [[-16, 8], [0, 16]], A.is_ge, 0, 1)
+    sel(B1, c("B0"), [[16, 8], [0, 16]], A.is_ge, 15, -1)
+    iota(c("SI"), [[16, 6], [0, SEG]], 0)
+    iota(c("SF"), [[1, K2]], 0)
+    iota(c("D1"), [[0, 6 * SEG]], -1)
+    sel(c("D0"), c("D1"), [[0, 6], [1, SEG]], A.not_equal, -(SEG - 1), 0, 66.0)
+    ring_table(0)
+    act(c("YA", 0, 896), c("Y0", 0, 896), F.Identity, 2.0, 1.0021)
 
     for t in range(RO):
-        M, Mn = T["M%d" % t], "M%d" % t
-        last = t == RO - 1
+        M, MV, MW = "M%d" % t, "MV%d" % t, "MV%d" % (t + 1)
+        Y, YN = ("YA", "YB")[t % 2], ("YB", "YA")[t % 2]
+        last, later = t == RO - 1, min(t, 1)
         ns = 128 if t == 0 else 256
-        off = 0.0 if t == 0 else float(OFF)
-        if t == 0:
-            ts("Y0", "C0", T.C0[:, :], T.Y0[:, 896:NV], 0.0, A.is_ge, 2000.0, A.mult)
-            fill("SIL", T.SIL[:, :], SILU_ONE)
-            tt("C0 PRt", "C1", T.C1[:, :], T.C0[:, :], T.PR[:, 896:NV], A.max)
-            fill("Yd", Y[:, DUMP:YW_], 0.0)
-            tt("C1 DS", "C", T.C[:, 0:128], T.C1[:, :], T.DS[:, :], A.min)
-            ts("Y0", "Yt", Y[:, 896:NV], T.Y0[:, 896:NV], 2.0, A.add)
-        else:
-            ts("PD", "W", T.W[:, :], T.PD[:, 0:64], 1.0, A.is_equal)
-            places([(0, 64, 0)], [])
-            ts("BN%d" % t, "AB", T.AB[:, :], T["BN%d" % t][:, :], 2.0, A.is_lt)
-            ts("PK", "RK", T.RK[:, :], T.PK[:, 0:64], -1.0, A.add)
-            act("PRF RK", "WS", T.WS[:, :].indirect(T.RK[:, 32:64]), T.PRF[:, 512:NV], F.Silu)
-            cp("PRF RK", "WV", T.WV[:, :].indirect(T.RK[:, 0:32]), T.PRF[:, 0:512])
-            turn("LG%d" % t, "PG")
-            ts("PG", "Yg", Y[:, NV:DUMP], T.PG[:, 0:NG], 1.5, A.max)
-            tt("WV WS", "C", T.C[:, :], T.WV[:, 0:256], T.WS[:, 0:256], A.min)
-        if t == 0:
-            op("v", "C", "CT", lambda: V.transpose(T.CT[:, 0:ns], T.C[:, 0:ns]))
-            ts("C", "LS", T.LS[:, 0:ns], T.C[:, 0:ns], -off, A.add)
-        else:
-            ts("C", "LS", T.LS[:, 0:ns], T.C[:, 0:ns], -off, A.add)
-            op("v", "C", "CT", lambda: V.transpose(T.CT[:, 0:ns], T.C[:, 0:ns]))
+        off = float(OFF * later)
+        nv = ns - S_SLOTS[later]
         kc = ns // 16
+        if t == 0:
+            ts(c("C0"), c("Y0", 896, NV), 0.0, A.is_ge, 2000.0, A.mult)
+            tt(c("C1"), c("C0"), c("PR", 896, NV), A.max)
+            tt(c("C", 0, 128), c("C1"), c("DS"), A.min)
+        else:
+            wanted(c("W"))
+            scan(c("E"), c("W"), c("W"), A.add, A.max)
+            tt(c("WT"), c("W"), c("TT"), A.mult)
+            o = c("PK", 0, 64)
+            mm([(o, ID, c("TT"), True, False), (o, NU, c("W"), False, False), (o, B1, c("E"), False, False),
+                (o, NI, c("WT"), False, True)])
+            ts(c("RK"), o, -1.0, A.add)
+            act(ind(c("WS"), c("RK", 32, 64)), c("PRF", 512, NV), F.Silu)
+            cp(ind(c("WV"), c("RK", 0, 32)), c("PRF", 0, 512))
+            ghosts(Y, t)
+            tt(c("C"), c("WV", 0, 256), c("WS", 0, 256), A.min)
+            ts(c("LS"), c("C"), -off, A.add)
+        op("v", [c("CT", 0, ns)], [c("C", 0, ns)], lambda: V.transpose(T.CT[:, 0:ns], T.C[:, 0:ns]))
         items = []
         for b in range(ns // 32):
             for h in (0, 1):
                 for gg in (0, 1):
                     x = 16 - 16 * (gg - h)
-                    items.append((T.PL[:, 2 * b + h:ns:kc], T["Z%d" % h][:, x:x + 128],
-                                  T.CT[:, 32 * b + 16 * gg:32 * b + 16 * gg + 16], gg == 0, gg == 1))
-        mm("CT Z0 Z1", "PL", items)
+                    items.append((c("PL", 2 * b + h, ns, kc), c("Z%d" % h, x, x + 128),
+                                  c("CT", 32 * b + 16 * gg, 32 * b + 16 * gg + 16), gg == 0, gg == 1))
+        mm(items)
 
-        def gather(e, a, b):
-            names = " ".join("G%d" % j for j in range(a // 16, (b + 15) // 16))
-            o, i = T.G[:, 16 * a:16 * b], Ywin.indirect(T.LS[:, a:b])
-            if e == "v":
-                ts(YA + " LS", names, o, i, -1.75, A.add)
-            else:
-                act(YA + " LS", names, o, i, F.Identity, -1.75, 1.0)
+        def gather(a, b):
+            while a < b:
+                x = min(b, (a // PIECE + 1) * PIECE)
+                tt(c("G", 16 * a, 16 * x), ind(c(Y), c("LS", a, x)), c("RA", 16 * (a % PIECE), 16 * (a % PIECE + x - a)), A.add)
+                a = x
 
-        def naming(a, b):
-            for k in range(a, b):
-                act("L SIL", Mn, M[:, :].indirect(T.L[:, kc * k:kc * k + kc]), T.SIL[:, 0:ns], F.Silu)
+        names = V_NAME[later]
+        at = [ns - sum(names)]
+        marks = [MV] if t or sum(names) else []
+
+        def naming(e, a, b):
+            while a < b:
+                x = min(b, (a // kc + 1) * kc)
+                if e == "s":
+                    act(ind(c(M), c("L", a, x)), c("SIL", 0, 16 * (x - a)), F.Silu)
+                else:
+                    cp(ind(c(MV), c("L", a, x)), c("TAG", 0, 16 * (x - a)))
+                a = x
 
         def naming_v(j):
-            for k in range(16 - sum(V_K[j:]), 16 - sum(V_K[j + 1:])):
-                cp("L TAG", "MV", T.MV[:, :].indirect(T.L[:, 16 * k:16 * k + 16]), T.TAG[:, :])
+            naming("v", at[0], at[0] + names[j])
+            at[0] += names[j]
 
         if t == 0:
-            fill("ALF", T.ALF[:, :], ABSENT)
-            fill("RESz", T.RES[:, 256:272], 0.0)
-            ts("BN0", "AB", T.AB[:, :], T.BN0[:, :], 2.0, A.is_lt)
-            ts("PL", "L", T.L[:, 0:ns], T.PL[:, 0:ns], 0.0, A.add)
-            naming(0, T0_K)
-            ts("PI", "PI2", T.PI2[:, :], T.PI[:, :], 15, A.bitwise_and)
-            turn("LG0", "PG")
-            cp("PI2", "CC", T.CC[:, :], T.PI2[:, :])
-            ts("B1", "NB", T.NB[:, :], T.B1[:, :], -1.0, A.mult)
-            sel("NB", "NU", T.NU[:, :], T.NB[:, :], [[-1, 128]], A.is_gt, 0, 1)
-            iota("IDS", T.IDS[:, :], [[1, 640]], 256)
-            iota("RW", T.RW[:, 0:K2], [[1, K2]], DUMP)
-            for n in ("PR", "CO", "MO"):
-                iota(n + "z", T[n][:, NV:1312], [[0, 288]], 0, 0, False)
-            ts("TF CC", "TT", T.TT[:, :], T.TF[:, :], T.CC[:, :], A.add)
-            ts("TF CC", "NT", T.NT[:, :], T.TF[:, :], T.CC[:, :], A.add, -1.0, A.mult)
-            ts("I16 CC", "KB", T.KB[:, :], T.I16[:, :], T.CC[:, :], A.subtract, 1.0, A.is_equal)
-            ts("I16 CC", "KA", T.KA[:, :], T.I16[:, :], T.CC[:, :], A.not_equal)
-            ts("PG", "Yg", Y[:, NV:DUMP], T.PG[:, 0:NG], 1.5, A.max)
-            if T0_S:
-                gather("s", ns - T0_S, ns)
-            naming(T0_K, 16)
-            gather("v", 0, ns - T0_S)
+            ts(c("LS", 0, ns), c("C", 0, ns), 0.0, A.add)
+            ts(c(Y, 896, NV), c("Y0", 896, NV), 2.0, A.add)
+            fill(c("R0", 0, None, 16), STEP / 2.0)
+            fill(c(Y, DUMP, YW_ - 16), 0.0)
+            ts(c("L", 0, ns), c("PL", 0, ns), 0.0, A.add)
+            naming("s", 0, T0_K * kc)
+            fill(c(Y, YW_ - 16, YW_), 1.0)
+            scan(c("RA"), c("R0"), c("R0"), A.add, A.add, -float(STEP * (PIECE // 2 + 1)))
+            ghosts(Y, 0)
+            naming("s", T0_K * kc, at[0])
+            ts(NI, ID, -1.0, A.mult)
+            fill(c("TWO"), 2.0)
+            if marks:
+                fill(c("MV0", 0, DUMP), 0.0)
+            gather(0, nv)
+            sel(c("ZA"), c("ONE", 0, 160), [[-16, 10], [-999, 16]], A.is_ge, 16, 1)
+            sel(c("ZB"), c("ZA"), [[16, 10], [0, 16]], A.is_ge, -1, -1)
+            ts(c("NB"), B1, -1.0, A.mult)
+            sel(NU, c("NB"), [[-1, 128]], A.is_gt, 0, 1)
+            iota(c("PR", NV), [[0, DUMP + K2 - NV]], 0)
+            iota(c("CO", RINGN), [[0, TW - RINGN]], YW_ - 1)
+            iota(c("MO", RINGN), [[0, TW - RINGN]], 0)
+            fill(c(YN, NV, YW_ - 16), 1.5)
+            fill(c(YN, YW_ - 16, YW_), 1.0)
         else:
-            cuts = [ns - S_COLS] + [x for x in S_CUTS if x > ns - S_COLS] + [ns]
-            for a, b in zip(cuts, cuts[1:]):
-                gather("s", a, b)
-            gather("v", 0, V_FIRST)
-            ts("PK", "RK2", T.RK2[:, :], T.PK[:, 0:64], -1.0, A.add, 256.0, A.min)
-            ts("PL", "L", T.L[:, 0:ns], T.PL[:, 0:ns], -off, A.add)
-            naming(0, 16 - sum(V_K))
-            naming_v(0)
-            if V_FIRST < ns - S_COLS:
-                gather("v", V_FIRST, ns - S_COLS)
-        if not last:
-            iota("WV", T.WV[:, 0:256], [[1, 256]], DUMP + OFF)
-            iota("WS", T.WS[:, 0:256], [[1, 256]], DUMP + OFF)
-            if t == 0:
-                iota("PH", T.PH[:, 256:896], [[0, 640]], 0)
+            if nv < ns:
+                act(c("GS", 16 * nv, 16 * ns), ind(c(Y), c("LS", nv, ns)), F.Identity, 0.0, 1.0)
+            gather(0, V_FIRST)
+            ts(c("L"), c("PL", 0, ns), -off, A.add)
+            naming("s", 0, at[0])
+            gather(V_FIRST, nv)
+            ring_table(t)
+            if not last:
+                iota(c("WV", 0, 256), [[1, 256]], DUMP + OFF)
+                iota(c("WS", 0, 256), [[1, 256]], DUMP + OFF)
+            iota(c(MW, 0, DUMP), [[0, DUMP]], 0)
+            if not last:
+                iota(c("M%d" % (t + 1), 0, DUMP), [[0, DUMP]], 0)
             else:
-                iota("M%d" % (t + 1), T["M%d" % (t + 1)][:, :], [[0, YW_]], 0)
-        else:
-            iota("OFz", T.OF[:, 0:256], [[0, 256]], 0)
-            iota("OFy", T.OF[:, 896:NV], [[0, 128]], 0)
-        if t == 0:
-            exchange(Mn, M, NV, "LN%d" % t, "nt%d" % t)
-            iota("M1", T.M1[:, :], [[0, YW_]], 0)
+                iota(c("OF", 0, RING0), [[0, RING0]], 0)
+                iota(c("OF", 896, NV), [[0, 128]], 0)
+        naming_v(0)
 
-        for j in range(ns // 64):
-            gs = " ".join("G%d" % x for x in range(4 * j, 4 * j + 4))
-            sl = slice(1024 * j, 1024 * j + 1024)
-            scan(gs + " K2", "MN%d" % j, T.MN[:, sl], T.K2[:, :], T.G[:, sl], A.max, A.min)
-            scan(gs + " K3", "MX%d" % j, T.MX[:, sl], T.K3[:, :], T.G[:, sl], A.min, A.max)
-            o, ends = T.PS[:, 128 + 64 * j:192 + 64 * j], slice(1024 * j + 15, 1024 * j + 1024, 16)
-            mm("MN%d MX%d ID NI" % (j, j), "PS", [(o, T.NI[:, :], T.MN[:, ends], True, False), (o, T.ID[:, :], T.MX[:, ends], False, True)])
-        ts(" ".join("MN%d" % j for j in range(ns // 64)), "R1", T.R1[:, 0:ns], T.MN[:, 15:16 * ns:16], 128.0, A.mult, 2.0, A.min)
-        tt("R1 PS", "RES", T.RES[:, 0:ns], T.PS[:, 128:128 + ns], T.R1[:, 0:ns], A.add)
-        if t == 0:
-            tt("RES Yt", "Yt", Y[:, 896:NV], T.RES[:, 0:128], Y[:, 896:NV], A.max)
-        else:
-            tt("RES RESz RK2 Yo Yt", "Yo Yt", Y[:, 0:NV], T.RES[:, :].indirect(T.RK2[:, :]), Y[:, 0:NV], A.max)
+        pieces = [(a, min(a + PIECE, nv)) for a in range(0, nv, PIECE)]
+        rest = [(a, min(a + 64, ns)) for a in range(nv, ns, 64)]
+        def spread(a, b, low, high):
+            o = c("PS", 128 + a, 128 + b)
+            mm([(o, ID, c("TWO", 0, b - a), True, False), (o, NI, low, False, False), (o, ID, high, False, True)])
 
-        diagonal()
+        for a, b in pieces:
+            scan(c("MN", 8 * b - 1, 8 * a - 1, -1), c("G", 16 * b - 1, 16 * a - 1, -2), c("G", 16 * b - 2, 16 * a - 1, -2),
+                 A.min, A.min, 2000.0)
+            mm([(c("PN", 256 + a, 256 + b), ID, c("MN", 8 * a, 8 * b, 8), True, False),
+                (c("PN", 256 + a, 256 + b), NI, c("RA", 0, 16 * (b - a), 16), False, True)])
+        for a, b in rest:
+            scan(c("MNS", 16 * a, 16 * b), c("K2", 0, 16 * (b - a)), c("GS", 16 * a, 16 * b), A.max, A.min)
+            mm([(c("PN", 256 + a, 256 + b), ID, c("MNS", 16 * a + 15, 16 * b, 16), True, True)])
+        for a, b in rest:
+            scan(c("MXS", 16 * a, 16 * b), c("K3", 0, 16 * (b - a)), c("GS", 16 * a, 16 * b), A.min, A.max)
+            spread(a, b, c("MNS", 16 * a + 15, 16 * b, 16), c("MXS", 16 * a + 15, 16 * b, 16))
+        for a, b in pieces:
+            scan(c("MX", 8 * a, 8 * b), c("G", 16 * a, 16 * b, 2), c("G", 16 * a + 1, 16 * b, 2), A.max, A.max, -2000.0)
+            spread(a, b, c("MN", 8 * a, 8 * b, 8), c("MX", 8 * a + 7, 8 * b, 8))
+        ts(c("FL", 0, ns), c("PN", 256, 256 + ns), 2.0, A.is_ge)
+        tt(c("RES", 0, ns), c("PS", 128, 128 + ns), c("FL", 0, ns), A.mult)
         if t == 0:
-            ts("KB", "KC", T.KC[:, :], T.KB[:, :], 65536.0, A.mult)
-            ts("CC", "SC", T.SC[:, :], T.CC[:, :], 15.0, A.is_equal, 1.0 / 65536, A.max)
-            ts("PRb", "PRF", T.PRF[:, 0:512], T.PR[:, 0:512], OFF + 0.125, A.add)
-            tt("KA KC", "KD", T.KD[:, :], T.KA[:, :], T.KC[:, :], A.max)
-            fill("TAG", T.TAG[:, :], TAG)
+            tt(c(Y, 896, NV), c("RES", 0, 128), c(Y, 896, NV), A.max)
         else:
-            naming_v(1)
-        ts("PD", "W", T.W[:, :], T.PD[:, 0:64], 2.0, A.is_ge)
-        s0 = 16 + (9 * t) % 40
-        col = lambda j: T.PK[:, j:j + 1]
-        e_ = lambda j: T.E[:, j:j + 1]
-        extra = [(col(64), T.NB[:, :], e_(s0 - 1), True, True), (col(66), T.B1[:, :], e_(63), True, True)]
-        if s0 > 16:
-            extra += [(col(65), T.NB[:, :], e_(15), True, False), (col(65), T.B1[:, :], e_(55), False, False),
-                      (col(65), T.NB[:, :], e_(s0 - 1), False, True)]
-        places([(s0, 56, 0)] + ([(16, s0, 56 - s0)] if s0 > 16 else []), extra)
-        if t > 0:
-            naming_v(2)
-            mm("Yo Yt ID MV", "PY0 PY1",
-               [(T.PY0[:, :], T.ID[:, :], Y[:, 0:512], True, False), (T.PY0[:, :], T.ID[:, :], T.MV[:, 0:512], False, True),
-                (T.PY1[:, :], T.ID[:, :], Y[:, 512:NV], True, False), (T.PY1[:, :], T.ID[:, :], T.MV[:, 512:NV], False, True)])
-        else:
-            mm("Yo Yt ID", "PY0 PY1", [(T.PY0[:, :], T.ID[:, :], Y[:, 0:512], True, True),
-                                       (T.PY1[:, :], T.ID[:, :], Y[:, 512:NV], True, True)])
-            ts("PRt PRb PRF", "PRF", T.PRF[:, 512:NV], T.PR[:, 512:NV], OFF + 0.125, A.add)
-        ts("PK", "RR", T.RR[:, s0 - 16:40], T.PK[:, s0:56], col(64), A.add, -1.0, A.add)
-        if s0 > 16:
-            ts("PK", "RRb", T.RR[:, 0:s0 - 16], T.PK[:, 16:s0], col(65), A.add, -1.0, A.add)
-        ts("PK", "E1", T.E1[:, :], col(66), -519.0, A.add, 1.0, A.max)
-        cp("RR RRb IDS", "RW", T.RW[:, :].indirect(T.RR[:, :]), T.IDS[:, :])
-        scan("RW KD", "DG1", T.DG1[:, :], T.KD[:, :], T.RW[:, 0:K2], A.mult, A.add)
-        ts("RW E1", "EL", T.EL[:, :], T.RW[:, 0:K2], float(NV), A.is_lt, T.E1[:, :], A.mult)
-        if t > 0:
-            ts("MV", "BV%d" % t, T["BV%d" % t][:, :], T.MV[:, NV:DUMP], 0.0, A.is_gt)
-        ts("DG1 SC", "CL", CL, T.DG1[:, 15:K2:16], T.SC[:, :], A.mult)
-        cp("PRt PRb PRz CL", "PRL", T.PRL[:, :], T.PR[:, :].indirect(CL))
-        cp(YA + " CL", "OI", T.OI[:, :], Ywin.indirect(CL))
-        dv = K2 - D_S[min(t, 1)]
+            tt(c(Y, 0, NV), ind(c("RES"), c("RK")), c(Y, 0, NV), A.max)
+
+        diagonal(Y, True, True)
+        if t == 0:
+            ts(c("PI2"), c("PI"), 15, A.bitwise_and)
+            cp(c("CC"), c("PI2"))
+            ts(c("SG"), c("SI"), c("CC"), A.add)
+            fill(c("WR", 0, 1), 0.0)
+            fill(c("WR", 41, SEG), 1.0)
+            ts(c("I16"), ID, 16.0, A.mult)
+            mm([(c("PL", 256 + 40, 256 + 60), ID, c("ONE", 0, 20), True, True)])
+        elif last:
+            ts(c("OY", 0, RING0), c(Y, 0, RING0), -2.0, A.add, -1.0, A.max)
+            ts(c("OY", 896, NV), c(Y, 896, NV), -2.0, A.add, -1.0, A.max)
+            dma("q", "o_a", [], [c("OY", 0, RING0), c("OY", 896, NV), c("OF", 0, RING0), c("OF", 896, NV)],
+                [(T.yy[:, 0:RING0], T.OY[:, 0:RING0]), (T.yy[:, 896:NV], T.OY[:, 896:NV]),
+                 (T.yf[:, 0:RING0], T.OF[:, 0:RING0]), (T.yf[:, 896:NV], T.OF[:, 896:NV])])
+        naming_v(1)
+        s0 = (9 * t) % 40
+        parts = [(s0, 40, 1)] + ([(0, s0, 41 - s0)] if s0 else [])
+        for a, b, x in parts:
+            ts(c("WR", x, x + b - a), c("PD", 16 + a, 16 + b), 2.0, A.is_ge)
+        scan(c("ER", 0, SEG), c("WR", 0, SEG), c("WR", 0, SEG), A.add, A.max)
+        mm([(c("PK", 64 + SEG * j, 64 + SEG * (j + 1)), B1, c("ER", 0, SEG), True, True) for j in range(6)])
+        items = []
+        for a, b, x in parts + [(60, 66, 41)]:
+            items += [(c("PL", 256 + a, 256 + b), B1, c("ER", x, x + b - a), True, False),
+                      (c("PL", 256 + a, 256 + b), NU, c("WR", x, x + b - a), False, True)]
+        mm(items)
+        mm([(c("PY%d" % j), ID, c(Y, 512 * j, 512 * j + 512), True, not marks) for j in (0, 1)])
+        if t == 0:
+            ts(c("IH"), ID, -256.0, A.mult)
+            ts(c("BF"), B1, -32.0, A.mult)
+            fill(c("CX"), -0.9375)
+        naming_v(2)
+        tt(c("GT"), c("PK", 64, 64 + 6 * SEG), c("SG"), A.is_gt)
+        scan(c("BS"), c("GT"), c("D"), A.mult, A.add)
+        cp(c("RT", 0, 66), c("PL", 256, 256 + 66))
+        ends = c("BS", SEG - 1, None, SEG)
+        ts(c("BL"), ends, 0.0, A.add)
+        tt(c("X1"), ind(c("RT", 0, 66), c("BL")), c("SF"), A.is_le)
+        o = c("PG", 384, 390)
+        mm([(o, c("I16"), ends, True, False)]
+           + [(o, c("ZB", 16 - i, 144 - i), c("X1", i, None, 16), False, i == 15) for i in range(16)])
+        if t == 0:
+            ts(c("PRF", 512, NV), c("PR", 512, NV), OFF + 0.125, A.add)
+        naming_v(3)
+        cp(CL, o)
+        cp(c("PRL"), ind(c("PR", RING0), CL))
+        naming_v(4)
+        if marks:
+            mm([(c("PY%d" % j), ID, c(MV, 512 * j, 512 * j + 512), False, True) for j in (0, 1)], True)
+        cp(c("COL"), ind(c("CO"), CL))
+        cp(c("OI"), ind(c(Y, RING0), CL))
+        if t == 0:
+            ts(c("PRF", 0, 512), c("PR", 0, 512), OFF + 0.125, A.add)
+        ts(c("OD"), c("OI"), 1, A.bitwise_and)
+        tt(c("OM"), ind(c("MO"), CL), c("OD"), A.mult)
+
+        act(c("NN"), c(M, NV, DUMP), F.Identity, 0.0, 1.0)
+        turn([("NN", 0)] + [(x, NV) for x in marks], "PN")
+        act(c("SN"), c("PD", 0, 64), F.Sign, -1.5, 1.0, c("CN"))
+        act(block("NM", t), c("PN", 0, NG), F.Sign, 0.0, 1.0)
+        exchange("NM", "LN", t, "nt")
+        if t == 0:
+            iota(c(MW, 0, DUMP), [[0, DUMP]], 0)
+            iota(c("TF"), [[-16, 64]], FAR)
+            iota(c("PH", 0, RINGN), [[0, RINGN]], 0)
+            iota(c("WV", 0, 256), [[1, 256]], DUMP + OFF)
+            iota(c("WS", 0, 256), [[1, 256]], DUMP + OFF)
+        left = c("PK", 480, 481)
+        mm([(left, c("BF"), c("CX"), True, False), (left, c("BF"), c("CN"), False, True)])
+        dv, hv = D_V[later], H_V[later]
+        if dv:
+            ts(c("DG", 0, 16 * dv), ind(c(Y), c("PRL", 0, dv)), 2.0, A.is_lt)
         if dv < K2:
-            act(YA + " PRL", "DGs", T.DG[:, 16 * dv:1536], Ywin.indirect(T.PRL[:, dv:K2]), F.Relu, 4.0, -2.0)
-        ts(YA + " PRL", "DGv", T.DG[:, 0:16 * dv], Ywin.indirect(T.PRL[:, 0:dv]), 2.0, A.is_lt)
-        mm("DGv DGs ID", "PS", [(T.PS[:, 0:K2], T.ID[:, :], T.DG[:, k:1536:16], k == 0, k == 15) for k in range(16)])
-        if not last:
-            iota("RW", T.RW[:, 0:K2], [[1, K2]], DUMP)
-            if t > 0:
-                iota("MV", T.MV[:, :], [[0, YW_]], 0)
-        if t > 0:
-            exchange(Mn + " BV%d" % t, M, NV, "LN%d" % t, "nt%d" % t, T["BV%d" % t])
-        ts("OI", "OD", T.OD[:, :], T.OI[:, :], 1, A.bitwise_and)
-        cp("COa COz CL", "COL", T.COL[:, :], T.CO[:, :].indirect(CL))
-        tt("MOa MOz CL OD", "OM", T.OM[:, :], T.MO[:, :].indirect(CL), T.OD[:, :], A.mult)
-        ts("OI", "OC", T.OC[:, :], T.OI[:, :], -1.0, A.add)
-
-        tt("PY0 " + Mn, "Ya Yo", Y[:, 0:512], T.PY0[:, :], M[:, 0:512], A.max)
-        tt("PY1 " + Mn, "Yb Yt", Y[:, 512:NV], T.PY1[:, :], M[:, 512:NV], A.max)
-        wrote["Yo"] = wrote["Yt"]
-        act(YA + " COL", "HGs", T.HG[:, 16 * H_V:1536], Ywin.indirect(T.COL[:, H_V:K2]), F.Abs, -8192.0, 8192.0)
-        ts(YA + " COL", "HGv", T.HG[:, 0:16 * H_V], Ywin.indirect(T.COL[:, 0:H_V]), 1.0, A.not_equal, 32.0, A.mult)
-        tt("PS OM", "FF", T.FF[:, :], T.PS[:, 0:K2], T.OM[:, :], A.min)
-        mm("FF B1 ID ALF", "PG", [(PC, T.ID[:, :], T.ALF[:, :], True, False), (PC, T.B1[:, :], T.FF[:, :], False, True)])
-        scan("K2 HGv", "HSv", T.HS[:, 0:16 * H_V], T.K2[:, 0:16 * H_V], T.HG[:, 0:16 * H_V], A.max, A.min)
-        ts("PG", "T1", T.T1[:, :], PC, 16.5, A.is_lt, ABSENT, A.max)
-        scan("K2 HGs", "HSs", T.HS[:, 16 * H_V:1536], T.K2[:, 0:1536 - 16 * H_V], T.HG[:, 16 * H_V:1536], A.max, A.min)
-        tt("PG T1", "CD", T.CD[:, :], PC, T.T1[:, :], A.min)
-        hs = T.HS[:, 15:1536:16]
-        scan("HSv HSs", "CF", T.CF[:, :], hs, hs, A.add, A.max)
-        tt("HSv HSs EL", "EF", T.EF[:, :], hs, T.EL[:, :], A.mult)
-        turn("LN%d" % t, "PN")
-        tt("CF EF", "KP", T.KP[:, :], T.CF[:, :], T.EF[:, :], A.is_ge)
-        tt("KP OC", "KO", T.KO[:, :], T.KP[:, :], T.OC[:, :], A.mult)
-        tt("KO CD CL", YA, Ywin.indirect(CL), T.KO[:, :], T.CD[:, :], A.add)
-        tt("PN AB", "NN", T.NN[:, :], T.PN[:, 0:NG], T.AB[:, :], A.min)
-
-        bn = "BN%d" % (t + 1)
-        tt("Yo Yt BD NN", bn, T[bn][:, :], Y[:, 0:NV].indirect(T.BD[:, :]), T.NN[:, :], A.max)
-        if not last:
-            exchange(bn, T[bn], 0, "LG%d" % (t + 1), "gh%d" % (t + 1))
-            cp(bn + " BD", "Yo Yt", Y[:, 0:NV].indirect(T.BD[:, :]), T[bn][:, :])
-            diagonal()
-            if t == 0:
-                iota("MV", T.MV[:, :], [[0, YW_]], 0)
-        phases()
+            act(c("DG", 16 * dv), ind(c(Y), c("PRL", dv)), F.Relu, 4.0, -2.0)
+        for j in (0, 1):
+            tt(c(YN, 512 * j, 512 * j + 512), c("PY%d" % j), c(M, 512 * j, 512 * j + 512), A.max)
+        mm(sums(c("PS", 0, K2), "DG", 0, K2, ID, True))
+        held = c("PK", 384, 384 + K2)
+        for a, x, b in hv:
+            act(c("HG", 16 * x, 16 * b), ind(c(YN), c("COL", x, b)), F.Silu, 318.75, -320.0)
+            ts(c("HG", 16 * a, 16 * x), ind(c(YN), c("COL", a, x)), 1.0, A.is_equal, -0.25, A.mult)
+            o = c("PK", 384 + a, 384 + b)
+            mm([(o, ID, c("ONE", 0, b - a), True, False)] + sums(o, "HG", a, b, c("IH"), False))
+        tt(c("FF"), c("PS", 0, K2), c("OM"), A.min)
+        mm([(c("PG", 256, 256 + K2), B1, c("FF"), True, True)])
+        act(c("OC"), ind(c(Y, RING0), CL), F.Identity, 0.0, 1.0)
+        act(c("A8"), c("PG", 256, 256 + K2), F.Abs, -8.0, 1.0)
+        act(c("CD"), c("A8"), F.Silu, -1600.006, 200.0)
+        tt(ind(c(MW, 0, NV), BD), block("LN", t), c("AB"), A.mult)
+        diagonal(MW, True, False, last)
         if last:
-            mm("PH ID", "PY0 PY1", [(T.PY0[:, :], T.ID[:, :], T.PH[:, 256:768], True, True),
-                                    (T.PY1[:, 0:128], T.ID[:, :], T.PH[:, 768:896], True, True)])
+            tt(ind(c("PH"), CL), c("FF"), c("FF"), A.add)
+        ts(c("FR"), held, 2.0, A.is_lt, 32.0, A.mult)
+        scan(c("CF"), c("FR"), c("FR"), A.add, A.add, left)
+        tt(c("U"), held, c("CF"), A.max)
+        tt(c("KO"), c("OC"), c("U"), A.min)
+        tt(ind(c(YN, RING0), CL), c("KO"), c("CD"), A.add)
+        diagonal(YN, False, True, last)
 
-    act("Yo Yt", "OZ", T.OZ[:, :], Y[:, 0:NV], F.Relu, -1.0, 1.0)
-    act("OZ", "OY", T.OY[:, :], T.OZ[:, :], F.Identity, -1.0, 1.0)
-    dma("s", "o_y", "OY", "", [(T.yy[:, :], T.OY[:, :])])
-    ts("Yo Yt", "OW", T.OW[:, :], Y[:, 0:NV], 1.0, A.is_equal)
-    ts(bn, "BW", T.BW[:, :], T[bn][:, :], 1.0, A.is_equal)
-    tt("PY0 Yo Yt", "OFa", T.OF[:, 256:768], T.PY0[:, :], Y[:, 256:768], A.is_gt)
-    tt("PY1 Yo Yt", "OFb", T.OF[:, 768:896], T.PY1[:, 0:128], Y[:, 768:896], A.is_gt)
-    cp("BW BD", "OW", T.OW[:, :].indirect(T.BD[:, :]), T.BW[:, :])
-    dma("q", "o_f", "OFa OFb OFz OFy", "", [(T.yf[:, :], T.OF[:, :])])
-    dma("q", "o_w", "OW", "", [(T.yw[:, :], T.OW[0:128:16, :])])
-    g.wait_ge(T.sem.sent, sent[0])
+        if not last:
+            border(YN, t + 1, -1.5)
+            if t == 0:
+                ts(c("TT"), c("TF"), c("CC"), A.subtract)
+                iota(c("M1", 0, DUMP), [[0, DUMP]], 0)
+                iota(c("K2"), [[0, 64], [-40, 16]], 32)
+                iota(c("K3"), [[0, 64], [40, 16]], -8)
+                iota(c("RES", 256), [[0, FAR - 256]], 0)
+            tt(ind(c("PH"), CL), c("FF"), c("FF"), A.add)
+
+    for j, (a, b) in enumerate(((0, 512), (512, RINGN))):
+        o = c("PY%d" % j, 0, b - a)
+        mm([(o, ID, c("PH", a, b), True, False), (o, NI, c(YN, RING0 + a, RING0 + b), False, True)])
+        act(c("OF", RING0 + a, RING0 + b), o, F.Relu, -0.001, 1.0)
+    ts(c("OY", RING0, 896), c(YN, RING0, 896), -2.0, A.add, -1.0, A.max)
+    dma("q", "o_y", [], [c("OY", RING0, 896)], [(T.yy[:, RING0:896], T.OY[:, RING0:896])])
+    wanted(c("OW"))
+    dma("q", "o_w", [], [c("OW")], [(T.yw[:, :], T.OW[:, :])])
+    dma("s", "o_f", [], [c("OF", RING0, 896)], [(T.yf[:, RING0:896], T.OF[:, RING0:896])])
+    g.wait_ge(T.sem.sent, (sent[0] - 1) * sum(ENG))
     for sem, n in list(count.items()) + list(dmas.items()):
         need("q", (sem, n))

@@ -7,18 +7,34 @@ YW_ = DUMP + 256
 RING0, RINGN = 256, 640
 TW = DUMP + K2 - RING0
 SEG = 47
+NC = 80
+Z0_ = 96
+DELTA = 1.0 / 256
+BIG = 29952.0
+SEARCH = False
 OFF = 32
+FAR = NV + 256
+TAG = 2.0 ** -9
+GHOST = 1.25
 SILU_ONE = 1.278464542761074
 ROUND = 65536.0 + 2.0 ** -7
-STEP = 20
-PIECE = 96
-S_SLOTS = (0, 112)
-V_FIRST = 64
-V_NAME = ((0, 0, 0, 0, 0), (16, 16, 16, 16, 0))
-T0_K = 2
-D_V = (16, 24)
-H_V = (((0, 48, 96),),) * 2
-FAR = NV + 256
+STEP = 18
+S_SLOTS = 120
+PIECE = 256 - S_SLOTS
+V_FIRST = 80
+V_NAME = {1: 16, 3: 16, 5: 16, 8: 16}
+D_V = ((24, 24, 24), (28, 28, 52))
+TURNS = (7, 5)
+EARLY = {6: (0, 128), 7: (128, 256)}
+NOTES = {0: (0, 64), 2: (64, 192)}
+NEAR = 1
+T0_S, T0_AT, V_NAME0 = 32, 4, {}
+SPLIT_C = True
+TAIL = "y"
+SCANS = "NnXx"
+TURN_FIRST = True
+S_LATE = 0
+H_V = (((0, 24, 48), (48, 72, 96)),) * 2
 ENG = (4, 4, 4)
 
 
@@ -28,46 +44,50 @@ def _sb(n, d):
 
 SCRATCH = {
     "YA": _sb(YW_, "bfloat16"), "YB": _sb(YW_, "bfloat16"), "Y0": _sb(NV, "bfloat16"),
-    "PR": _sb(DUMP + K2, "int32"), "CO": _sb(TW, "int32"), "MO": _sb(TW, "int32"), "PRF": _sb(NV, "float32"),
+    "PR": _sb(YW_, "int32"), "CO": _sb(TW, "int32"), "MO": _sb(TW, "int32"),
     "BDI": _sb(12, "int32"), "BD": _sb(12, "uint16"), "AB": _sb(NG, "bfloat16"), "NN": _sb(NG, "bfloat16"),
-    "WV": _sb(FAR, "float32"), "WS": _sb(FAR, "float32"),
+    "MB": _sb(YW_, "float32"), "YT": _sb(DUMP, "bfloat16"),
+    "W": _sb(NC, "bfloat16"), "E": _sb(NC + 1, "bfloat16"), "PAY": _sb(NC, "float32"), "PP": _sb(2 * NC, "float32"),
+    "ZL": _sb(6, "uint16"), "Z": _sb(Z0_ + 16 * NC, "float32"), "X": _sb(256, "float16"), "NP": _sb(256, "float32"),
+    "NL": _sb(16, "uint16"), "XI": _sb(256, "bfloat16"), "XJ": _sb(2 * NC, "bfloat16"), "CI": _sb(2 * NC, "bfloat16"),
+    "CJ": _sb(2 * NC, "bfloat16"), "NE": _sb(2 * NC, "bfloat16"), "H0": _sb(2 * NC, "bfloat16"),
+    "MK": _sb(256, "bfloat16"), "DL": _sb(256, "bfloat16"), "B2": _sb(128, "bfloat16"),
     "C": _sb(256, "float16"), "CT": _sb(256, "float16"), "LS": _sb(256, "uint16"), "L": _sb(256, "uint16"),
     "C0": _sb(128, "float32"), "C1": _sb(128, "float32"), "DS": _sb(128, "float32"),
     "G": _sb(4096, "float16"), "GS": _sb(4096, "bfloat16"), "MX": _sb(2048, "float16"), "MN": _sb(2048, "float16"),
     "MXS": _sb(4096, "bfloat16"), "MNS": _sb(4096, "bfloat16"),
-    "K2": _sb(1024, "bfloat16"), "K3": _sb(1024, "bfloat16"), "R0": _sb(16 * PIECE, "float16"), "RA": _sb(16 * PIECE, "float16"),
-    "FL": _sb(256, "bfloat16"), "RES": _sb(FAR, "bfloat16"), "TWO": _sb(256, "bfloat16"),
-    "W": _sb(64, "float16"), "E": _sb(64, "float16"), "WT": _sb(64, "float16"), "TT": _sb(64, "float16"),
+    "K2": _sb(2560, "bfloat16"), "K3": _sb(2560, "bfloat16"), "R0": _sb(3072, "float16"), "RA": _sb(3072, "float16"),
+    "FL": _sb(256, "bfloat16"), "RES": _sb(FAR, "bfloat16"), "PRF": _sb(NV, "float32"),
+    "WV": _sb(FAR, "float32"), "WS": _sb(FAR, "float32"), "WT": _sb(64, "float16"), "TT": _sb(64, "float16"),
     "TF": _sb(64, "float32"), "RK": _sb(64, "uint16"), "OC": _sb(K2, "bfloat16"),
     "WR": _sb(48, "bfloat16"), "ER": _sb(48, "bfloat16"), "SI": _sb(6 * SEG, "bfloat16"), "SG": _sb(6 * SEG, "bfloat16"),
     "GT": _sb(6 * SEG, "bfloat16"), "D0": _sb(6 * SEG, "bfloat16"), "D1": _sb(6 * SEG, "bfloat16"), "D": _sb(6 * SEG, "bfloat16"),
     "BS": _sb(6 * SEG, "bfloat16"), "BL": _sb(6, "uint16"), "RT": _sb(80, "bfloat16"), "SF": _sb(K2, "bfloat16"),
     "X1": _sb(K2, "bfloat16"), "SIL": _sb(256, "float32"), "SN": _sb(64, "bfloat16"), "CN": _sb(1, "float32"),
-    "PI": _sb(1, "int32"), "PI2": _sb(1, "int32"), "CC": _sb(1, "float32"), "CX": _sb(1, "float32"),
+    "CC": _sb(1, "float32"), "CX": _sb(1, "float32"),
     "CL": _sb(6, "uint16"), "COL": _sb(K2, "uint16"), "PRL": _sb(K2, "uint16"),
     "DG": _sb(1536, "bfloat16"), "HG": _sb(1536, "bfloat16"), "TAG": _sb(256, "bfloat16"),
     "OI": _sb(K2, "int32"), "OD": _sb(K2, "int32"), "OM": _sb(K2, "bfloat16"), "FF": _sb(K2, "bfloat16"),
-    "A8": _sb(K2, "float32"), "CD": _sb(K2, "bfloat16"), "FR": _sb(K2, "bfloat16"), "CF": _sb(K2, "bfloat16"),
-    "U": _sb(K2, "bfloat16"), "KO": _sb(K2, "bfloat16"),
-    "PH": _sb(TW, "bfloat16"), "OY": _sb(NV, "bfloat16"), "OF": _sb(NV, "bfloat16"), "OW": _sb(64, "bfloat16"),
+    "A8": _sb(K2, "float32"), "CD": _sb(K2, "bfloat16"), "FR": _sb(K2, "bfloat16"), "CF": _sb(2 * K2, "bfloat16"),
+    "KO": _sb(2 * K2, "bfloat16"),
+    "PH": _sb(TW, "bfloat16"), "OY": _sb(RING0 + TW, "bfloat16"), "OF": _sb(RING0 + TW, "bfloat16"), "OW": _sb(64, "bfloat16"),
     "ONE": _sb(288, "bfloat16"),
     "Z0": _sb(160, "bfloat16"), "Z1": _sb(160, "bfloat16"), "ZS": _sb(160, "bfloat16"), "ZA": _sb(160, "bfloat16"),
     "ZB": _sb(160, "bfloat16"), "ID": _sb(128, "bfloat16"), "I16": _sb(128, "bfloat16"), "IH": _sb(128, "bfloat16"),
     "B0": _sb(128, "bfloat16"), "B1": _sb(128, "bfloat16"), "NB": _sb(128, "bfloat16"), "NU": _sb(128, "bfloat16"),
     "NI": _sb(128, "bfloat16"), "BF": _sb(128, "float32"), "P1": _sb(128, "bfloat16"), "P2": _sb(128, "bfloat16"),
 }
-for _t in range(RO):
+for _t in range(2):
     SCRATCH["M%d" % _t] = _sb(YW_, "float32")
+    SCRATCH["MV%d" % _t] = _sb(YW_, "bfloat16")
 for _n in ("BN", "LG", "LN", "NM"):
     SCRATCH[_n] = _sb(RO * NG, "bfloat16")
-for _t in range(RO + 1):
-    SCRATCH["MV%d" % _t] = _sb(YW_, "bfloat16")
-PSUM = ("PD", "PK", "PL", "PG", "PN", "PS", "PY0", "PY1")
+PSUM = ("PD", "PK", "PL", "PG", "PN", "PS", "PY")
 for _n in PSUM:
-    SCRATCH[_n] = ("psum", [128, 512], "float32")
+    SCRATCH[_n] = ("psum", [128, NV if _n == "PY" else 512], "float32")
 
 SEMAPHORES = (["v", "s", "p", "g", "first", "sent", "d_y", "d_bd", "d_pt", "d_pr", "d_pa", "d_co", "d_mo", "o_a", "o_y", "o_f", "o_w"]
-              + ["gh%d" % t for t in range(RO)] + ["nt%d" % t for t in range(RO)])
+              + ["gh%d" % t for t in range(RO)] + ["nt%d" % t for t in range(RO)] + ["nn%d" % t for t in range(RO)])
 
 
 def rank_program(g, core, T, topo):
@@ -159,17 +179,22 @@ def rank_program(g, core, T, topo):
         masks[j] = sum(1 << x for x in free)
     sent = [0]
 
-    def exchange(src, land, t, sem):
+    def exchange(src, land, t, sem, near=None):
         order("g", [], [(src, NG * t, NG * t + NG)])
         tr = []
         for j in range(3):
             rid, pid = topo.addr(peers[j], core)
             third = slice(NG * t + 64 * j, NG * t + 64 * j + 64)
-            tr.append(RemoteDMATransfer(dst_ids=[DstId(rid=rid, pnc=pid)], dma_engine_mask=masks[j], remote_sem=T.sem[sem + str(t)],
+            name = (near if near and j == 0 else sem) + str(t)
+            tr.append(RemoteDMATransfer(dst_ids=[DstId(rid=rid, pnc=pid)], dma_engine_mask=masks[j], remote_sem=T.sem[name],
                                         srcs=[T[src][:, third]], dsts=[T[land][:, third]], alu_op=0))
         g.remote_dma_fused(tr, local_sem=T.sem["sent" if sent[0] else "first"])
         sent[0] += 1
-        log[land] = [[NG * t, NG * t + NG, (sem + str(t), sum(ENG)), True, "far"]]
+        if near:
+            log[land] = [[NG * t, NG * t + 64, (near + str(t), ENG[0]), True, "far"],
+                         [NG * t + 64, NG * t + NG, (sem + str(t), ENG[1] + ENG[2]), True, "far"]]
+        else:
+            log[land] = [[NG * t, NG * t + NG, (sem + str(t), sum(ENG)), True, "far"]]
 
     def ts(out, in0, s1, o1, s2=None, o2=None):
         if o2 is None:
@@ -197,6 +222,9 @@ def rank_program(g, core, T, topo):
         else:
             op("s", [out], [a], lambda: S.activation(out["ap"], a["ap"], f, bias=bias, scale=scale))
 
+    def times(out, a, x):
+        act(out, a, F.Identity, 0.0, x)
+
     def iota(out, pat, base, cm=0):
         if SCRATCH[out["at"][0]][2] == "int32":
             op("g", [out], [], lambda: g.iota(out["ap"], pat, base, cm))
@@ -206,8 +234,8 @@ def rank_program(g, core, T, topo):
     def sel(out, a, pat, cmp, base, cm, other=0.0):
         op("g", [out], [a], lambda: g.affine_select(out["ap"], a["ap"], pat, cmp, other, base, cm))
 
-    CL, BD = c("CL"), c("BD")
-    ID, NI, B1, NU = c("ID"), c("NI"), c("B1"), c("NU")
+    CL, BD, KO = c("CL"), c("BD"), c("KO", 1, None, 2)
+    ID, NI, B1, NU, IH = c("ID"), c("NI"), c("B1"), c("NU"), c("IH")
 
     def block(name, t):
         return c(name, NG * t, NG * t + NG)
@@ -219,11 +247,7 @@ def rank_program(g, core, T, topo):
     def border(name, t, shift):
         act(block("BN", t), ind(c(name, 0, NV), BD), F.Relu, shift, 1.0)
         exchange("BN", "LG", t, "gh")
-        act(c("AB"), block("BN", t), F.Relu, 0.003, -0.012)
-
-    def ghosts(name, t):
-        turn([("LG", NG * t)], "PG")
-        act(c(name, NV, DUMP), c("PG", 0, NG), F.Identity, 1.5, 1.0)
+        act(c("AB"), block("BN", t), F.Relu, TAG, -0.012)
 
     def diagonal(name, first, final, blocks=False):
         mm([(c("PD", 0, 64), c("ZS", 16 - i, 144 - i), c(name, 64 * i, 64 * i + 64) if blocks else c(name, i, NV, 16),
@@ -243,12 +267,33 @@ def rank_program(g, core, T, topo):
             src = "D1"
         sel(c("D"), c(src), [[0, 6], [1, SEG]], A.not_equal, -39, 0, float((s0 - 1) % 40 - 60))
 
+    def payload(a, b, first):
+        o = c("PN", a, b)
+        mm([(o, IH, c("SF", first, first + b - a), True, False)])
+        return lambda: (mm([(o, B1, c("W", a, b), False, False), (o, NU, c("W", a, b), False, True)], True),
+                        act(c("PAY", a, b), o, F.Identity, 1024.5 - DELTA / 2, -DELTA))
+
+    def ring_out(x):
+        if x == "y":
+            tt(ind(c("OY", RING0), CL), KO, c("OM"), A.add)
+            dma("q", "o_y", [], [c("OY", RING0, 896)], [(T.yy[:, RING0:896], T.OY[:, RING0:896])])
+        else:
+            tt(ind(c("OF", RING0), CL), c("FF"), c("FR"), A.mult)
+            dma("s", "o_f", [], [c("OF", RING0, 896)], [(T.yf[:, RING0:896], T.OF[:, RING0:896])])
+
+    def clear_lists():
+        if SEARCH:
+            iota(c("Z", Z0_, Z0_ + 256), [[0, 256]], 0)
+        else:
+            iota(c("WV", 0, 256), [[1, 256]], DUMP + OFF)
+            iota(c("WS", 0, 256), [[1, 256]], DUMP + OFF)
+
     dma("q", "d_y", [c("Y0")], [], [(T.Y0[:, :], T.y0[:, :])])
     dma("s", "d_bd", [c("BDI")], [], [(T.BDI[:, :], T.bd[:, :])])
-    dma("s", "d_pt", [c("PR", 896, NV)], [], [(T.PR[:, 896:NV], T.pr[:, 896:NV])])
+    dma("q", "d_pt", [c("PR", 896, NV)], [], [(T.PR[:, 896:NV], T.pr[:, 896:NV])])
 
     fill(c("ONE"), 1.0)
-    act(c("TAG"), c("ONE", 0, 256), F.Silu, 0.0, 0.00586)
+    act(c("TAG"), c("ONE", 0, 256), F.Silu, 0.0, 0.0039025)
     sel(ID, c("ONE", 0, 128), [[-1, 128]], A.is_equal, 0, 1)
     iota(c("DS"), [[1, 128]], DUMP)
     for h, z in ((0, "Z0"), (1, "Z1")):
@@ -256,8 +301,12 @@ def rank_program(g, core, T, topo):
     fill(c("M0", 0, DUMP), 0.0)
     fill(c("SIL"), SILU_ONE)
     cp(BD, c("BDI"))
-    fill(c("R0"), 0.0)
-    border("Y0", 0, 0.5)
+    ramp = max(128, PIECE)
+    fill(c("R0", 0, 16 * ramp), 0.0)
+    times(NI, ID, -1.0)
+    times(IH, ID, -256.0)
+    times(c("I16"), ID, 16.0)
+    border("Y0", 0, 2.0 - GHOST)
     need("q", ("first", sum(ENG)))
     dma("q", "d_pr", [c("PR", RING0, 896)], [], [(T.PR[:, RING0:896], T.pr[:, RING0:896])])
     dma("q", "d_co", [c("CO", 0, RINGN)], [], [(T.CO[:, 0:RINGN], T.co[:, RING0:896])])
@@ -266,42 +315,75 @@ def rank_program(g, core, T, topo):
     sel(c("P1"), c("ONE", 0, 128), [[16, 8], [-1, 16]], A.is_equal, -112, 1)
     sel(c("P2", 16, 128), c("ONE", 16, 128), [[16, 7], [-1, 16]], A.is_equal, -112, 1)
     sel(c("P2", 0, 16), c("ONE", 0, 16), [[-1, 16]], A.is_equal, 0, 1)
-    iota(c("PI"), [[0, 1]], 0, 1)
-    sel(c("ZS"), c("ONE", 0, 160), [[-16, 10], [999, 16]], A.is_equal, 16, 1)
     sel(c("B0"), c("ONE", 0, 128), [[-16, 8], [0, 16]], A.is_ge, 0, 1)
     sel(B1, c("B0"), [[16, 8], [0, 16]], A.is_ge, 15, -1)
-    iota(c("SI"), [[16, 6], [0, SEG]], 0)
-    iota(c("SF"), [[1, K2]], 0)
+    sel(c("ZS"), c("ONE", 0, 160), [[-16, 10], [999, 16]], A.is_equal, 16, 1)
     iota(c("D1"), [[0, 6 * SEG]], -1)
-    sel(c("D0"), c("D1"), [[0, 6], [1, SEG]], A.not_equal, -(SEG - 1), 0, 66.0)
-    ring_table(0)
+    sel(c("NB"), c("D1", 0, 128), [[-1, 128]], A.is_gt, 0, 1)
+    iota(c("SI"), [[16, 6], [0, SEG]], 0)
+    sel(NU, c("NB"), [[16, 8], [0, 16]], A.is_ge, 15, -1)
     act(c("YA", 0, 896), c("Y0", 0, 896), F.Identity, 2.0, 1.0021)
+    times(c("MB", 0, DUMP), c("M0", 0, DUMP), 0.0)
 
     for t in range(RO):
-        M, MV, MW = "M%d" % t, "MV%d" % t, "MV%d" % (t + 1)
+        M, MV, MW = "M%d" % (t % 2), "MV%d" % (t % 2), "MV%d" % ((t + 1) % 2)
         Y, YN = ("YA", "YB")[t % 2], ("YB", "YA")[t % 2]
         last, later = t == RO - 1, min(t, 1)
         ns = 128 if t == 0 else 256
-        off = float(OFF * later)
-        nv = ns - S_SLOTS[later]
+        nv = PIECE if t else ns - T0_S
         kc = ns // 16
+        off = 0.0 if SEARCH else float(OFF * later)
         if t == 0:
             ts(c("C0"), c("Y0", 896, NV), 0.0, A.is_ge, 2000.0, A.mult)
-            tt(c("C1"), c("C0"), c("PR", 896, NV), A.max)
-            tt(c("C", 0, 128), c("C1"), c("DS"), A.min)
-        else:
-            wanted(c("W"))
-            scan(c("E"), c("W"), c("W"), A.add, A.max)
-            tt(c("WT"), c("W"), c("TT"), A.mult)
+            ts(c(Y, 896, NV), c("Y0", 896, NV), 2.0, A.add)
+            tt(c("C1"), c("C0"), c("DS"), A.min)
+            fill(c("R0", 0, 16 * ramp, 16), STEP / 2.0)
+            tt(c("C", 0, 128), c("C1"), c("PR", 896, NV), A.max)
+            fill(c(Y, DUMP), 1.0)
+        elif not SEARCH:
+            W = c("W", 0, 64)
+            wanted(W)
+            scan(c("E", 0, 64), W, W, A.add, A.max)
+            tt(c("WT"), W, c("TT"), A.mult)
             o = c("PK", 0, 64)
-            mm([(o, ID, c("TT"), True, False), (o, NU, c("W"), False, False), (o, B1, c("E"), False, False),
+            mm([(o, ID, c("TT"), True, False), (o, NU, W, False, False), (o, B1, c("E", 0, 64), False, False),
                 (o, NI, c("WT"), False, True)])
+            if t == 1:
+                times(c(M, 0, DUMP), c(YN, 0, DUMP), 0.0)
             ts(c("RK"), o, -1.0, A.add)
             act(ind(c("WS"), c("RK", 32, 64)), c("PRF", 512, NV), F.Silu)
             cp(ind(c("WV"), c("RK", 0, 32)), c("PRF", 0, 512))
-            ghosts(Y, t)
-            tt(c("C"), c("WV", 0, 256), c("WS", 0, 256), A.min)
-            ts(c("LS"), c("C"), -off, A.add)
+            turn([("LG", NG * t)], "PG")
+            act(c(Y, NV, DUMP), c("PG", 0, NG), F.Identity, GHOST, 1.0)
+            if t == 1:
+                times(c("MB", 0, DUMP), c(YN, 0, DUMP), 0.0)
+            halves = ((nv, ns), (0, nv)) if SPLIT_C else ((0, ns),)
+            for a, b in halves:
+                tt(c("C", a, b), c("WV", a, b), c("WS", a, b), A.min)
+            for a, b in halves:
+                ts(c("LS", a, b), c("C", a, b), -off, A.add)
+        else:
+            rest_of_payload = payload(0, 64, 0)
+            pl, nodes = c("PK", 0, 2 * NC), c("PS", 0, 256)
+            mm([(pl, ID, c("NE"), True, False), (pl, ID, c("CJ"), False, False)])
+            wanted(c("W", 0, 64))
+            scan(c("E", 1), c("W"), c("W"), A.add, A.max)
+            rest_of_payload()
+            mm([(c("PK", 0, 2 * NC, 2), c("B2"), c("W"), False, False), (c("PK", 1, 2 * NC, 2), B1, c("E", 0, NC), False, True)], True)
+            if t == 1:
+                times(c(M, 0, DUMP), c(YN, 0, DUMP), 0.0)
+            tt(ind(c("PH"), CL), c("FF"), c("FF"), A.add)
+            scan(c("PP"), c("H0"), pl, A.max, A.min)
+            cp(c("ZL", 0, 5), c("PP", 31, 2 * NC, 32))
+            cp(ind(c("Z"), c("ZL", 0, 5)), c("PAY"))
+            scan(c("X"), c("Z", Z0_, Z0_ + 256), c("DL"), A.max, A.add)
+            mm([(nodes, B1, c("X"), True, True)])
+            turn([("LG", NG * t)], "PG")
+            act(c(Y, NV, DUMP), c("PG", 0, NG), F.Identity, GHOST, 1.0)
+            scan(c("NP"), c("MK"), nodes, A.max, A.min)
+            ts(c("NL"), c("NP", 15, 256, 16), -16384.0, A.add)
+            ts(c("C"), ind(c("PR"), c("NL")), 0.0, A.add)
+            ts(c("LS"), c("C"), 0.0, A.add)
         op("v", [c("CT", 0, ns)], [c("C", 0, ns)], lambda: V.transpose(T.CT[:, 0:ns], T.C[:, 0:ns]))
         items = []
         for b in range(ns // 32):
@@ -313,107 +395,119 @@ def rank_program(g, core, T, topo):
         mm(items)
 
         def gather(a, b):
-            while a < b:
-                x = min(b, (a // PIECE + 1) * PIECE)
-                tt(c("G", 16 * a, 16 * x), ind(c(Y), c("LS", a, x)), c("RA", 16 * (a % PIECE), 16 * (a % PIECE + x - a)), A.add)
-                a = x
+            if a < b:
+                tt(c("G", 16 * a, 16 * b), ind(c(Y), c("LS", a, b)), c("RA", 16 * a, 16 * b), A.add)
 
-        names = V_NAME[later]
-        at = [ns - sum(names)]
-        marks = [MV] if t or sum(names) else []
+        names = V_NAME if t else V_NAME0
+        at = [ns - sum(names.values())]
+        s_end = at[0]
+        turns = TURNS[later]
+        cut = max([0] + [b for a, b in EARLY.values()])
+        marks = [MV] if names else []
 
         def naming(e, a, b):
             while a < b:
                 x = min(b, (a // kc + 1) * kc)
                 if e == "s":
-                    act(ind(c(M), c("L", a, x)), c("SIL", 0, 16 * (x - a)), F.Silu)
+                    k = a // kc
+                    act(ind(c("MB" if k % 2 and k < 2 * turns else M), c("L", a, x)), c("SIL", 0, 16 * (x - a)), F.Silu)
+                    if k == 2 * turns:
+                        times(c("YT", cut), c("MB", cut, DUMP), TAG)
                 else:
                     cp(ind(c(MV), c("L", a, x)), c("TAG", 0, 16 * (x - a)))
                 a = x
 
         def naming_v(j):
-            naming("v", at[0], at[0] + names[j])
-            at[0] += names[j]
+            naming("v", at[0], at[0] + names.get(j, 0))
+            at[0] += names.get(j, 0)
+            if j in EARLY:
+                a, b = EARLY[j]
+                tt(c("YT", a, b), c("PY", a, b), c("MB", a, b), A.max)
+
 
         if t == 0:
             ts(c("LS", 0, ns), c("C", 0, ns), 0.0, A.add)
-            ts(c(Y, 896, NV), c("Y0", 896, NV), 2.0, A.add)
-            fill(c("R0", 0, None, 16), STEP / 2.0)
-            fill(c(Y, DUMP, YW_ - 16), 0.0)
             ts(c("L", 0, ns), c("PL", 0, ns), 0.0, A.add)
-            naming("s", 0, T0_K * kc)
-            fill(c(Y, YW_ - 16, YW_), 1.0)
-            scan(c("RA"), c("R0"), c("R0"), A.add, A.add, -float(STEP * (PIECE // 2 + 1)))
-            ghosts(Y, 0)
-            naming("s", T0_K * kc, at[0])
-            ts(NI, ID, -1.0, A.mult)
-            fill(c("TWO"), 2.0)
+            naming("s", 0, T0_AT * kc)
+            scan(c("RA", 0, 16 * ramp), c("R0", 0, 16 * ramp), c("R0", 0, 16 * ramp), A.add, A.add, -float(STEP * (ramp // 2 + 1)))
             if marks:
-                fill(c("MV0", 0, DUMP), 0.0)
+                fill(c(MV, 0, DUMP), 0.0)
+            if T0_S:
+                fill(c("K2", 0, 16 * T0_S), 0.0)
+                fill(c("K3", 0, 16 * T0_S), 32.0)
+                fill(c("K2", 0, 16 * T0_S, 16), 32.0)
+                fill(c("K3", 0, 16 * T0_S, 16), 0.0)
+            naming_v("g")
+            turn([("LG", 0)], "PG")
+            ts(c(Y, NV, DUMP), c("PG", 0, NG), GHOST, A.add)
+            if T0_S:
+                act(c("GS", 16 * nv, 16 * ns), ind(c(Y), c("LS", nv, ns)), F.Identity, 0.0, 1.0)
+            naming("s", T0_AT * kc, s_end)
             gather(0, nv)
+            sel(c("D0"), c("D1"), [[0, 6], [1, SEG]], A.not_equal, -(SEG - 1), 0, 66.0)
+            ring_table(0)
+            sel(c("WR"), c("ONE", 0, 48), [[1, 48]], A.is_gt, 0, 0)
+            iota(c("SF"), [[1, K2]], 0)
             sel(c("ZA"), c("ONE", 0, 160), [[-16, 10], [-999, 16]], A.is_ge, 16, 1)
             sel(c("ZB"), c("ZA"), [[16, 10], [0, 16]], A.is_ge, -1, -1)
-            ts(c("NB"), B1, -1.0, A.mult)
-            sel(NU, c("NB"), [[-1, 128]], A.is_gt, 0, 1)
-            iota(c("PR", NV), [[0, DUMP + K2 - NV]], 0)
-            iota(c("CO", RINGN), [[0, TW - RINGN]], YW_ - 1)
-            iota(c("MO", RINGN), [[0, TW - RINGN]], 0)
-            fill(c(YN, NV, YW_ - 16), 1.5)
-            fill(c(YN, YW_ - 16, YW_), 1.0)
+            iota(c("PR", DUMP), [[1, 256]], DUMP)
+            iota(c("CO", TW - K2), [[0, K2]], YW_ - 1)
+            iota(c("MO", TW - K2), [[0, K2]], 0)
         else:
-            if nv < ns:
-                act(c("GS", 16 * nv, 16 * ns), ind(c(Y), c("LS", nv, ns)), F.Identity, 0.0, 1.0)
+            act(c("GS", 16 * nv, 16 * ns), ind(c(Y), c("LS", nv, ns)), F.Identity, 0.0, 1.0)
             gather(0, V_FIRST)
             ts(c("L"), c("PL", 0, ns), -off, A.add)
-            naming("s", 0, at[0])
+            naming("s", 0, s_end - S_LATE)
             gather(V_FIRST, nv)
             ring_table(t)
             if not last:
-                iota(c("WV", 0, 256), [[1, 256]], DUMP + OFF)
-                iota(c("WS", 0, 256), [[1, 256]], DUMP + OFF)
+                clear_lists()
             iota(c(MW, 0, DUMP), [[0, DUMP]], 0)
             if not last:
-                iota(c("M%d" % (t + 1), 0, DUMP), [[0, DUMP]], 0)
+                iota(c("M%d" % ((t + 1) % 2), 0, DUMP), [[0, DUMP]], 0)
             else:
                 iota(c("OF", 0, RING0), [[0, RING0]], 0)
                 iota(c("OF", 896, NV), [[0, 128]], 0)
         naming_v(0)
 
-        pieces = [(a, min(a + PIECE, nv)) for a in range(0, nv, PIECE)]
-        rest = [(a, min(a + 64, ns)) for a in range(nv, ns, 64)]
         def spread(a, b, low, high):
             o = c("PS", 128 + a, 128 + b)
-            mm([(o, ID, c("TWO", 0, b - a), True, False), (o, NI, low, False, False), (o, ID, high, False, True)])
+            mm([(o, ID, c("ONE", 0, b - a), i == 0, False) for i in range(1 if t and SEARCH else 2)]
+               + [(o, NI, low, False, False), (o, ID, high, False, True)])
 
-        for a, b in pieces:
-            scan(c("MN", 8 * b - 1, 8 * a - 1, -1), c("G", 16 * b - 1, 16 * a - 1, -2), c("G", 16 * b - 2, 16 * a - 1, -2),
-                 A.min, A.min, 2000.0)
-            mm([(c("PN", 256 + a, 256 + b), ID, c("MN", 8 * a, 8 * b, 8), True, False),
-                (c("PN", 256 + a, 256 + b), NI, c("RA", 0, 16 * (b - a), 16), False, True)])
-        for a, b in rest:
-            scan(c("MNS", 16 * a, 16 * b), c("K2", 0, 16 * (b - a)), c("GS", 16 * a, 16 * b), A.max, A.min)
-            mm([(c("PN", 256 + a, 256 + b), ID, c("MNS", 16 * a + 15, 16 * b, 16), True, True)])
-        for a, b in rest:
-            scan(c("MXS", 16 * a, 16 * b), c("K3", 0, 16 * (b - a)), c("GS", 16 * a, 16 * b), A.min, A.max)
-            spread(a, b, c("MNS", 16 * a + 15, 16 * b, 16), c("MXS", 16 * a + 15, 16 * b, 16))
-        for a, b in pieces:
-            scan(c("MX", 8 * a, 8 * b), c("G", 16 * a, 16 * b, 2), c("G", 16 * a + 1, 16 * b, 2), A.max, A.max, -2000.0)
-            spread(a, b, c("MN", 8 * a, 8 * b, 8), c("MX", 8 * a + 7, 8 * b, 8))
+        for x in SCANS if nv < ns else "nx":
+            if x == "n":
+                scan(c("MN", 8 * nv - 1, -1, -1), c("G", 16 * nv - 1, -1, -2), c("G", 16 * nv - 2, -1, -2), A.min, A.min, 4000.0)
+                mm([(c("PN", 256, 256 + nv), ID, c("MN", 0, 8 * nv, 8), True, False),
+                    (c("PN", 256, 256 + nv), NI, c("RA", 0, 16 * nv, 16), False, True)])
+            elif x == "x":
+                scan(c("MX", 0, 8 * nv), c("G", 0, 16 * nv, 2), c("G", 1, 16 * nv, 2), A.max, A.max, -4000.0)
+                spread(0, nv, c("MN", 0, 8 * nv, 8), c("MX", 7, 8 * nv, 8))
+            elif x == "N":
+                scan(c("MNS", 16 * nv, 16 * ns), c("K2", 0, 16 * (ns - nv)), c("GS", 16 * nv, 16 * ns), A.max, A.min)
+                mm([(c("PN", 256 + nv, 256 + ns), ID, c("MNS", 16 * nv + 15, 16 * ns, 16), True, True)])
+            else:
+                scan(c("MXS", 16 * nv, 16 * ns), c("K3", 0, 16 * (ns - nv)), c("GS", 16 * nv, 16 * ns), A.min, A.max)
+                spread(nv, ns, c("MNS", 16 * nv + 15, 16 * ns, 16), c("MXS", 16 * nv + 15, 16 * ns, 16))
+        if t == 0:
+            mm([(c("PG", 384, 385), B1, c("ONE", 0, 1), True, False), (c("PG", 384, 385), NU, c("ONE", 0, 1), False, True)])
         ts(c("FL", 0, ns), c("PN", 256, 256 + ns), 2.0, A.is_ge)
+        naming_v(1)
         tt(c("RES", 0, ns), c("PS", 128, 128 + ns), c("FL", 0, ns), A.mult)
+        naming_v(2)
         if t == 0:
             tt(c(Y, 896, NV), c("RES", 0, 128), c(Y, 896, NV), A.max)
+        elif SEARCH:
+            tt(ind(c(Y), c("NL")), c("RES", 0, 256), c("ONE", 0, 256), A.add)
         else:
             tt(c(Y, 0, NV), ind(c("RES"), c("RK")), c(Y, 0, NV), A.max)
 
         diagonal(Y, True, True)
+        mm([(c("PY", 0, 512), ID, c(Y, 0, 512), True, cut > 0)])
         if t == 0:
-            ts(c("PI2"), c("PI"), 15, A.bitwise_and)
-            cp(c("CC"), c("PI2"))
+            ts(c("CC"), c("PG", 384, 385), -1.0, A.add)
+            cp(c(YN, NV), c(Y, NV))
             ts(c("SG"), c("SI"), c("CC"), A.add)
-            fill(c("WR", 0, 1), 0.0)
-            fill(c("WR", 41, SEG), 1.0)
-            ts(c("I16"), ID, 16.0, A.mult)
             mm([(c("PL", 256 + 40, 256 + 60), ID, c("ONE", 0, 20), True, True)])
         elif last:
             ts(c("OY", 0, RING0), c(Y, 0, RING0), -2.0, A.add, -1.0, A.max)
@@ -421,11 +515,12 @@ def rank_program(g, core, T, topo):
             dma("q", "o_a", [], [c("OY", 0, RING0), c("OY", 896, NV), c("OF", 0, RING0), c("OF", 896, NV)],
                 [(T.yy[:, 0:RING0], T.OY[:, 0:RING0]), (T.yy[:, 896:NV], T.OY[:, 896:NV]),
                  (T.yf[:, 0:RING0], T.OF[:, 0:RING0]), (T.yf[:, 896:NV], T.OF[:, 896:NV])])
-        naming_v(1)
+        naming_v(3)
         s0 = (9 * t) % 40
         parts = [(s0, 40, 1)] + ([(0, s0, 41 - s0)] if s0 else [])
         for a, b, x in parts:
             ts(c("WR", x, x + b - a), c("PD", 16 + a, 16 + b), 2.0, A.is_ge)
+        naming_v(4)
         scan(c("ER", 0, SEG), c("WR", 0, SEG), c("WR", 0, SEG), A.add, A.max)
         mm([(c("PK", 64 + SEG * j, 64 + SEG * (j + 1)), B1, c("ER", 0, SEG), True, True) for j in range(6)])
         items = []
@@ -433,98 +528,149 @@ def rank_program(g, core, T, topo):
             items += [(c("PL", 256 + a, 256 + b), B1, c("ER", x, x + b - a), True, False),
                       (c("PL", 256 + a, 256 + b), NU, c("WR", x, x + b - a), False, True)]
         mm(items)
-        mm([(c("PY%d" % j), ID, c(Y, 512 * j, 512 * j + 512), True, not marks) for j in (0, 1)])
+        mm([(c("PY", 512), ID, c(Y, 512, NV), True, False)])
         if t == 0:
-            ts(c("IH"), ID, -256.0, A.mult)
             ts(c("BF"), B1, -32.0, A.mult)
             fill(c("CX"), -0.9375)
-        naming_v(2)
+            fill(c(MW, 0, DUMP), 0.0)
+        naming_v(5)
         tt(c("GT"), c("PK", 64, 64 + 6 * SEG), c("SG"), A.is_gt)
-        scan(c("BS"), c("GT"), c("D"), A.mult, A.add)
         cp(c("RT", 0, 66), c("PL", 256, 256 + 66))
+        naming_v(10)
+        scan(c("BS"), c("GT"), c("D"), A.mult, A.add)
+        naming_v(6)
         ends = c("BS", SEG - 1, None, SEG)
         ts(c("BL"), ends, 0.0, A.add)
+        naming_v(7)
         tt(c("X1"), ind(c("RT", 0, 66), c("BL")), c("SF"), A.is_le)
         o = c("PG", 384, 390)
         mm([(o, c("I16"), ends, True, False)]
            + [(o, c("ZB", 16 - i, 144 - i), c("X1", i, None, 16), False, i == 15) for i in range(16)])
-        if t == 0:
-            ts(c("PRF", 512, NV), c("PR", 512, NV), OFF + 0.125, A.add)
-        naming_v(3)
+        if t == 0 and SEARCH:
+            fill(c("DL"), DELTA)
+            ts(c("B2"), B1, 2048.0, A.mult)
+            fill(c("W", 64), 1.0)
+            fill(c("E", 0, 1), 0.0)
+        elif t == 0:
+            ts(c("PRF"), c("PR", 0, NV), OFF + 0.125, A.add)
+        if 0 < cut < 512:
+            mm([(c("PY", 512), ID, c("YT", 512, NV), False, not marks), (c("PY", 0, 512), ID, c("YT", 0, 512), True, False),
+                (c("PY", cut, 512), ID, c(Y, cut, 512), False, not marks)])
+        else:
+            mm([(c("PY", a, a + 512), ID, c("YT", a, a + 512), a < cut, not marks) for a in (512, 0)])
+        naming_v(8)
         cp(CL, o)
-        cp(c("PRL"), ind(c("PR", RING0), CL))
-        naming_v(4)
-        if marks:
-            mm([(c("PY%d" % j), ID, c(MV, 512 * j, 512 * j + 512), False, True) for j in (0, 1)], True)
-        cp(c("COL"), ind(c("CO"), CL))
-        cp(c("OI"), ind(c(Y, RING0), CL))
-        if t == 0:
-            ts(c("PRF", 0, 512), c("PR", 0, 512), OFF + 0.125, A.add)
-        ts(c("OD"), c("OI"), 1, A.bitwise_and)
-        tt(c("OM"), ind(c("MO"), CL), c("OD"), A.mult)
-
         act(c("NN"), c(M, NV, DUMP), F.Identity, 0.0, 1.0)
-        turn([("NN", 0)] + [(x, NV) for x in marks], "PN")
+        if TURN_FIRST:
+            turn([(x, NV) for x in ["YT"] + marks] + [("NN", 0)], "PN")
+        if marks:
+            mm([(c("PY", a, a + 512), ID, c(MV, a, a + 512), False, True) for a in (512, 0)], True)
+        if not TURN_FIRST:
+            turn([(x, NV) for x in ["YT"] + marks] + [("NN", 0)], "PN")
+        cp(c("PRL"), ind(c("PR", RING0), CL))
+        cp(c("OI"), ind(c(Y, RING0), CL))
+        cp(c("COL"), ind(c("CO"), CL))
+        ts(c("OD"), c("OI"), 1, A.bitwise_and)
+
+        def dirty(a, b):
+            if a < b:
+                act(c("DG", 16 * a, 16 * b), ind(c(Y), c("PRL", a, b)), F.Relu, 4.0, -2.0)
+
+        dv, d1, d2 = D_V[later]
+        hv = H_V[later]
         act(c("SN"), c("PD", 0, 64), F.Sign, -1.5, 1.0, c("CN"))
+        dirty(dv, d2)
         act(block("NM", t), c("PN", 0, NG), F.Sign, 0.0, 1.0)
-        exchange("NM", "LN", t, "nt")
+        exchange("NM", "LN", t, "nt", "nn" if NEAR else None)
         if t == 0:
-            iota(c(MW, 0, DUMP), [[0, DUMP]], 0)
-            iota(c("TF"), [[-16, 64]], FAR)
+            if SEARCH:
+                iota(c("XI"), [[0, 16], [1, 16]], 0)
+                iota(c("XJ"), [[0, 5], [1, 16], [100, 2]], 0)
+                iota(c("CI"), [[16, 5], [1, 16], [0, 2]], 1)
+                sel(c("CJ"), c("CI"), [[0, NC], [1, 2]], A.is_equal, 0, 0, float(Z0_))
+            else:
+                iota(c("TF"), [[-16, 64]], FAR)
+            iota(c("CF", 0, None, 2), [[0, K2]], 8192)
             iota(c("PH", 0, RINGN), [[0, RINGN]], 0)
-            iota(c("WV", 0, 256), [[1, 256]], DUMP + OFF)
-            iota(c("WS", 0, 256), [[1, 256]], DUMP + OFF)
+            clear_lists()
+        elif not last:
+            iota(c("MB", 0, DUMP), [[0, DUMP]], 0)
         left = c("PK", 480, 481)
         mm([(left, c("BF"), c("CX"), True, False), (left, c("BF"), c("CN"), False, True)])
-        dv, hv = D_V[later], H_V[later]
         if dv:
             ts(c("DG", 0, 16 * dv), ind(c(Y), c("PRL", 0, dv)), 2.0, A.is_lt)
-        if dv < K2:
-            act(c("DG", 16 * dv), ind(c(Y), c("PRL", dv)), F.Relu, 4.0, -2.0)
-        for j in (0, 1):
-            tt(c(YN, 512 * j, 512 * j + 512), c("PY%d" % j), c(M, 512 * j, 512 * j + 512), A.max)
+        dirty(d2, K2)
+        tt(c(YN, 0, NV), c("PY"), c(M, 0, NV), A.max)
+        tt(c("OM"), ind(c("MO"), CL), c("OD"), A.mult)
+        if last:
+            mm([(c("PY", a, b), l, c(n, x + a, x + b), n == "PH", n != "PH")
+                for a, b in ((0, 512), (512, RINGN)) for l, n, x in ((ID, "PH", 0), (NI, YN, RING0))])
         mm(sums(c("PS", 0, K2), "DG", 0, K2, ID, True))
-        held = c("PK", 384, 384 + K2)
+        held = c("PK", 256, 256 + 2 * K2, 2)
+        act(c("OC"), ind(c(Y, RING0), CL), F.Identity, 0.0, 1.0)
+        mm([(c("PK", 257, 256 + 2 * K2, 2), ID, c("OC"), True, True)])
         for a, x, b in hv:
             act(c("HG", 16 * x, 16 * b), ind(c(YN), c("COL", x, b)), F.Silu, 318.75, -320.0)
             ts(c("HG", 16 * a, 16 * x), ind(c(YN), c("COL", a, x)), 1.0, A.is_equal, -0.25, A.mult)
-            o = c("PK", 384 + a, 384 + b)
-            mm([(o, ID, c("ONE", 0, b - a), True, False)] + sums(o, "HG", a, b, c("IH"), False))
+            o = c("PK", 256 + 2 * a, 256 + 2 * b, 2)
+            mm([(o, ID, c("ONE", 0, b - a), True, False)] + sums(o, "HG", a, b, IH, False))
         tt(c("FF"), c("PS", 0, K2), c("OM"), A.min)
         mm([(c("PG", 256, 256 + K2), B1, c("FF"), True, True)])
-        act(c("OC"), ind(c(Y, RING0), CL), F.Identity, 0.0, 1.0)
+        if last:
+            act(c("OF", RING0, 896), c("PY", 0, RINGN), F.Relu, -0.001, 1.0)
         act(c("A8"), c("PG", 256, 256 + K2), F.Abs, -8.0, 1.0)
         act(c("CD"), c("A8"), F.Silu, -1600.006, 200.0)
-        tt(ind(c(MW, 0, NV), BD), block("LN", t), c("AB"), A.mult)
-        diagonal(MW, True, False, last)
-        if last:
-            tt(ind(c("PH"), CL), c("FF"), c("FF"), A.add)
+        def notices(j):
+            if j in NOTES:
+                a, b = NOTES[j]
+                tt(ind(c(MW, 0, NV), c("BD", a // 16, b // 16)), c("LN", NG * t + a, NG * t + b), c("AB", a, b), A.mult)
+                if j == max(NOTES):
+                    diagonal(MW, j < 4, j == 4, last)
+
+        notices(0)
+
+        if t == 0:
+            if SEARCH:
+                payload(64, NC, 76)()
         ts(c("FR"), held, 2.0, A.is_lt, 32.0, A.mult)
-        scan(c("CF"), c("FR"), c("FR"), A.add, A.add, left)
-        tt(c("U"), held, c("CF"), A.max)
-        tt(c("KO"), c("OC"), c("U"), A.min)
-        tt(ind(c(YN, RING0), CL), c("KO"), c("CD"), A.add)
-        diagonal(YN, False, True, last)
+        notices(1)
+        if last:
+            ts(c("OY", RING0, 896), c(Y, RING0, 896), -2.0, A.add, -1.0, A.max)
+            fill(c("OM"), -2.0)
+        scan(c("CF", 1, None, 2), c("FR"), c("FR"), A.add, A.add, left)
+        notices(2)
+        scan(c("KO"), c("CF"), c("PK", 256, 256 + 2 * K2), A.max, A.min)
+        notices(3)
+        if last:
+            for x in TAIL:
+                ring_out(x)
+            ts(c("FR"), KO, 2.0, A.is_lt)
+        tt(ind(c(YN, RING0), CL), KO, c("CD"), A.add)
+        diagonal(YN, 4 in NOTES, 4 not in NOTES, last)
+        notices(4)
 
         if not last:
-            border(YN, t + 1, -1.5)
+            if not SEARCH:
+                if t == 0:
+                    ts(c("TT"), c("TF"), c("CC"), A.subtract)
+                tt(ind(c("PH"), CL), c("FF"), c("FF"), A.add)
+            elif t == 0:
+                for u in (0, 1):
+                    ts(c("NE", u, None, 2), c("XI", 0, NC), c("CC"), A.not_equal, BIG, A.mult)
+                ts(c("H0"), c("XJ"), c("CC"), A.is_equal, BIG, A.mult)
+                ts(c("MK"), c("XI"), c("CC"), A.is_le, BIG, A.mult)
+            border(YN, t + 1, -GHOST)
             if t == 0:
-                ts(c("TT"), c("TF"), c("CC"), A.subtract)
-                iota(c("M1", 0, DUMP), [[0, DUMP]], 0)
-                iota(c("K2"), [[0, 64], [-40, 16]], 32)
-                iota(c("K3"), [[0, 64], [40, 16]], -8)
-                iota(c("RES", 256), [[0, FAR - 256]], 0)
-            tt(ind(c("PH"), CL), c("FF"), c("FF"), A.add)
+                iota(c("K2", 16 * T0_S, 16 * S_SLOTS), [[0, S_SLOTS - T0_S], [-40, 16]], 32)
+                iota(c("K3", 16 * T0_S, 16 * S_SLOTS), [[0, S_SLOTS - T0_S], [40, 16]], -8)
+                if not SEARCH:
+                    iota(c("RES", 256), [[0, FAR - 256]], 0)
 
-    for j, (a, b) in enumerate(((0, 512), (512, RINGN))):
-        o = c("PY%d" % j, 0, b - a)
-        mm([(o, ID, c("PH", a, b), True, False), (o, NI, c(YN, RING0 + a, RING0 + b), False, True)])
-        act(c("OF", RING0 + a, RING0 + b), o, F.Relu, -0.001, 1.0)
-    ts(c("OY", RING0, 896), c(YN, RING0, 896), -2.0, A.add, -1.0, A.max)
-    dma("q", "o_y", [], [c("OY", RING0, 896)], [(T.yy[:, RING0:896], T.OY[:, RING0:896])])
+    for x in "yf":
+        if x not in TAIL:
+            ring_out(x)
     wanted(c("OW"))
     dma("q", "o_w", [], [c("OW")], [(T.yw[:, :], T.OW[:, :])])
-    dma("s", "o_f", [], [c("OF", RING0, 896)], [(T.yf[:, RING0:896], T.OF[:, RING0:896])])
     g.wait_ge(T.sem.sent, (sent[0] - 1) * sum(ENG))
     for sem, n in list(count.items()) + list(dmas.items()):
         need("q", (sem, n))

@@ -6,35 +6,43 @@ DUMP = NV + NG
 YW_ = DUMP + 256
 RING0, RINGN = 256, 640
 TW = DUMP + K2 - RING0
-SEG = 47
-NC = 80
+NC, NR = 80, 48
 Z0_ = 96
 DELTA = 1.0 / 256
 BIG = 29952.0
-SEARCH = False
-OFF = 32
-FAR = NV + 256
 TAG = 2.0 ** -9
 GHOST = 1.25
 SILU_ONE = 1.278464542761074
 ROUND = 65536.0 + 2.0 ** -7
 STEP = 18
-S_SLOTS = 120
-PIECE = 256 - S_SLOTS
-V_FIRST = 80
-V_NAME = {1: 16, 3: 16, 5: 16, 8: 16}
-D_V = ((24, 24, 24), (28, 28, 52))
-TURNS = (7, 5)
-EARLY = {6: (0, 128), 7: (128, 256)}
-NOTES = {0: (0, 64), 2: (64, 192)}
-NEAR = 1
-T0_S, T0_AT, V_NAME0 = 32, 4, {}
-SPLIT_C = True
-TAIL = "y"
-SCANS = "NnXx"
+
+S_SLOTS = (32, 128)
+RAMP = 128
+LS_FIRST = True
+V_FIRST = 76
+FILL = ({"L0": [8], "L1": [8], "L2": [8], "L3": [8], "B": [8], "C": [8], "Z": ["G"]},
+        {"1": [8], "s": [8], "A": [16, "X0"], "W": ["X1"], "B": [16], "B4": ["X2"], "C": [16], "C2": ["X3"], "D0": [16], "D": ["x"]})
+T0_AT = 16
 TURN_FIRST = True
-S_LATE = 0
-H_V = (((0, 24, 48), (48, 72, 96)),) * 2
+SCANS = ("nxNX", "NnXx")
+EARLY = {"e": (0, 128), "f": (128, 256)}
+TURNS = (0, 4)
+FL_AT = (None, 4)
+PY_EARLY = True
+DEFER = (True, True)
+ODD_S = False
+D_LATE = 0
+PARTS = 4
+MINS = ("nNfoFcd", "NnF1f")
+RES_ON = "s"
+LS_MODE, V_ZERO = 2, 16
+YT_G = (512, 1)
+TAIL_FIRST = True
+TAIL = "y"
+D_V = ((48, 64, 64), (12, 60, 60))
+H_V = (((0, 28, 48), (48, 72, 96)), ((0, 28, 48), (48, 70, 96)))
+OUT_AT = {1: "ac", 2: "r"}
+NOTES = {1: (0, 64), 2: (64, 192)}
 ENG = (4, 4, 4)
 
 
@@ -43,37 +51,33 @@ def _sb(n, d):
 
 
 SCRATCH = {
-    "YA": _sb(YW_, "bfloat16"), "YB": _sb(YW_, "bfloat16"), "Y0": _sb(NV, "bfloat16"),
+    "YA": _sb(YW_, "bfloat16"), "YB": _sb(YW_, "bfloat16"), "Y0": _sb(YW_, "bfloat16"),
     "PR": _sb(YW_, "int32"), "CO": _sb(TW, "int32"), "MO": _sb(TW, "int32"),
     "BDI": _sb(12, "int32"), "BD": _sb(12, "uint16"), "AB": _sb(NG, "bfloat16"), "NN": _sb(NG, "bfloat16"),
     "MB": _sb(YW_, "float32"), "YT": _sb(DUMP, "bfloat16"),
-    "W": _sb(NC, "bfloat16"), "E": _sb(NC + 1, "bfloat16"), "PAY": _sb(NC, "float32"), "PP": _sb(2 * NC, "float32"),
-    "ZL": _sb(6, "uint16"), "Z": _sb(Z0_ + 16 * NC, "float32"), "X": _sb(256, "float16"), "NP": _sb(256, "float32"),
-    "NL": _sb(16, "uint16"), "XI": _sb(256, "bfloat16"), "XJ": _sb(2 * NC, "bfloat16"), "CI": _sb(2 * NC, "bfloat16"),
+    "W": _sb(NC, "bfloat16"), "E": _sb(NC + 2, "bfloat16"), "WR": _sb(NR, "bfloat16"), "ER": _sb(NR + 2, "bfloat16"),
+    "PAY": _sb(NC, "float32"), "PP": _sb(2 * NC, "float32"), "ZL": _sb(6, "uint16"),
+    "Z": _sb(Z0_ + 16 * NC, "float32"), "ZR": _sb(Z0_ + 16 * NR, "float32"), "X": _sb(256, "float16"),
+    "NL": _sb(16, "uint16"), "XI": _sb(2 * NC, "bfloat16"),
     "CJ": _sb(2 * NC, "bfloat16"), "NE": _sb(2 * NC, "bfloat16"), "H0": _sb(2 * NC, "bfloat16"),
-    "MK": _sb(256, "bfloat16"), "DL": _sb(256, "bfloat16"), "B2": _sb(128, "bfloat16"),
+    "DL": _sb(256, "bfloat16"), "B2": _sb(128, "bfloat16"),
     "C": _sb(256, "float16"), "CT": _sb(256, "float16"), "LS": _sb(256, "uint16"), "L": _sb(256, "uint16"),
     "C0": _sb(128, "float32"), "C1": _sb(128, "float32"), "DS": _sb(128, "float32"),
-    "G": _sb(4096, "float16"), "GS": _sb(4096, "bfloat16"), "MX": _sb(2048, "float16"), "MN": _sb(2048, "float16"),
-    "MXS": _sb(4096, "bfloat16"), "MNS": _sb(4096, "bfloat16"),
-    "K2": _sb(2560, "bfloat16"), "K3": _sb(2560, "bfloat16"), "R0": _sb(3072, "float16"), "RA": _sb(3072, "float16"),
-    "FL": _sb(256, "bfloat16"), "RES": _sb(FAR, "bfloat16"), "PRF": _sb(NV, "float32"),
-    "WV": _sb(FAR, "float32"), "WS": _sb(FAR, "float32"), "WT": _sb(64, "float16"), "TT": _sb(64, "float16"),
-    "TF": _sb(64, "float32"), "RK": _sb(64, "uint16"), "OC": _sb(K2, "bfloat16"),
-    "WR": _sb(48, "bfloat16"), "ER": _sb(48, "bfloat16"), "SI": _sb(6 * SEG, "bfloat16"), "SG": _sb(6 * SEG, "bfloat16"),
-    "GT": _sb(6 * SEG, "bfloat16"), "D0": _sb(6 * SEG, "bfloat16"), "D1": _sb(6 * SEG, "bfloat16"), "D": _sb(6 * SEG, "bfloat16"),
-    "BS": _sb(6 * SEG, "bfloat16"), "BL": _sb(6, "uint16"), "RT": _sb(80, "bfloat16"), "SF": _sb(K2, "bfloat16"),
-    "X1": _sb(K2, "bfloat16"), "SIL": _sb(256, "float32"), "SN": _sb(64, "bfloat16"), "CN": _sb(1, "float32"),
-    "CC": _sb(1, "float32"), "CX": _sb(1, "float32"),
+    "G": _sb(3072, "float16"), "GS": _sb(3072, "bfloat16"), "MX": _sb(1536, "float16"), "MN": _sb(1536, "float16"),
+    "MXS": _sb(3072, "bfloat16"), "MNS": _sb(3072, "bfloat16"), "K2": _sb(3072, "bfloat16"), "K3": _sb(3072, "bfloat16"),
+    "R0": _sb(3072, "bfloat16"), "RA": _sb(3072, "float16"), "R2": _sb(192, "float16"), "I32": _sb(128, "bfloat16"), "IT": _sb(128, "bfloat16"),
+    "I64": _sb(128, "bfloat16"), "IN": _sb(128, "bfloat16"), "MF": _sb(TW, "bfloat16"), "O1": _sb(K2, "bfloat16"), "O2": _sb(K2, "bfloat16"),
+    "FL": _sb(256, "bfloat16"), "RES": _sb(256, "bfloat16"), "OC": _sb(K2, "bfloat16"), "SF": _sb(112, "bfloat16"),
+    "SG": _sb(6, "bfloat16"), "WI": _sb(6, "bfloat16"),
+    "SIL": _sb(256, "float32"), "SN": _sb(64, "bfloat16"), "CN": _sb(1, "float32"), "CC": _sb(1, "float32"), "CX": _sb(1, "float32"),
     "CL": _sb(6, "uint16"), "COL": _sb(K2, "uint16"), "PRL": _sb(K2, "uint16"),
     "DG": _sb(1536, "bfloat16"), "HG": _sb(1536, "bfloat16"), "TAG": _sb(256, "bfloat16"),
     "OI": _sb(K2, "int32"), "OD": _sb(K2, "int32"), "OM": _sb(K2, "bfloat16"), "FF": _sb(K2, "bfloat16"),
     "A8": _sb(K2, "float32"), "CD": _sb(K2, "bfloat16"), "FR": _sb(K2, "bfloat16"), "CF": _sb(2 * K2, "bfloat16"),
     "KO": _sb(2 * K2, "bfloat16"),
     "PH": _sb(TW, "bfloat16"), "OY": _sb(RING0 + TW, "bfloat16"), "OF": _sb(RING0 + TW, "bfloat16"), "OW": _sb(64, "bfloat16"),
-    "ONE": _sb(288, "bfloat16"),
-    "Z0": _sb(160, "bfloat16"), "Z1": _sb(160, "bfloat16"), "ZS": _sb(160, "bfloat16"), "ZA": _sb(160, "bfloat16"),
-    "ZB": _sb(160, "bfloat16"), "ID": _sb(128, "bfloat16"), "I16": _sb(128, "bfloat16"), "IH": _sb(128, "bfloat16"),
+    "ONE": _sb(256, "bfloat16"), "Z0": _sb(160, "bfloat16"), "Z1": _sb(160, "bfloat16"),
+    "ZB": _sb(160, "bfloat16"), "ID": _sb(128, "bfloat16"), "IH": _sb(128, "bfloat16"),
     "B0": _sb(128, "bfloat16"), "B1": _sb(128, "bfloat16"), "NB": _sb(128, "bfloat16"), "NU": _sb(128, "bfloat16"),
     "NI": _sb(128, "bfloat16"), "BF": _sb(128, "float32"), "P1": _sb(128, "bfloat16"), "P2": _sb(128, "bfloat16"),
 }
@@ -86,7 +90,7 @@ PSUM = ("PD", "PK", "PL", "PG", "PN", "PS", "PY")
 for _n in PSUM:
     SCRATCH[_n] = ("psum", [128, NV if _n == "PY" else 512], "float32")
 
-SEMAPHORES = (["v", "s", "p", "g", "first", "sent", "d_y", "d_bd", "d_pt", "d_pr", "d_pa", "d_co", "d_mo", "o_a", "o_y", "o_f", "o_w"]
+SEMAPHORES = (["v", "s", "p", "g", "first", "sent", "d_y", "d_yt", "d_bd", "d_pt", "d_pr", "d_pa", "d_co", "d_mo", "o_a", "o_b", "o_c", "o_y", "o_f", "o_w"]
               + ["gh%d" % t for t in range(RO)] + ["nt%d" % t for t in range(RO)] + ["nn%d" % t for t in range(RO)])
 
 
@@ -129,7 +133,7 @@ def rank_program(g, core, T, topo):
         for (name, a, b), writes in [(x, True) for x in w] + [(x, False) for x in r]:
             for lo, hi, m, wrote, q in log.get(name, []):
                 meet = lo < b and a < hi and (writes or wrote) and not (more and q == e and name in PSUM)
-                if meet or (name in PSUM and q != e):
+                if meet or (name in PSUM and q != e and lo // 512 <= (b - 1) // 512 and a // 512 <= (hi - 1) // 512):
                     marks[m[0]] = max(marks.get(m[0], 0), m[1])
         for m in marks.items():
             need(e, m)
@@ -139,7 +143,7 @@ def rank_program(g, core, T, topo):
         for (name, a, b), writes in [(x, False) for x in r] + [(x, True) for x in w]:
             old = log.get(name, [])
             if name in PSUM:
-                old = [x for x in old if x[4] == e]
+                old = [x for x in old if x[4] == e or x[0] // 512 > (b - 1) // 512 or a // 512 > (x[1] - 1) // 512]
             old = [x for x in old if not (a <= x[0] and x[1] <= b and (writes or (x[4] == e and not x[3] and x[2][0] == mark[0])))]
             log[name] = old + [[a, b, mark, writes, e]]
 
@@ -231,10 +235,16 @@ def rank_program(g, core, T, topo):
         else:
             op("g", [out], [], lambda: g.iota(out["ap"], pat, base, cm, allow_small_or_imprecise_dtypes=True))
 
+    def clear(out):
+        iota(out, [[0, out["at"][2] - out["at"][1]]], 0)
+
     def sel(out, a, pat, cmp, base, cm, other=0.0):
         op("g", [out], [a], lambda: g.affine_select(out["ap"], a["ap"], pat, cmp, other, base, cm))
 
-    CL, BD, KO = c("CL"), c("BD"), c("KO", 1, None, 2)
+    def narrow(out, a):
+        sel(out, a, [[0, out["at"][2] - out["at"][1]]], A.is_equal, 0, 0)
+
+    CL, NL, BD, KO = c("CL"), c("NL"), c("BD"), c("KO", 1, None, 2)
     ID, NI, B1, NU, IH = c("ID"), c("NI"), c("B1"), c("NU"), c("IH")
 
     def block(name, t):
@@ -250,28 +260,49 @@ def rank_program(g, core, T, topo):
         act(c("AB"), block("BN", t), F.Relu, TAG, -0.012)
 
     def diagonal(name, first, final, blocks=False):
-        mm([(c("PD", 0, 64), c("ZS", 16 - i, 144 - i), c(name, 64 * i, 64 * i + 64) if blocks else c(name, i, NV, 16),
+        mm([(c("PD", 0, 64), c("ZB", 16 - i, 144 - i), c(name, 64 * i, 64 * i + 64) if blocks else c(name, i, NV, 16),
              first and i == 0, final and i == 15) for i in range(16)], not first)
 
     def wanted(out):
-        ts(out, c("PD", 0, 64), ROUND, A.add, ROUND + 1.0, A.is_equal)
+        ts(out, c("PD", 0, 64), 16 * ROUND, A.add, 16 * (ROUND + 1.0), A.is_equal)
 
     def sums(out, name, a, b, lhs, first):
         return [(out, lhs, c(name, 16 * a + k, 16 * b, 16), first and k == 0, k == 15) for k in range(16)]
 
-    def ring_table(t):
-        s0 = (9 * t) % 40
-        src = "D0"
-        if s0:
-            sel(c("D1"), c("D0"), [[0, 6], [1, SEG]], A.not_equal, -(39 - s0), 0, 39.0)
-            src = "D1"
-        sel(c("D"), c(src), [[0, 6], [1, SEG]], A.not_equal, -39, 0, float((s0 - 1) % 40 - 60))
+    def search_tables(n, numbers):
+        mm([(c("PK", 0, 2 * n), ID, c("NE", 0, 2 * n), True, False), (c("PK", 0, 2 * n), ID, c("CJ", 0, 2 * n), False, False)])
+        at, items = 0, []
+        for a, b in numbers:
+            items.append((c("PN", at, at + b - a), IH, c("SF", a, b), at == 0, False))
+            at += b - a
+        mm(items)
 
-    def payload(a, b, first):
-        o = c("PN", a, b)
-        mm([(o, IH, c("SF", first, first + b - a), True, False)])
-        return lambda: (mm([(o, B1, c("W", a, b), False, False), (o, NU, c("W", a, b), False, True)], True),
-                        act(c("PAY", a, b), o, F.Identity, 1024.5 - DELTA / 2, -DELTA))
+    def search(w, e, n, z, slots, out, on_scalar, wait, wrap=0):
+        W = c(w, 0, n)
+        scan(c(e, 1, n + 1), W, W, A.add, A.max)
+        mm([(c("PN", 0, n), B1, W, False, False), (c("PN", 0, n), NU, W, False, True)], True)
+        mm([(c("PK", 0, 2 * n, 2), c("B2"), W, False, False), (c("PK", 1, 2 * n, 2), B1, c(e, 0, n), False, True)], True)
+        if wrap:
+            mm([(c("PN", 128, 129), B1, c(e, wrap, wrap + 1), True, True)])
+        wait("B")
+        if on_scalar:
+            act(c("PAY", 0, n), c("PN", 0, n), F.Identity, 1024.5 - DELTA / 2, -DELTA)
+        scan(c("PP", 0, 2 * n), c("H0", 0, 2 * n), c("PK", 0, 2 * n), A.max, A.min)
+        if not on_scalar:
+            ts(c("PAY", 0, n), c("PN", 0, n), -DELTA, A.mult, 1024.5 - DELTA / 2, A.add)
+        wait("B2")
+        cp(c("ZL", 0, n // 16), c("PP", 31, 2 * n, 32))
+        if wrap:
+            ts(c("WI"), c("SG"), c("PN", 128, 129), A.is_ge, -float(RINGN), A.mult)
+        wait("B3")
+        cp(ind(c(z), c("ZL", 0, n // 16)), c("PAY", 0, n))
+        wait("B4")
+        scan(c("X", 0, slots), c(z, Z0_, Z0_ + slots), c("DL", 0, slots), A.max, A.add)
+        o = c("PS", 0, slots // 16)
+        mm([(o, ID, c("WI"), True, False)] * min(wrap, 1)
+           + [(o, c("ZB", 16 - i, 144 - i), c("X", i, slots, 16), i == 0 and not wrap, i == 15) for i in range(16)])
+        wait("C")
+        ts(out, o, -16384.0, A.add)
 
     def ring_out(x):
         if x == "y":
@@ -281,109 +312,149 @@ def rank_program(g, core, T, topo):
             tt(ind(c("OF", RING0), CL), c("FF"), c("FR"), A.mult)
             dma("s", "o_f", [], [c("OF", RING0, 896)], [(T.yf[:, RING0:896], T.OF[:, RING0:896])])
 
-    def clear_lists():
-        if SEARCH:
-            iota(c("Z", Z0_, Z0_ + 256), [[0, 256]], 0)
-        else:
-            iota(c("WV", 0, 256), [[1, 256]], DUMP + OFF)
-            iota(c("WS", 0, 256), [[1, 256]], DUMP + OFF)
-
-    dma("q", "d_y", [c("Y0")], [], [(T.Y0[:, :], T.y0[:, :])])
     dma("s", "d_bd", [c("BDI")], [], [(T.BDI[:, :], T.bd[:, :])])
-    dma("q", "d_pt", [c("PR", 896, NV)], [], [(T.PR[:, 896:NV], T.pr[:, 896:NV])])
+    if TAIL_FIRST:
+        dma("q", "d_yt", [c("Y0", 896, NV)], [], [(T.Y0[:, 896:NV], T.y0[:, 896:NV])])
+        dma("s", "d_pt", [c("PR", 896, NV)], [], [(T.PR[:, 896:NV], T.pr[:, 896:NV])])
+        dma("q", "d_y", [c("Y0", 0, 896)], [], [(T.Y0[:, 0:896], T.y0[:, 0:896])])
+    else:
+        dma("q", "d_y", [c("Y0", 0, NV)], [], [(T.Y0[:, 0:NV], T.y0[:, :])])
+        dma("q", "d_pt", [c("PR", 896, NV)], [], [(T.PR[:, 896:NV], T.pr[:, 896:NV])])
+    dma("q", "d_pr", [c("PR", RING0, 896)], [], [(T.PR[:, RING0:896], T.pr[:, RING0:896])])
 
     fill(c("ONE"), 1.0)
-    act(c("TAG"), c("ONE", 0, 256), F.Silu, 0.0, 0.0039025)
-    sel(ID, c("ONE", 0, 128), [[-1, 128]], A.is_equal, 0, 1)
+    act(c("TAG"), c("ONE"), F.Silu, 0.0, 0.0039025)
     iota(c("DS"), [[1, 128]], DUMP)
+    sel(c("B0"), c("ONE", 0, 128), [[-1, 8], [0, 16]], A.is_equal, 0, 1)
+    sel(ID, c("ONE", 0, 128), [[-1, 128]], A.is_equal, 0, 1)
+    mm([(c("PG", 0, 128), c("B0"), c("B0"), True, True)])
+    ramp0 = max(128 - S_SLOTS[0], DUMP // 16)
+    ramp_low = -float(STEP * (RAMP // 2 + 1))
+    fill(c("R0", 0, 16 * ramp0), 0.0)
+    fill(c("SIL"), SILU_ONE)
+    cp(B1, c("PG", 0, 128))
+    ts(c("NB"), c("PG", 0, 128), -1.0, A.mult)
+    fill(c("ZB"), 0.0)
+    fill(c("MV0", 0, DUMP), 0.0)
     for h, z in ((0, "Z0"), (1, "Z1")):
         sel(c(z), c("ONE", 0, 160), [[-32, 5], [984, 2], [-1, 16]], A.is_equal, 16 - 1000 * (1 - h), 1)
-    fill(c("M0", 0, DUMP), 0.0)
-    fill(c("SIL"), SILU_ONE)
+    sel(NU, c("NB"), [[-1, 128]], A.is_gt, 0, 1)
+    iota(c("XI"), [[0, 5], [1, 16], [0, 2]], 0)
+    iota(c("SF"), [[1, 112]], 0)
+    times(c("M0", 0, DUMP), c("R0", 0, DUMP), 0.0)
     cp(BD, c("BDI"))
-    ramp = max(128, PIECE)
-    fill(c("R0", 0, 16 * ramp), 0.0)
-    times(NI, ID, -1.0)
     times(IH, ID, -256.0)
-    times(c("I16"), ID, 16.0)
-    border("Y0", 0, 2.0 - GHOST)
+    times(c("B2"), B1, 2048.0)
+    act(block("BN", 0), ind(c("Y0", 0, NV), BD), F.Relu, 2.0 - GHOST, 1.0)
+    exchange("BN", "LG", 0, "gh")
     need("q", ("first", sum(ENG)))
-    dma("q", "d_pr", [c("PR", RING0, 896)], [], [(T.PR[:, RING0:896], T.pr[:, RING0:896])])
     dma("q", "d_co", [c("CO", 0, RINGN)], [], [(T.CO[:, 0:RINGN], T.co[:, RING0:896])])
     dma("q", "d_mo", [c("MO", 0, RINGN)], [], [(T.MO[i:128:16, 0:RINGN], T.mo[:, RING0:896]) for i in range(16)])
     dma("q", "d_pa", [c("PR", 0, RING0)], [], [(T.PR[:, 0:RING0], T.pr[:, 0:RING0])])
-    sel(c("P1"), c("ONE", 0, 128), [[16, 8], [-1, 16]], A.is_equal, -112, 1)
-    sel(c("P2", 16, 128), c("ONE", 16, 128), [[16, 7], [-1, 16]], A.is_equal, -112, 1)
-    sel(c("P2", 0, 16), c("ONE", 0, 16), [[-1, 16]], A.is_equal, 0, 1)
-    sel(c("B0"), c("ONE", 0, 128), [[-16, 8], [0, 16]], A.is_ge, 0, 1)
-    sel(B1, c("B0"), [[16, 8], [0, 16]], A.is_ge, 15, -1)
-    sel(c("ZS"), c("ONE", 0, 160), [[-16, 10], [999, 16]], A.is_equal, 16, 1)
-    iota(c("D1"), [[0, 6 * SEG]], -1)
-    sel(c("NB"), c("D1", 0, 128), [[-1, 128]], A.is_gt, 0, 1)
-    iota(c("SI"), [[16, 6], [0, SEG]], 0)
-    sel(NU, c("NB"), [[16, 8], [0, 16]], A.is_ge, 15, -1)
-    act(c("YA", 0, 896), c("Y0", 0, 896), F.Identity, 2.0, 1.0021)
-    times(c("MB", 0, DUMP), c("M0", 0, DUMP), 0.0)
 
     for t in range(RO):
         M, MV, MW = "M%d" % (t % 2), "MV%d" % (t % 2), "MV%d" % ((t + 1) % 2)
         Y, YN = ("YA", "YB")[t % 2], ("YB", "YA")[t % 2]
         last, later = t == RO - 1, min(t, 1)
         ns = 128 if t == 0 else 256
-        nv = PIECE if t else ns - T0_S
+        sn = S_SLOTS[later]
+        vn = ns - sn
         kc = ns // 16
-        off = 0.0 if SEARCH else float(OFF * later)
+        s0 = (9 * t) % 40
+        ring = [(s0, 40)] + ([(0, s0)] if s0 else [])
+        fills = FILL[later]
+        turns = TURNS[later]
+        defer = DEFER[later]
+        odd_s = ODD_S and t > 0
+        cut = max([0] + [EARLY[x][1] for v in fills.values() for x in v if x in EARLY]) if turns else 0
+        at = [ns - sum(x for v in fills.values() for x in v if isinstance(x, int))]
+        s_end = at[0]
+
+        def naming(e, a, b):
+            while a < b:
+                x = min(b, (a // kc + 1) * kc)
+                if e == "s":
+                    k = a // kc
+                    act(ind(c("MB" if k % 2 and k < 2 * turns else M), c("L", a, x)), c("SIL", 0, 16 * (x - a)), F.Silu)
+                    if turns and k == 2 * turns and not YT_G[later]:
+                        times(c("YT", cut), c("MB", cut, DUMP), 1.0)
+                else:
+                    cp(ind(c(MV), c("L", a, x)), c("TAG", 0, 16 * (x - a)))
+                a = x
+
+        def spread(a, b, low, high):
+            o = c("PL", 256 + a, 256 + b)
+            mm(([(o, c("I32"), c("FL", a, b), True, False)] if defer else
+                [(o, ID, c("ONE", 0, b - a), i == 0, False) for i in range(2 - later)])
+               + [(o, NI, low, False, False), (o, ID, high, False, True)])
+
+        def spreads():
+            spread(0, sn, c("MNS", 15, 16 * sn, 16), c("MXS", 15, 16 * sn, 16))
+            spread(sn, ns, c("MN", 0, 8 * vn, 8), c("MX", 7, 8 * vn, 8))
+
+        def greatest(x):
+            if x == "x":
+                scan(c("MX", 0, 8 * vn), c("G", 0, 16 * vn, 2), c("G", 1, 16 * vn, 2), A.max, A.max, -4000.0)
+            else:
+                a, b = (0, 16 * sn) if x == "X" else (16 * (sn * int(x[1]) // PARTS), 16 * (sn * (int(x[1]) + 1) // PARTS))
+                scan(c("MXS", a, b), c("K3", a, b), c("GS", a, b), A.min, A.max)
+
+        def wait(j):
+            if t and j == "B" and PY_EARLY:
+                mm([(c("PY", 512), ID, c(Y, 512, NV), True, False)])
+            for x in fills.get(j, []):
+                if x == "G":
+                    ghosts0()
+                elif str(x)[0] in "xX":
+                    greatest(x)
+                elif x in EARLY:
+                    if turns:
+                        a, b = EARLY[x]
+                        tt(c("YT", a, b), c("PY", a, b), c("MB", a, b), A.max)
+                else:
+                    naming("v", at[0], at[0] + x)
+                    at[0] += x
+
+        def ring_search():
+            x = 0
+            for a, b in ring:
+                ts(c("WR", x, x + b - a), c("PD", 16 + a, 16 + b), 32.0 * later - 8.0, A.is_ge)
+                x += b - a
+            wait("W")
+            search("WR", "ER", NR, "ZR", K2, CL, False, wait, 40 - s0)
+
         if t == 0:
             ts(c("C0"), c("Y0", 896, NV), 0.0, A.is_ge, 2000.0, A.mult)
-            ts(c(Y, 896, NV), c("Y0", 896, NV), 2.0, A.add)
+            ts(c("YA", 896, NV), c("Y0", 896, NV), 2.0, A.add)
             tt(c("C1"), c("C0"), c("DS"), A.min)
-            fill(c("R0", 0, 16 * ramp, 16), STEP / 2.0)
+            cp(c("ZB", 16, 144, 16), c("B1", 0, 128, 16))
             tt(c("C", 0, 128), c("C1"), c("PR", 896, NV), A.max)
-            fill(c(Y, DUMP), 1.0)
-        elif not SEARCH:
-            W = c("W", 0, 64)
-            wanted(W)
-            scan(c("E", 0, 64), W, W, A.add, A.max)
-            tt(c("WT"), W, c("TT"), A.mult)
-            o = c("PK", 0, 64)
-            mm([(o, ID, c("TT"), True, False), (o, NU, W, False, False), (o, B1, c("E", 0, 64), False, False),
-                (o, NI, c("WT"), False, True)])
-            if t == 1:
-                times(c(M, 0, DUMP), c(YN, 0, DUMP), 0.0)
-            ts(c("RK"), o, -1.0, A.add)
-            act(ind(c("WS"), c("RK", 32, 64)), c("PRF", 512, NV), F.Silu)
-            cp(ind(c("WV"), c("RK", 0, 32)), c("PRF", 0, 512))
-            turn([("LG", NG * t)], "PG")
-            act(c(Y, NV, DUMP), c("PG", 0, NG), F.Identity, GHOST, 1.0)
-            if t == 1:
-                times(c("MB", 0, DUMP), c(YN, 0, DUMP), 0.0)
-            halves = ((nv, ns), (0, nv)) if SPLIT_C else ((0, ns),)
-            for a, b in halves:
-                tt(c("C", a, b), c("WV", a, b), c("WS", a, b), A.min)
-            for a, b in halves:
-                ts(c("LS", a, b), c("C", a, b), -off, A.add)
+            fill(c("CJ"), float(Z0_))
+            Y = "Y0"
         else:
-            rest_of_payload = payload(0, 64, 0)
-            pl, nodes = c("PK", 0, 2 * NC), c("PS", 0, 256)
-            mm([(pl, ID, c("NE"), True, False), (pl, ID, c("CJ"), False, False)])
-            wanted(c("W", 0, 64))
-            scan(c("E", 1), c("W"), c("W"), A.add, A.max)
-            rest_of_payload()
-            mm([(c("PK", 0, 2 * NC, 2), c("B2"), c("W"), False, False), (c("PK", 1, 2 * NC, 2), B1, c("E", 0, NC), False, True)], True)
-            if t == 1:
-                times(c(M, 0, DUMP), c(YN, 0, DUMP), 0.0)
+            search_tables(NC, [(0, 64), (76, 92)])
             tt(ind(c("PH"), CL), c("FF"), c("FF"), A.add)
-            scan(c("PP"), c("H0"), pl, A.max, A.min)
-            cp(c("ZL", 0, 5), c("PP", 31, 2 * NC, 32))
-            cp(ind(c("Z"), c("ZL", 0, 5)), c("PAY"))
-            scan(c("X"), c("Z", Z0_, Z0_ + 256), c("DL"), A.max, A.add)
-            mm([(nodes, B1, c("X"), True, True)])
+            wanted(c("W", 0, 64))
+            rest = c("R0", 16 * ramp0, 16 * RAMP)
+            search("W", "E", NC, "Z", 256, NL, True, lambda j: t == 1 and j == "C" and ramp0 < RAMP and scan(
+                c("RA", 16 * ramp0, 16 * RAMP), rest, rest, A.add, A.add, ramp_low + STEP * ramp0))
             turn([("LG", NG * t)], "PG")
             act(c(Y, NV, DUMP), c("PG", 0, NG), F.Identity, GHOST, 1.0)
-            scan(c("NP"), c("MK"), nodes, A.max, A.min)
-            ts(c("NL"), c("NP", 15, 256, 16), -16384.0, A.add)
-            ts(c("C"), ind(c("PR"), c("NL")), 0.0, A.add)
-            ts(c("LS"), c("C"), 0.0, A.add)
+            if t == 1:
+                ts(c("R2", 0, RAMP), c("RA", 0, 16 * RAMP, 16), 2.0, A.add)
+            if LS_MODE == 0:
+                cp(c("LS", 0, sn), ind(c("PR"), c("NL", 0, sn // 16)))
+                cp(c("LS", sn, ns), ind(c("PR"), c("NL", sn // 16, 16)))
+                ts(c("C", 0, sn), c("LS", 0, sn), 0.0, A.add)
+                ts(c("C", sn, ns), c("LS", sn, ns), 0.0, A.add)
+            elif LS_MODE == 1:
+                cp(c("LS"), ind(c("PR"), NL))
+                ts(c("C"), ind(c("PR"), NL), 0.0, A.add)
+                tt(c("G", 0, 16 * V_ZERO), ind(c(Y), c("LS", sn, sn + V_ZERO)), c("RA", 0, 16 * V_ZERO), A.add)
+            else:
+                cp(c("LS", 0, sn), ind(c("PR"), c("NL", 0, sn // 16)))
+                ts(c("C"), ind(c("PR"), NL), 0.0, A.add)
+                cp(c("LS", sn, ns), ind(c("PR"), c("NL", sn // 16, 16)))
         op("v", [c("CT", 0, ns)], [c("C", 0, ns)], lambda: V.transpose(T.CT[:, 0:ns], T.C[:, 0:ns]))
         items = []
         for b in range(ns // 32):
@@ -394,277 +465,342 @@ def rank_program(g, core, T, topo):
                                   c("CT", 32 * b + 16 * gg, 32 * b + 16 * gg + 16), gg == 0, gg == 1))
         mm(items)
 
-        def gather(a, b):
+        def gather_s():
+            if sn:
+                act(c("GS", 0, 16 * sn), ind(c(Y), c("LS", 0, sn)), F.Identity, 0.0, 1.0)
+
+        def gather_v(a, b):
             if a < b:
-                tt(c("G", 16 * a, 16 * b), ind(c(Y), c("LS", a, b)), c("RA", 16 * a, 16 * b), A.add)
+                tt(c("G", 16 * a, 16 * b), ind(c(Y), c("LS", sn + a, sn + b)), c("RA", 16 * a, 16 * b), A.add)
 
-        names = V_NAME if t else V_NAME0
-        at = [ns - sum(names.values())]
-        s_end = at[0]
-        turns = TURNS[later]
-        cut = max([0] + [b for a, b in EARLY.values()])
-        marks = [MV] if names else []
-
-        def naming(e, a, b):
-            while a < b:
-                x = min(b, (a // kc + 1) * kc)
-                if e == "s":
-                    k = a // kc
-                    act(ind(c("MB" if k % 2 and k < 2 * turns else M), c("L", a, x)), c("SIL", 0, 16 * (x - a)), F.Silu)
-                    if k == 2 * turns:
-                        times(c("YT", cut), c("MB", cut, DUMP), TAG)
-                else:
-                    cp(ind(c(MV), c("L", a, x)), c("TAG", 0, 16 * (x - a)))
-                a = x
-
-        def naming_v(j):
-            naming("v", at[0], at[0] + names.get(j, 0))
-            at[0] += names.get(j, 0)
-            if j in EARLY:
-                a, b = EARLY[j]
-                tt(c("YT", a, b), c("PY", a, b), c("MB", a, b), A.max)
-
-
-        if t == 0:
-            ts(c("LS", 0, ns), c("C", 0, ns), 0.0, A.add)
-            ts(c("L", 0, ns), c("PL", 0, ns), 0.0, A.add)
-            naming("s", 0, T0_AT * kc)
-            scan(c("RA", 0, 16 * ramp), c("R0", 0, 16 * ramp), c("R0", 0, 16 * ramp), A.add, A.add, -float(STEP * (ramp // 2 + 1)))
-            if marks:
-                fill(c(MV, 0, DUMP), 0.0)
-            if T0_S:
-                fill(c("K2", 0, 16 * T0_S), 0.0)
-                fill(c("K3", 0, 16 * T0_S), 32.0)
-                fill(c("K2", 0, 16 * T0_S, 16), 32.0)
-                fill(c("K3", 0, 16 * T0_S, 16), 0.0)
-            naming_v("g")
-            turn([("LG", 0)], "PG")
-            ts(c(Y, NV, DUMP), c("PG", 0, NG), GHOST, A.add)
-            if T0_S:
-                act(c("GS", 16 * nv, 16 * ns), ind(c(Y), c("LS", nv, ns)), F.Identity, 0.0, 1.0)
-            naming("s", T0_AT * kc, s_end)
-            gather(0, nv)
-            sel(c("D0"), c("D1"), [[0, 6], [1, SEG]], A.not_equal, -(SEG - 1), 0, 66.0)
-            ring_table(0)
-            sel(c("WR"), c("ONE", 0, 48), [[1, 48]], A.is_gt, 0, 0)
-            iota(c("SF"), [[1, K2]], 0)
-            sel(c("ZA"), c("ONE", 0, 160), [[-16, 10], [-999, 16]], A.is_ge, 16, 1)
-            sel(c("ZB"), c("ZA"), [[16, 10], [0, 16]], A.is_ge, -1, -1)
-            iota(c("PR", DUMP), [[1, 256]], DUMP)
-            iota(c("CO", TW - K2), [[0, K2]], YW_ - 1)
-            iota(c("MO", TW - K2), [[0, K2]], 0)
-        else:
-            act(c("GS", 16 * nv, 16 * ns), ind(c(Y), c("LS", nv, ns)), F.Identity, 0.0, 1.0)
-            gather(0, V_FIRST)
-            ts(c("L"), c("PL", 0, ns), -off, A.add)
-            naming("s", 0, s_end - S_LATE)
-            gather(V_FIRST, nv)
-            ring_table(t)
-            if not last:
-                clear_lists()
-            iota(c(MW, 0, DUMP), [[0, DUMP]], 0)
-            if not last:
-                iota(c("M%d" % ((t + 1) % 2), 0, DUMP), [[0, DUMP]], 0)
-            else:
-                iota(c("OF", 0, RING0), [[0, RING0]], 0)
-                iota(c("OF", 896, NV), [[0, 128]], 0)
-        naming_v(0)
-
-        def spread(a, b, low, high):
-            o = c("PS", 128 + a, 128 + b)
-            mm([(o, ID, c("ONE", 0, b - a), i == 0, False) for i in range(1 if t and SEARCH else 2)]
-               + [(o, NI, low, False, False), (o, ID, high, False, True)])
-
-        for x in SCANS if nv < ns else "nx":
-            if x == "n":
-                scan(c("MN", 8 * nv - 1, -1, -1), c("G", 16 * nv - 1, -1, -2), c("G", 16 * nv - 2, -1, -2), A.min, A.min, 4000.0)
-                mm([(c("PN", 256, 256 + nv), ID, c("MN", 0, 8 * nv, 8), True, False),
-                    (c("PN", 256, 256 + nv), NI, c("RA", 0, 16 * nv, 16), False, True)])
-            elif x == "x":
-                scan(c("MX", 0, 8 * nv), c("G", 0, 16 * nv, 2), c("G", 1, 16 * nv, 2), A.max, A.max, -4000.0)
-                spread(0, nv, c("MN", 0, 8 * nv, 8), c("MX", 7, 8 * nv, 8))
-            elif x == "N":
-                scan(c("MNS", 16 * nv, 16 * ns), c("K2", 0, 16 * (ns - nv)), c("GS", 16 * nv, 16 * ns), A.max, A.min)
-                mm([(c("PN", 256 + nv, 256 + ns), ID, c("MNS", 16 * nv + 15, 16 * ns, 16), True, True)])
-            else:
-                scan(c("MXS", 16 * nv, 16 * ns), c("K3", 0, 16 * (ns - nv)), c("GS", 16 * nv, 16 * ns), A.min, A.max)
-                spread(nv, ns, c("MNS", 16 * nv + 15, 16 * ns, 16), c("MXS", 16 * nv + 15, 16 * ns, 16))
+        fl_at = None if defer else FL_AT[later]
         if t == 0:
             mm([(c("PG", 384, 385), B1, c("ONE", 0, 1), True, False), (c("PG", 384, 385), NU, c("ONE", 0, 1), False, True)])
-        ts(c("FL", 0, ns), c("PN", 256, 256 + ns), 2.0, A.is_ge)
-        naming_v(1)
-        tt(c("RES", 0, ns), c("PS", 128, 128 + ns), c("FL", 0, ns), A.mult)
-        naming_v(2)
-        if t == 0:
-            tt(c(Y, 896, NV), c("RES", 0, 128), c(Y, 896, NV), A.max)
-        elif SEARCH:
-            tt(ind(c(Y), c("NL")), c("RES", 0, 256), c("ONE", 0, 256), A.add)
-        else:
-            tt(c(Y, 0, NV), ind(c("RES"), c("RK")), c(Y, 0, NV), A.max)
-
-        diagonal(Y, True, True)
-        mm([(c("PY", 0, 512), ID, c(Y, 0, 512), True, cut > 0)])
-        if t == 0:
+            iota(c("CJ", 0, None, 2), [[1, NC]], 1)
+            sel(c("P1"), c("ONE", 0, 128), [[16, 8], [-1, 16]], A.is_equal, -112, 1)
+            sel(c("P2", 16, 128), c("ONE", 16, 128), [[16, 7], [-1, 16]], A.is_equal, -112, 1)
+            sel(c("P2", 0, 16), c("ONE", 0, 16), [[-1, 16]], A.is_equal, 0, 1)
+            ts(c("LS", 0, ns), c("C", 0, ns), 0.0, A.add)
+            fill(c("H0"), 0.0)
+            fill(c("WR", 40), 1.0)
+            fill(c(Y, DUMP, DUMP + ns), -1.0)
+            ts(c("L", 0, ns), c("PL", 0, ns), 0.0, A.add)
             ts(c("CC"), c("PG", 384, 385), -1.0, A.add)
-            cp(c(YN, NV), c(Y, NV))
-            ts(c("SG"), c("SI"), c("CC"), A.add)
-            mm([(c("PL", 256 + 40, 256 + 60), ID, c("ONE", 0, 20), True, True)])
-        elif last:
-            ts(c("OY", 0, RING0), c(Y, 0, RING0), -2.0, A.add, -1.0, A.max)
-            ts(c("OY", 896, NV), c(Y, 896, NV), -2.0, A.add, -1.0, A.max)
-            dma("q", "o_a", [], [c("OY", 0, RING0), c("OY", 896, NV), c("OF", 0, RING0), c("OF", 896, NV)],
-                [(T.yy[:, 0:RING0], T.OY[:, 0:RING0]), (T.yy[:, 896:NV], T.OY[:, 896:NV]),
-                 (T.yf[:, 0:RING0], T.OF[:, 0:RING0]), (T.yf[:, 896:NV], T.OF[:, 896:NV])])
-        naming_v(3)
-        s0 = (9 * t) % 40
-        parts = [(s0, 40, 1)] + ([(0, s0, 41 - s0)] if s0 else [])
-        for a, b, x in parts:
-            ts(c("WR", x, x + b - a), c("PD", 16 + a, 16 + b), 2.0, A.is_ge)
-        naming_v(4)
-        scan(c("ER", 0, SEG), c("WR", 0, SEG), c("WR", 0, SEG), A.add, A.max)
-        mm([(c("PK", 64 + SEG * j, 64 + SEG * (j + 1)), B1, c("ER", 0, SEG), True, True) for j in range(6)])
-        items = []
-        for a, b, x in parts + [(60, 66, 41)]:
-            items += [(c("PL", 256 + a, 256 + b), B1, c("ER", x, x + b - a), True, False),
-                      (c("PL", 256 + a, 256 + b), NU, c("WR", x, x + b - a), False, True)]
-        mm(items)
-        mm([(c("PY", 512), ID, c(Y, 512, NV), True, False)])
-        if t == 0:
-            ts(c("BF"), B1, -32.0, A.mult)
-            fill(c("CX"), -0.9375)
-            fill(c(MW, 0, DUMP), 0.0)
-        naming_v(5)
-        tt(c("GT"), c("PK", 64, 64 + 6 * SEG), c("SG"), A.is_gt)
-        cp(c("RT", 0, 66), c("PL", 256, 256 + 66))
-        naming_v(10)
-        scan(c("BS"), c("GT"), c("D"), A.mult, A.add)
-        naming_v(6)
-        ends = c("BS", SEG - 1, None, SEG)
-        ts(c("BL"), ends, 0.0, A.add)
-        naming_v(7)
-        tt(c("X1"), ind(c("RT", 0, 66), c("BL")), c("SF"), A.is_le)
-        o = c("PG", 384, 390)
-        mm([(o, c("I16"), ends, True, False)]
-           + [(o, c("ZB", 16 - i, 144 - i), c("X1", i, None, 16), False, i == 15) for i in range(16)])
-        if t == 0 and SEARCH:
-            fill(c("DL"), DELTA)
-            ts(c("B2"), B1, 2048.0, A.mult)
-            fill(c("W", 64), 1.0)
-            fill(c("E", 0, 1), 0.0)
-        elif t == 0:
-            ts(c("PRF"), c("PR", 0, NV), OFF + 0.125, A.add)
-        if 0 < cut < 512:
-            mm([(c("PY", 512), ID, c("YT", 512, NV), False, not marks), (c("PY", 0, 512), ID, c("YT", 0, 512), True, False),
-                (c("PY", cut, 512), ID, c(Y, cut, 512), False, not marks)])
+            diagonal(Y, True, True)
+            between = [lambda: act(c("AB"), block("BN", 0), F.Relu, TAG, -0.012), lambda: times(NI, ID, -1.0), lambda: times(c("IT"), ID, TAG),
+                       lambda: times(c("BF"), B1, -32.0), lambda: times(c("DL", 0, K2), c("ONE", 0, K2), DELTA),
+                       lambda: times(c("CX"), c("ONE", 0, 1), -0.9375), lambda: times(c("ER", 0, 1), c("ONE", 0, 1), 0.0),
+                       lambda: times(c("ZR", Z0_, Z0_ + K2), c("ONE", 0, K2), 0.0)]
+
+            def names0(a, b):
+                for k in range(a, b, kc):
+                    naming("s", k, min(k + kc, b))
+                    if between:
+                        between.pop()()
+
+            def ghosts0():
+                turn([("LG", 0)], "PG")
+                ts(c(Y, NV, DUMP), c("PG", 0, NG), GHOST - 2.0, A.add)
+                if T0_AT * kc < s_end:
+                    gather_s()
+                    names0(T0_AT * kc, s_end)
+                times(c("YT", YT_G[0]), c(M, YT_G[0], DUMP), 1.0)
+                if YT_G[0]:
+                    narrow(c("YT", 0, YT_G[0]), c(M, 0, YT_G[0]))
+                if T0_AT * kc >= s_end:
+                    gather_s()
+                gather_v(0, vn)
+
+            names0(0, min(T0_AT * kc, s_end))
+            setup = [lambda: ts(c("NE"), c("XI"), c("CC"), A.not_equal, BIG, A.mult),
+                     lambda: ts(c("H0", 0, None, 2), c("XI", 0, None, 2), c("CC"), A.is_equal, BIG, A.mult),
+                     lambda: ts(c("SG"), c("SF", 0, K2, 16), c("CC"), A.add),
+                     lambda: fill(c("R0", 0, 16 * ramp0, 16), STEP / 2.0),
+                     lambda: scan(c("RA", 0, 16 * ramp0), c("R0", 0, 16 * ramp0), c("R0", 0, 16 * ramp0), A.add, A.add, ramp_low)]
+            for j, f in enumerate(setup):
+                f()
+                wait("L%d" % j)
+            search_tables(NR, [(s0, s0 + 40), (100, 108)])
+            if sn:
+                iota(c("K2", 0, 16 * sn), [[0, sn], [-40, 16]], 32)
+            iota(c("PR", DUMP, DUMP + K2), [[1, K2]], DUMP)
+            if sn:
+                iota(c("K3", 0, 16 * sn), [[0, sn], [40, 16]], -8)
+            iota(c("CO", TW - K2), [[0, K2]], YW_ - 1)
+            iota(c("MO", TW - K2), [[0, K2]], 0)
+            ring_search()
+            wait("Z")
+            turn([("YT", NV), (MV, NV)], "PN")
+            for a, b in ((512, 896), (0, 512)):
+                mm([(c("PY", a, b), c("IT") if n == "YT" else ID, c(n, a, b), n == Y, n == "YT") for n in (Y, MV, "YT")])
+            act(block("NM", t), c("PN", 0, NG), F.Sign, 0.0, 1.0)
+            exchange("NM", "LN", t, "nt", "nn")
+            act(c(YN, 0, 896), c("PY", 0, 896), F.Identity, 2.0, 1.0021)
+            act(c(YN, NV, DUMP), c(Y, NV, DUMP), F.Identity, 2.0, 1.0)
+            times(c("I32"), ID, 32.0)
+            iota(c(YN, DUMP), [[0, 256]], 1)
+            cp(c("PRL"), ind(c("PR", RING0), CL))
         else:
-            mm([(c("PY", a, a + 512), ID, c("YT", a, a + 512), a < cut, not marks) for a in (512, 0)])
-        naming_v(8)
-        cp(CL, o)
-        act(c("NN"), c(M, NV, DUMP), F.Identity, 0.0, 1.0)
-        if TURN_FIRST:
-            turn([(x, NV) for x in ["YT"] + marks] + [("NN", 0)], "PN")
-        if marks:
-            mm([(c("PY", a, a + 512), ID, c(MV, a, a + 512), False, True) for a in (512, 0)], True)
-        if not TURN_FIRST:
-            turn([(x, NV) for x in ["YT"] + marks] + [("NN", 0)], "PN")
-        cp(c("PRL"), ind(c("PR", RING0), CL))
-        cp(c("OI"), ind(c(Y, RING0), CL))
-        cp(c("COL"), ind(c("CO"), CL))
-        ts(c("OD"), c("OI"), 1, A.bitwise_and)
+            gather_s()
+            gather_v(V_ZERO if LS_MODE == 1 else 0, min(vn, V_FIRST))
+            ts(c("L"), c("PL", 0, ns), 0.0, A.add)
+            naming("s", 0, s_end if fl_at is None else fl_at * kc)
+            gather_v(V_FIRST, vn)
+            search_tables(NR, [(s0, s0 + 40), (100, 108)])
+            clear(c("ZR", Z0_, Z0_ + K2))
+            if not last:
+                clear(c("Z", Z0_, Z0_ + 256))
+            clear(c(MW, 0, DUMP))
+            if YT_G[later] and turns and t == 1:
+                narrow(c("YT", NV), c("MB", NV, DUMP))
+                narrow(c("YT", 0, NV), c("MB", 0, NV))
+            if not last:
+                clear(c("M%d" % ((t + 1) % 2), 0, DUMP))
+            else:
+                clear(c("OF", 0, RING0))
+                clear(c("OF", 896, NV))
+                dma("q", "o_b", [], [c("OF", 0, RING0), c("OF", 896, NV)],
+                    [(T.yf[:, 0:RING0], T.OF[:, 0:RING0]), (T.yf[:, 896:NV], T.OF[:, 896:NV])])
+            if YT_G[later] and turns and t > 1:
+                narrow(c("YT", NV), c("MB", NV, DUMP))
+                narrow(c("YT", 0, NV), c("MB", 0, NV))
+            wait("g")
+
+        least = c("PG", 256, 256 + ns)
+        if defer:
+            for x in MINS[later]:
+                if x == "N":
+                    scan(c("MNS", 0, 16 * sn), c("K2", 0, 16 * sn), c("GS", 0, 16 * sn), A.max, A.min)
+                elif x == "n":
+                    scan(c("MN", 8 * vn - 1, -1, -1), c("G", 16 * vn - 1, -1, -2), c("G", 16 * vn - 2, -1, -2), A.min, A.min, 4000.0)
+                elif x == "F":
+                    ts(c("FL", 0, sn), c("MNS", 15, 16 * sn, 16), 2.0 * later, A.is_ge)
+                elif x == "f":
+                    tt(c("FL", sn, ns), c("MN", 0, 8 * vn, 8), c("R2", 0, vn) if t else c("RA", 0, 16 * vn, 16), A.is_ge)
+                elif x == "c":
+                    cp(c("COL"), ind(c("CO"), CL))
+                elif x == "o":
+                    cp(c("OI"), ind(c(Y, RING0), CL))
+                elif x == "d":
+                    ts(c("OD"), c("OI"), 1, A.bitwise_and)
+                else:
+                    wait(x)
+            wait("s")
+            if t:
+                tt(ind(c(Y), NL), c("FL"), c("ONE"), A.add)
+            else:
+                tt(c(YN, 896, NV), c("FL", 0, ns), c("YA", 896, NV), A.add)
+                Y = YN
+        for x in "" if defer else SCANS[later] if sn else "nx":
+            if x == "n":
+                scan(c("MN", 8 * vn - 1, -1, -1), c("G", 16 * vn - 1, -1, -2), c("G", 16 * vn - 2, -1, -2), A.min, A.min, 4000.0)
+                mm([(c("PG", 256 + sn, 256 + ns), ID, c("MN", 0, 8 * vn, 8), True, False),
+                    (c("PG", 256 + sn, 256 + ns), NI, c("RA", 0, 16 * vn, 16), False, True)])
+            elif x == "N":
+                scan(c("MNS", 0, 16 * sn), c("K2", 0, 16 * sn), c("GS", 0, 16 * sn), A.max, A.min)
+                mm([(c("PG", 256, 256 + sn), ID, c("MNS", 15, 16 * sn, 16), True, True)])
+            elif x == "x":
+                scan(c("MX", 0, 8 * vn), c("G", 0, 16 * vn, 2), c("G", 1, 16 * vn, 2), A.max, A.max, -4000.0)
+                spread(sn, ns, c("MN", 0, 8 * vn, 8), c("MX", 7, 8 * vn, 8))
+            else:
+                scan(c("MXS", 0, 16 * sn), c("K3", 0, 16 * sn), c("GS", 0, 16 * sn), A.min, A.max)
+                spread(0, sn, c("MNS", 15, 16 * sn, 16), c("MXS", 15, 16 * sn, 16))
+            if fl_at is not None and x == [y for y in SCANS[later] if y in "nN"][-1]:
+                act(c("FL", 0, ns), least, F.Relu, -96.0, 64.0)
+                naming("s", fl_at * kc, s_end)
+            wait(x)
+        if fl_at is None and not defer:
+            ts(c("FL", 0, ns), least, 2.0 * later, A.is_ge, 32.0, A.mult)
+        if t == 0 and not defer:
+            cp(c("COL"), ind(c("CO"), CL))
+        if not defer:
+            wait("r")
+            tt(c("RES", 0, ns), c("PL", 256, 256 + ns), c("FL", 0, ns), A.min)
+        if defer:
+            pass
+        elif t == 0:
+            cp(c("OI"), ind(c(Y, RING0), CL))
+            tt(c(YN, 896, NV), c("RES", 0, ns), c("YA", 896, NV), A.max)
+            ts(c("OD"), c("OI"), 1, A.bitwise_and)
+            Y = YN
+        else:
+            wait("s")
+            tt(ind(c(Y), NL), c("RES"), c("ONE"), A.add)
 
         def dirty(a, b):
             if a < b:
                 act(c("DG", 16 * a, 16 * b), ind(c(Y), c("PRL", a, b)), F.Relu, 4.0, -2.0)
 
-        dv, d1, d2 = D_V[later]
-        hv = H_V[later]
-        act(c("SN"), c("PD", 0, 64), F.Sign, -1.5, 1.0, c("CN"))
-        dirty(dv, d2)
-        act(block("NM", t), c("PN", 0, NG), F.Sign, 0.0, 1.0)
-        exchange("NM", "LN", t, "nt", "nn" if NEAR else None)
-        if t == 0:
-            if SEARCH:
-                iota(c("XI"), [[0, 16], [1, 16]], 0)
-                iota(c("XJ"), [[0, 5], [1, 16], [100, 2]], 0)
-                iota(c("CI"), [[16, 5], [1, 16], [0, 2]], 1)
-                sel(c("CJ"), c("CI"), [[0, NC], [1, 2]], A.is_equal, 0, 0, float(Z0_))
+        dv, d2, run = D_V[later]
+        diagonal(Y, True, True)
+        if t:
+            mm([(c("PY", 0, 512), ID, c(Y, 0, 512), True, cut > 0)])
+            wait("A")
+            ring_search()
+            if not PY_EARLY:
+                mm([(c("PY", 512), ID, c(Y, 512, NV), True, False)])
+            act(c("NN"), c(M, NV, DUMP), F.Identity, 0.0, 1.0)
+            wait("C2")
+            if defer and RES_ON == "e":
+                spreads()
+            cp(c("PRL"), ind(c("PR", RING0), CL))
+            wait("D0")
+            act(c("SN"), c("PD", 0, 64), F.Sign, -24.0, 1.0, c("CN"))
+            if defer and RES_ON == "e":
+                act(c("RES"), c("PL", 256, 512), F.Relu, -31.0, 1.0)
+            if odd_s:
+                act(c("O1"), ind(c(Y, RING0), CL), F.Identity, 0.0, 1.0)
+                act(c("OM"), ind(c("MF"), CL), F.Identity, 0.0, 1.0)
+                act(c("O2"), c("O1"), F.Identity, 127.75, 0.5)
+                cp(c("COL"), ind(c("CO"), CL))
             else:
-                iota(c("TF"), [[-16, 64]], FAR)
+                cp(c("OI"), ind(c(Y, RING0), CL))
+                cp(c("COL"), ind(c("CO"), CL))
+                ts(c("OD"), c("OI"), 1, A.bitwise_and)
+        if not (defer and t):
+            act(c("OC"), ind(c(Y, RING0), CL), F.Identity, 0.0, 1.0)
+        dirty(dv, d2)
+        wait("D")
+        if t == 0:
+            act(c("SN"), c("PD", 0, 64), F.Sign, -24.0, 1.0, c("CN"))
+        elif cut:
+            mm([(c("PY", 512), ID, c("YT", 512, NV), False, False), (c("PY", 0, 512), ID, c("YT", 0, 512), True, False),
+                (c("PY", cut, 512), ID, c(Y, cut, 512), False, False)])
+        elif turns:
+            mm([(c("PY", a, a + 512), c("IT"), c("YT", a, a + 512), False, False) for a in (512, 0)])
+        if t:
+            if TURN_FIRST:
+                turn([(x, NV) for x in ["YT"] * min(turns, 1) + [MV]] + [("NN", 0)], "PN")
+            mm([(c("PY", a, a + 512), ID, c(MV, a, a + 512), False, True) for a in (512, 0)], True)
+            if not TURN_FIRST:
+                turn([(x, NV) for x in ["YT"] * min(turns, 1) + [MV]] + [("NN", 0)], "PN")
+            act(block("NM", t), c("PN", 0, NG), F.Sign, 0.0, 1.0)
+            exchange("NM", "LN", t, "nt", "nn")
+        if t == 0:
+            clear(c(MW, 0, DUMP))
             iota(c("CF", 0, None, 2), [[0, K2]], 8192)
-            iota(c("PH", 0, RINGN), [[0, RINGN]], 0)
-            clear_lists()
+            iota(c("PR", DUMP + K2), [[1, 256 - K2]], DUMP + K2)
+            clear(c("Z", Z0_, Z0_ + 256))
+            clear(c("PH", 0, RINGN))
+            clear(c("M1", 0, DUMP))
         elif not last:
-            iota(c("MB", 0, DUMP), [[0, DUMP]], 0)
-        left = c("PK", 480, 481)
+            clear(c("MB", 0, DUMP))
+        if defer and t and RES_ON != "e":
+            spreads()
+        left = c("PS", 480, 481)
         mm([(left, c("BF"), c("CX"), True, False), (left, c("BF"), c("CN"), False, True)])
-        if dv:
-            ts(c("DG", 0, 16 * dv), ind(c(Y), c("PRL", 0, dv)), 2.0, A.is_lt)
-        dirty(d2, K2)
-        tt(c(YN, 0, NV), c("PY"), c(M, 0, NV), A.max)
-        tt(c("OM"), ind(c("MO"), CL), c("OD"), A.mult)
+        def dirty_sums(a, b):
+            o = c("PS", a, b)
+            more = [(o, c(l), c(n, a, b), n == "O1", False) for l, n in (("I64", "O1"), ("I64", "OM"), ("IN", "O2"))] if odd_s else []
+            mm(more + sums(o, "DG", a, b, ID, not odd_s))
+
+        late = D_LATE if t else 0
+        if late < dv:
+            ts(c("DG", 16 * late, 16 * dv), ind(c(Y), c("PRL", late, dv)), 2.0, A.is_lt)
+        dirty(d2, run)
+        if not late:
+            dirty_sums(0, run)
+        dirty(max(d2, run), K2)
+        if defer and t and RES_ON == "s":
+            act(c("RES"), c("PL", 256, 512), F.Relu, -31.0, 1.0)
+        wait("E")
+        if t:
+            tt(c(YN, 0, NV), c("PY"), c(M, 0, NV), A.max)
+        if late:
+            ts(c("DG", 0, 16 * late), ind(c(Y), c("PRL", 0, late)), 2.0, A.is_lt)
+            dirty_sums(0, run)
+        if not odd_s:
+            tt(c("OM"), ind(c("MO"), CL), c("OD"), A.mult)
+        if defer and RES_ON == "v":
+            ts(c("RES"), c("PL", 256, 512), -31.0, A.add, 0.0, A.max)
         if last:
             mm([(c("PY", a, b), l, c(n, x + a, x + b), n == "PH", n != "PH")
                 for a, b in ((0, 512), (512, RINGN)) for l, n, x in ((ID, "PH", 0), (NI, YN, RING0))])
-        mm(sums(c("PS", 0, K2), "DG", 0, K2, ID, True))
+        dirty_sums(run, K2)
         held = c("PK", 256, 256 + 2 * K2, 2)
-        act(c("OC"), ind(c(Y, RING0), CL), F.Identity, 0.0, 1.0)
-        mm([(c("PK", 257, 256 + 2 * K2, 2), ID, c("OC"), True, True)])
-        for a, x, b in hv:
+        if not (defer and t):
+            mm([(c("PK", 257, 256 + 2 * K2, 2), ID, c("OC"), True, True)])
+        for a, x, b in H_V[later]:
             act(c("HG", 16 * x, 16 * b), ind(c(YN), c("COL", x, b)), F.Silu, 318.75, -320.0)
             ts(c("HG", 16 * a, 16 * x), ind(c(YN), c("COL", a, x)), 1.0, A.is_equal, -0.25, A.mult)
             o = c("PK", 256 + 2 * a, 256 + 2 * b, 2)
             mm([(o, ID, c("ONE", 0, b - a), True, False)] + sums(o, "HG", a, b, IH, False))
-        tt(c("FF"), c("PS", 0, K2), c("OM"), A.min)
+        if odd_s:
+            ts(c("FF"), c("PS", 0, K2), 128.0 - 16384.0, A.is_gt)
+        else:
+            tt(c("FF"), c("PS", 0, K2), c("OM"), A.min)
         mm([(c("PG", 256, 256 + K2), B1, c("FF"), True, True)])
+        if defer and t:
+            tt(ind(c(YN), NL), c("RES"), c("ONE"), A.add)
+            act(c("OC"), ind(c(YN, RING0), CL), F.Identity, 0.0, 1.0)
+        elif defer:
+            greatest("x")
+            greatest("X")
+            spreads()
+            act(c("RES", 0, ns), c("PL", 256, 256 + ns), F.Relu, -31.0, 1.0)
         if last:
             act(c("OF", RING0, 896), c("PY", 0, RINGN), F.Relu, -0.001, 1.0)
         act(c("A8"), c("PG", 256, 256 + K2), F.Abs, -8.0, 1.0)
         act(c("CD"), c("A8"), F.Silu, -1600.006, 200.0)
+        if t == 0:
+            times(c("YA", DUMP), c("ONE"), 1.0)
+            times(c("YA", NV, DUMP), c("ONE", 0, NG), GHOST)
+            times(c("DL", K2), c("ONE", K2), DELTA)
+            if ODD_S:
+                times(c("I64"), ID, 64.0)
+                times(c("IN"), ID, -128.0)
+
+        def values_out(j):
+            for x in OUT_AT.get(j, "") if last else "":
+                if x == "r":
+                    ts(c("OY", RING0, 896), c(YN, RING0, 896), -2.0, A.add, -1.0, A.max)
+                else:
+                    a, b = (0, RING0) if x == "a" else (896, NV)
+                    ts(c("Y0", a, b), c(YN, a, b), -2.0, A.add, -1.0, A.max)
+                    dma("q", "o_" + x, [], [c("Y0", a, b)], [(T.yy[:, a:b], T.Y0[:, a:b])])
+
         def notices(j):
+            values_out(j)
             if j in NOTES:
                 a, b = NOTES[j]
                 tt(ind(c(MW, 0, NV), c("BD", a // 16, b // 16)), c("LN", NG * t + a, NG * t + b), c("AB", a, b), A.mult)
                 if j == max(NOTES):
-                    diagonal(MW, j < 4, j == 4, last)
-
-        notices(0)
+                    diagonal(MW, True, False, last)
 
         if t == 0:
-            if SEARCH:
-                payload(64, NC, 76)()
+            fill(c("W", 64), 1.0)
+            fill(c("E", 0, 1), 0.0)
+            if ODD_S:
+                cp(c("MF", 0, RINGN), c("MO", 0, RINGN))
+                fill(c("MF", TW - K2), 0.0)
+        notices(0)
         ts(c("FR"), held, 2.0, A.is_lt, 32.0, A.mult)
+        if defer and t:
+            mm([(c("PK", 257, 256 + 2 * K2, 2), ID, c("OC"), True, True)])
         notices(1)
         if last:
-            ts(c("OY", RING0, 896), c(Y, RING0, 896), -2.0, A.add, -1.0, A.max)
             fill(c("OM"), -2.0)
         scan(c("CF", 1, None, 2), c("FR"), c("FR"), A.add, A.add, left)
         notices(2)
         scan(c("KO"), c("CF"), c("PK", 256, 256 + 2 * K2), A.max, A.min)
         notices(3)
+        if defer and t == 0:
+            tt(c(YN, 896, NV), c("RES", 0, ns), c("YA", 896, NV), A.add)
         if last:
+            ts(c("FR"), KO, 2.0, A.is_lt)
             for x in TAIL:
                 ring_out(x)
-            ts(c("FR"), KO, 2.0, A.is_lt)
         tt(ind(c(YN, RING0), CL), KO, c("CD"), A.add)
-        diagonal(YN, 4 in NOTES, 4 not in NOTES, last)
-        notices(4)
+        diagonal(YN, False, True, last)
 
         if not last:
-            if not SEARCH:
-                if t == 0:
-                    ts(c("TT"), c("TF"), c("CC"), A.subtract)
-                tt(ind(c("PH"), CL), c("FF"), c("FF"), A.add)
-            elif t == 0:
-                for u in (0, 1):
-                    ts(c("NE", u, None, 2), c("XI", 0, NC), c("CC"), A.not_equal, BIG, A.mult)
-                ts(c("H0"), c("XJ"), c("CC"), A.is_equal, BIG, A.mult)
-                ts(c("MK"), c("XI"), c("CC"), A.is_le, BIG, A.mult)
             border(YN, t + 1, -GHOST)
+            if t == 0 and ramp0 < RAMP:
+                times(c("R0", 16 * ramp0, 16 * RAMP), c("R0", 0, 16 * (RAMP - ramp0)), 1.0)
             if t == 0:
-                iota(c("K2", 16 * T0_S, 16 * S_SLOTS), [[0, S_SLOTS - T0_S], [-40, 16]], 32)
-                iota(c("K3", 16 * T0_S, 16 * S_SLOTS), [[0, S_SLOTS - T0_S], [40, 16]], -8)
-                if not SEARCH:
-                    iota(c("RES", 256), [[0, FAR - 256]], 0)
+                clear(c("MB", 0, DUMP))
+                iota(c("K2", 16 * sn, 16 * S_SLOTS[1]), [[0, S_SLOTS[1] - sn], [-40, 16]], 32)
+                iota(c("K3", 16 * sn, 16 * S_SLOTS[1]), [[0, S_SLOTS[1] - sn], [40, 16]], -8)
 
     for x in "yf":
         if x not in TAIL:

from concourse.bass import DstId, RemoteDMATransfer
from concourse.mybir import AluOpType as A, ActivationFunctionType as F

NV, NG, RO, K2 = 1024, 192, 5, 96
DUMP = NV + NG
YW_ = DUMP + 256
RING0, RINGN = 256, 640
TW = DUMP + K2 - RING0
NC, NR = 80, 48
Z0_ = 96
DELTA = 1.0 / 256
BIG = 29952.0
TAG = 2.0 ** -9
GHOST = 1.25
SILU_ONE = 1.278464542761074
ROUND = 65536.0 + 2.0 ** -7
STEP = 18

S_SLOTS = (32, 128)
RAMP = 128
LS_FIRST = True
V_FIRST = 76
FILL = ({"L0": [8], "L1": [8], "L2": [8], "L3": [8], "B": [8], "C": [8], "Z": ["G"]},
        {"1": [8], "s": [8], "A": [16, "X0"], "W": ["X1"], "B": [16], "B4": ["X2"], "C": [16], "C2": ["X3"], "D0": [16], "D": ["x"]})
T0_AT = 16
TURN_FIRST = True
SCANS = ("nxNX", "NnXx")
EARLY = {"e": (0, 128), "f": (128, 256)}
TURNS = (0, 4)
FL_AT = (None, 4)
PY_EARLY = True
DEFER = (True, True)
ODD_S = False
D_LATE = 0
PARTS = 4
MINS = ("nNfoFcd", "NnF1f")
RES_ON = "s"
LS_MODE, V_ZERO = 2, 16
YT_G = (512, 1)
TAIL_FIRST = True
TAIL = "y"
D_V = ((48, 64, 64), (12, 60, 60))
H_V = (((0, 28, 48), (48, 72, 96)), ((0, 28, 48), (48, 70, 96)))
OUT_AT = {1: "ac", 2: "r"}
NOTES = {1: (0, 64), 2: (64, 192)}
ENG = (4, 4, 4)


def _sb(n, d):
    return ("sbuf", [128, n], d)


SCRATCH = {
    "YA": _sb(YW_, "bfloat16"), "YB": _sb(YW_, "bfloat16"), "Y0": _sb(YW_, "bfloat16"),
    "PR": _sb(YW_, "int32"), "CO": _sb(TW, "int32"), "MO": _sb(TW, "int32"),
    "BDI": _sb(12, "int32"), "BD": _sb(12, "uint16"), "AB": _sb(NG, "bfloat16"), "NN": _sb(NG, "bfloat16"),
    "MB": _sb(YW_, "float32"), "YT": _sb(DUMP, "bfloat16"),
    "W": _sb(NC, "bfloat16"), "E": _sb(NC + 2, "bfloat16"), "WR": _sb(NR, "bfloat16"), "ER": _sb(NR + 2, "bfloat16"),
    "PAY": _sb(NC, "float32"), "PP": _sb(2 * NC, "float32"), "ZL": _sb(6, "uint16"),
    "Z": _sb(Z0_ + 16 * NC, "float32"), "ZR": _sb(Z0_ + 16 * NR, "float32"), "X": _sb(256, "float16"),
    "NL": _sb(16, "uint16"), "XI": _sb(2 * NC, "bfloat16"),
    "CJ": _sb(2 * NC, "bfloat16"), "NE": _sb(2 * NC, "bfloat16"), "H0": _sb(2 * NC, "bfloat16"),
    "DL": _sb(256, "bfloat16"), "B2": _sb(128, "bfloat16"),
    "C": _sb(256, "float16"), "CT": _sb(256, "float16"), "LS": _sb(256, "uint16"), "L": _sb(256, "uint16"),
    "C0": _sb(128, "float32"), "C1": _sb(128, "float32"), "DS": _sb(128, "float32"),
    "G": _sb(3072, "float16"), "GS": _sb(3072, "bfloat16"), "MX": _sb(1536, "float16"), "MN": _sb(1536, "float16"),
    "MXS": _sb(3072, "bfloat16"), "MNS": _sb(3072, "bfloat16"), "K2": _sb(3072, "bfloat16"), "K3": _sb(3072, "bfloat16"),
    "R0": _sb(3072, "bfloat16"), "RA": _sb(3072, "float16"), "R2": _sb(192, "float16"), "I32": _sb(128, "bfloat16"), "IT": _sb(128, "bfloat16"),
    "I64": _sb(128, "bfloat16"), "IN": _sb(128, "bfloat16"), "MF": _sb(TW, "bfloat16"), "O1": _sb(K2, "bfloat16"), "O2": _sb(K2, "bfloat16"),
    "FL": _sb(256, "bfloat16"), "RES": _sb(256, "bfloat16"), "OC": _sb(K2, "bfloat16"), "SF": _sb(112, "bfloat16"),
    "SG": _sb(6, "bfloat16"), "WI": _sb(6, "bfloat16"),
    "SIL": _sb(256, "float32"), "SN": _sb(64, "bfloat16"), "CN": _sb(1, "float32"), "CC": _sb(1, "float32"), "CX": _sb(1, "float32"),
    "CL": _sb(6, "uint16"), "COL": _sb(K2, "uint16"), "PRL": _sb(K2, "uint16"),
    "DG": _sb(1536, "bfloat16"), "HG": _sb(1536, "bfloat16"), "TAG": _sb(256, "bfloat16"),
    "OI": _sb(K2, "int32"), "OD": _sb(K2, "int32"), "OM": _sb(K2, "bfloat16"), "FF": _sb(K2, "bfloat16"),
    "A8": _sb(K2, "float32"), "CD": _sb(K2, "bfloat16"), "FR": _sb(K2, "bfloat16"), "CF": _sb(2 * K2, "bfloat16"),
    "KO": _sb(2 * K2, "bfloat16"),
    "PH": _sb(TW, "bfloat16"), "OY": _sb(RING0 + TW, "bfloat16"), "OF": _sb(RING0 + TW, "bfloat16"), "OW": _sb(64, "bfloat16"),
    "ONE": _sb(256, "bfloat16"), "Z0": _sb(160, "bfloat16"), "Z1": _sb(160, "bfloat16"),
    "ZB": _sb(160, "bfloat16"), "ID": _sb(128, "bfloat16"), "IH": _sb(128, "bfloat16"),
    "B0": _sb(128, "bfloat16"), "B1": _sb(128, "bfloat16"), "NB": _sb(128, "bfloat16"), "NU": _sb(128, "bfloat16"),
    "NI": _sb(128, "bfloat16"), "BF": _sb(128, "float32"), "P1": _sb(128, "bfloat16"), "P2": _sb(128, "bfloat16"),
}
for _t in range(2):
    SCRATCH["M%d" % _t] = _sb(YW_, "float32")
    SCRATCH["MV%d" % _t] = _sb(YW_, "bfloat16")
for _n in ("BN", "LG", "LN", "NM"):
    SCRATCH[_n] = _sb(RO * NG, "bfloat16")
PSUM = ("PD", "PK", "PL", "PG", "PN", "PS", "PY")
for _n in PSUM:
    SCRATCH[_n] = ("psum", [128, NV if _n == "PY" else 512], "float32")

SEMAPHORES = (["v", "s", "p", "g", "first", "sent", "d_y", "d_yt", "d_bd", "d_pt", "d_pr", "d_pa", "d_co", "d_mo", "o_a", "o_b", "o_c", "o_y", "o_f", "o_w"]
              + ["gh%d" % t for t in range(RO)] + ["nt%d" % t for t in range(RO)] + ["nn%d" % t for t in range(RO)])


def rank_program(g, core, T, topo):
    rank = T.rank_of(core)
    if rank is None:
        return
    V, S, P, Q = g.vector, g.scalar, g.tensor, g.sync
    eng = {"v": V, "s": S, "p": P, "g": g, "q": Q}
    count = {"v": 0, "s": 0, "p": 0, "g": 0}
    known = {e: {} for e in eng}
    clock = {}
    log = {}

    def c(name, a=0, b=None, step=1):
        b = SCRATCH[name][1][1] if b is None else b
        if step > 0:
            return {"ap": T[name][:, a:b:step] if step > 1 else T[name][:, a:b], "at": (name, a, b)}
        return {"ap": T[name][:, a:(b if b >= 0 else None):step], "at": (name, b + 1, a + 1)}

    def ind(win, off):
        return {"ap": win["ap"].indirect(off["ap"]), "at": win["at"], "off": off["at"]}

    def need(e, mark):
        sem, val = mark
        if known[e].get(sem, 0) >= val:
            return
        eng[e].wait_ge(T.sem[sem], val)
        known[e][sem] = val
        for k, x in clock.get(mark, {}).items():
            if known[e].get(k, 0) < x:
                known[e][k] = x

    def spans(outs, ins):
        ins = [x for x in ins if isinstance(x, dict)]
        return ([x["at"] for x in outs], [x["at"] for x in ins] + [x["off"] for x in outs + ins if "off" in x])

    def order(e, w, r, more=False):
        marks = {}
        for (name, a, b), writes in [(x, True) for x in w] + [(x, False) for x in r]:
            for lo, hi, m, wrote, q in log.get(name, []):
                meet = lo < b and a < hi and (writes or wrote) and not (more and q == e and name in PSUM)
                if meet or (name in PSUM and q != e and lo // 512 <= (b - 1) // 512 and a // 512 <= (hi - 1) // 512):
                    marks[m[0]] = max(marks.get(m[0], 0), m[1])
        for m in marks.items():
            need(e, m)

    def done(e, mark, w, r):
        clock[mark] = dict(known[e])
        for (name, a, b), writes in [(x, False) for x in r] + [(x, True) for x in w]:
            old = log.get(name, [])
            if name in PSUM:
                old = [x for x in old if x[4] == e or x[0] // 512 > (b - 1) // 512 or a // 512 > (x[1] - 1) // 512]
            old = [x for x in old if not (a <= x[0] and x[1] <= b and (writes or (x[4] == e and not x[3] and x[2][0] == mark[0])))]
            log[name] = old + [[a, b, mark, writes, e]]

    def op(e, outs, ins, call, more=False):
        w, r = spans(outs, ins)
        order(e, w, r, more)
        count[e] += 1
        call().then_inc(T.sem[e], 1)
        done(e, (e, count[e]), w, r)

    def raw(x):
        return x["ap"] if isinstance(x, dict) else x

    def mm(items, more=False):
        def call():
            for o, l, r, a, b in items[:-1]:
                P.matmul(o["ap"], l["ap"], r["ap"], a, b)
            o, l, r, a, b = items[-1]
            return P.matmul(o["ap"], l["ap"], r["ap"], a, b)
        op("p", [x[0] for x in items], [x[1] for x in items] + [x[2] for x in items], call, more)

    dmas = {}

    def dma(e, sem, outs, ins, pairs):
        w, r = spans(outs, ins)
        order(e, w, r)
        for o, i in pairs:
            eng[e].dma_start(o, i).then_inc(T.sem[sem], 16)
        dmas[sem] = 16 * len(pairs)
        done(e, (sem, dmas[sem]), w, r)

    peers = [T.cores[rank ^ d] for d in (1, 2, 3)]
    masks, used = [0, 0, 0], []
    for j in sorted(range(3), key=lambda j: len(topo.engines(core, peers[j]))):
        free = [x for x in topo.engines(core, peers[j]) if x not in used][:ENG[j]]
        used.extend(free)
        masks[j] = sum(1 << x for x in free)
    sent = [0]

    def exchange(src, land, t, sem, near=None):
        order("g", [], [(src, NG * t, NG * t + NG)])
        tr = []
        for j in range(3):
            rid, pid = topo.addr(peers[j], core)
            third = slice(NG * t + 64 * j, NG * t + 64 * j + 64)
            name = (near if near and j == 0 else sem) + str(t)
            tr.append(RemoteDMATransfer(dst_ids=[DstId(rid=rid, pnc=pid)], dma_engine_mask=masks[j], remote_sem=T.sem[name],
                                        srcs=[T[src][:, third]], dsts=[T[land][:, third]], alu_op=0))
        g.remote_dma_fused(tr, local_sem=T.sem["sent" if sent[0] else "first"])
        sent[0] += 1
        if near:
            log[land] = [[NG * t, NG * t + 64, (near + str(t), ENG[0]), True, "far"],
                         [NG * t + 64, NG * t + NG, (sem + str(t), ENG[1] + ENG[2]), True, "far"]]
        else:
            log[land] = [[NG * t, NG * t + NG, (sem + str(t), sum(ENG)), True, "far"]]

    def ts(out, in0, s1, o1, s2=None, o2=None):
        if o2 is None:
            op("v", [out], [in0, s1], lambda: V.tensor_scalar(out["ap"], in0["ap"], raw(s1), None, o1))
        else:
            op("v", [out], [in0, s1, s2], lambda: V.tensor_scalar(out["ap"], in0["ap"], raw(s1), raw(s2), o1, o2))

    def tt(out, a, b, o):
        op("v", [out], [a, b], lambda: V.tensor_tensor(out["ap"], a["ap"], b["ap"], o))

    def cp(out, a):
        op("v", [out], [a], lambda: V.tensor_copy(out["ap"], a["ap"]))

    def fill(out, x):
        op("v", [out], [], lambda: V.memset(out["ap"], x))

    def scan(out, a, b, o0, o1, first=0.0):
        op("v", [out], [a, b, first], lambda: V.tensor_tensor_scan(out["ap"], a["ap"], b["ap"], raw(first), o0, o1))

    def act(out, a, f, bias=None, scale=None, total=None):
        if total is not None:
            op("s", [out, total], [a], lambda: S.activation(out["ap"], a["ap"], f, bias=bias, scale=scale, accum_out=total["ap"]))
        elif bias is None:
            op("s", [out], [a], lambda: S.activation(out["ap"], a["ap"], f))
        else:
            op("s", [out], [a], lambda: S.activation(out["ap"], a["ap"], f, bias=bias, scale=scale))

    def times(out, a, x):
        act(out, a, F.Identity, 0.0, x)

    def iota(out, pat, base, cm=0):
        if SCRATCH[out["at"][0]][2] == "int32":
            op("g", [out], [], lambda: g.iota(out["ap"], pat, base, cm))
        else:
            op("g", [out], [], lambda: g.iota(out["ap"], pat, base, cm, allow_small_or_imprecise_dtypes=True))

    def clear(out):
        iota(out, [[0, out["at"][2] - out["at"][1]]], 0)

    def sel(out, a, pat, cmp, base, cm, other=0.0):
        op("g", [out], [a], lambda: g.affine_select(out["ap"], a["ap"], pat, cmp, other, base, cm))

    def narrow(out, a):
        sel(out, a, [[0, out["at"][2] - out["at"][1]]], A.is_equal, 0, 0)

    CL, NL, BD, KO = c("CL"), c("NL"), c("BD"), c("KO", 1, None, 2)
    ID, NI, B1, NU, IH = c("ID"), c("NI"), c("B1"), c("NU"), c("IH")

    def block(name, t):
        return c(name, NG * t, NG * t + NG)

    def turn(srcs, ps):
        mm([(c(ps, 64 * j, 64 * j + 64), c(("P1", "P2", "ID")[j]), c(n, a + 64 * j, a + 64 * j + 64), i == 0, i == len(srcs) - 1)
            for j in range(3) for i, (n, a) in enumerate(srcs)])

    def border(name, t, shift):
        act(block("BN", t), ind(c(name, 0, NV), BD), F.Relu, shift, 1.0)
        exchange("BN", "LG", t, "gh")
        act(c("AB"), block("BN", t), F.Relu, TAG, -0.012)

    def diagonal(name, first, final, blocks=False):
        mm([(c("PD", 0, 64), c("ZB", 16 - i, 144 - i), c(name, 64 * i, 64 * i + 64) if blocks else c(name, i, NV, 16),
             first and i == 0, final and i == 15) for i in range(16)], not first)

    def wanted(out):
        ts(out, c("PD", 0, 64), 16 * ROUND, A.add, 16 * (ROUND + 1.0), A.is_equal)

    def sums(out, name, a, b, lhs, first):
        return [(out, lhs, c(name, 16 * a + k, 16 * b, 16), first and k == 0, k == 15) for k in range(16)]

    def search_tables(n, numbers):
        mm([(c("PK", 0, 2 * n), ID, c("NE", 0, 2 * n), True, False), (c("PK", 0, 2 * n), ID, c("CJ", 0, 2 * n), False, False)])
        at, items = 0, []
        for a, b in numbers:
            items.append((c("PN", at, at + b - a), IH, c("SF", a, b), at == 0, False))
            at += b - a
        mm(items)

    def search(w, e, n, z, slots, out, on_scalar, wait, wrap=0):
        W = c(w, 0, n)
        scan(c(e, 1, n + 1), W, W, A.add, A.max)
        mm([(c("PN", 0, n), B1, W, False, False), (c("PN", 0, n), NU, W, False, True)], True)
        mm([(c("PK", 0, 2 * n, 2), c("B2"), W, False, False), (c("PK", 1, 2 * n, 2), B1, c(e, 0, n), False, True)], True)
        if wrap:
            mm([(c("PN", 128, 129), B1, c(e, wrap, wrap + 1), True, True)])
        wait("B")
        if on_scalar:
            act(c("PAY", 0, n), c("PN", 0, n), F.Identity, 1024.5 - DELTA / 2, -DELTA)
        scan(c("PP", 0, 2 * n), c("H0", 0, 2 * n), c("PK", 0, 2 * n), A.max, A.min)
        if not on_scalar:
            ts(c("PAY", 0, n), c("PN", 0, n), -DELTA, A.mult, 1024.5 - DELTA / 2, A.add)
        wait("B2")
        cp(c("ZL", 0, n // 16), c("PP", 31, 2 * n, 32))
        if wrap:
            ts(c("WI"), c("SG"), c("PN", 128, 129), A.is_ge, -float(RINGN), A.mult)
        wait("B3")
        cp(ind(c(z), c("ZL", 0, n // 16)), c("PAY", 0, n))
        wait("B4")
        scan(c("X", 0, slots), c(z, Z0_, Z0_ + slots), c("DL", 0, slots), A.max, A.add)
        o = c("PS", 0, slots // 16)
        mm([(o, ID, c("WI"), True, False)] * min(wrap, 1)
           + [(o, c("ZB", 16 - i, 144 - i), c("X", i, slots, 16), i == 0 and not wrap, i == 15) for i in range(16)])
        wait("C")
        ts(out, o, -16384.0, A.add)

    def ring_out(x):
        if x == "y":
            tt(ind(c("OY", RING0), CL), KO, c("OM"), A.add)
            dma("q", "o_y", [], [c("OY", RING0, 896)], [(T.yy[:, RING0:896], T.OY[:, RING0:896])])
        else:
            tt(ind(c("OF", RING0), CL), c("FF"), c("FR"), A.mult)
            dma("s", "o_f", [], [c("OF", RING0, 896)], [(T.yf[:, RING0:896], T.OF[:, RING0:896])])

    dma("s", "d_bd", [c("BDI")], [], [(T.BDI[:, :], T.bd[:, :])])
    if TAIL_FIRST:
        dma("q", "d_yt", [c("Y0", 896, NV)], [], [(T.Y0[:, 896:NV], T.y0[:, 896:NV])])
        dma("s", "d_pt", [c("PR", 896, NV)], [], [(T.PR[:, 896:NV], T.pr[:, 896:NV])])
        dma("q", "d_y", [c("Y0", 0, 896)], [], [(T.Y0[:, 0:896], T.y0[:, 0:896])])
    else:
        dma("q", "d_y", [c("Y0", 0, NV)], [], [(T.Y0[:, 0:NV], T.y0[:, :])])
        dma("q", "d_pt", [c("PR", 896, NV)], [], [(T.PR[:, 896:NV], T.pr[:, 896:NV])])
    dma("q", "d_pr", [c("PR", RING0, 896)], [], [(T.PR[:, RING0:896], T.pr[:, RING0:896])])

    fill(c("ONE"), 1.0)
    act(c("TAG"), c("ONE"), F.Silu, 0.0, 0.0039025)
    iota(c("DS"), [[1, 128]], DUMP)
    sel(c("B0"), c("ONE", 0, 128), [[-1, 8], [0, 16]], A.is_equal, 0, 1)
    sel(ID, c("ONE", 0, 128), [[-1, 128]], A.is_equal, 0, 1)
    mm([(c("PG", 0, 128), c("B0"), c("B0"), True, True)])
    ramp0 = max(128 - S_SLOTS[0], DUMP // 16)
    ramp_low = -float(STEP * (RAMP // 2 + 1))
    fill(c("R0", 0, 16 * ramp0), 0.0)
    fill(c("SIL"), SILU_ONE)
    cp(B1, c("PG", 0, 128))
    ts(c("NB"), c("PG", 0, 128), -1.0, A.mult)
    fill(c("ZB"), 0.0)
    fill(c("MV0", 0, DUMP), 0.0)
    for h, z in ((0, "Z0"), (1, "Z1")):
        sel(c(z), c("ONE", 0, 160), [[-32, 5], [984, 2], [-1, 16]], A.is_equal, 16 - 1000 * (1 - h), 1)
    sel(NU, c("NB"), [[-1, 128]], A.is_gt, 0, 1)
    iota(c("XI"), [[0, 5], [1, 16], [0, 2]], 0)
    iota(c("SF"), [[1, 112]], 0)
    times(c("M0", 0, DUMP), c("R0", 0, DUMP), 0.0)
    cp(BD, c("BDI"))
    times(IH, ID, -256.0)
    times(c("B2"), B1, 2048.0)
    act(block("BN", 0), ind(c("Y0", 0, NV), BD), F.Relu, 2.0 - GHOST, 1.0)
    exchange("BN", "LG", 0, "gh")
    need("q", ("first", sum(ENG)))
    dma("q", "d_co", [c("CO", 0, RINGN)], [], [(T.CO[:, 0:RINGN], T.co[:, RING0:896])])
    dma("q", "d_mo", [c("MO", 0, RINGN)], [], [(T.MO[i:128:16, 0:RINGN], T.mo[:, RING0:896]) for i in range(16)])
    dma("q", "d_pa", [c("PR", 0, RING0)], [], [(T.PR[:, 0:RING0], T.pr[:, 0:RING0])])

    for t in range(RO):
        M, MV, MW = "M%d" % (t % 2), "MV%d" % (t % 2), "MV%d" % ((t + 1) % 2)
        Y, YN = ("YA", "YB")[t % 2], ("YB", "YA")[t % 2]
        last, later = t == RO - 1, min(t, 1)
        ns = 128 if t == 0 else 256
        sn = S_SLOTS[later]
        vn = ns - sn
        kc = ns // 16
        s0 = (9 * t) % 40
        ring = [(s0, 40)] + ([(0, s0)] if s0 else [])
        fills = FILL[later]
        turns = TURNS[later]
        defer = DEFER[later]
        odd_s = ODD_S and t > 0
        cut = max([0] + [EARLY[x][1] for v in fills.values() for x in v if x in EARLY]) if turns else 0
        at = [ns - sum(x for v in fills.values() for x in v if isinstance(x, int))]
        s_end = at[0]

        def naming(e, a, b):
            while a < b:
                x = min(b, (a // kc + 1) * kc)
                if e == "s":
                    k = a // kc
                    act(ind(c("MB" if k % 2 and k < 2 * turns else M), c("L", a, x)), c("SIL", 0, 16 * (x - a)), F.Silu)
                    if turns and k == 2 * turns and not YT_G[later]:
                        times(c("YT", cut), c("MB", cut, DUMP), 1.0)
                else:
                    cp(ind(c(MV), c("L", a, x)), c("TAG", 0, 16 * (x - a)))
                a = x

        def spread(a, b, low, high):
            o = c("PL", 256 + a, 256 + b)
            mm(([(o, c("I32"), c("FL", a, b), True, False)] if defer else
                [(o, ID, c("ONE", 0, b - a), i == 0, False) for i in range(2 - later)])
               + [(o, NI, low, False, False), (o, ID, high, False, True)])

        def spreads():
            spread(0, sn, c("MNS", 15, 16 * sn, 16), c("MXS", 15, 16 * sn, 16))
            spread(sn, ns, c("MN", 0, 8 * vn, 8), c("MX", 7, 8 * vn, 8))

        def greatest(x):
            if x == "x":
                scan(c("MX", 0, 8 * vn), c("G", 0, 16 * vn, 2), c("G", 1, 16 * vn, 2), A.max, A.max, -4000.0)
            else:
                a, b = (0, 16 * sn) if x == "X" else (16 * (sn * int(x[1]) // PARTS), 16 * (sn * (int(x[1]) + 1) // PARTS))
                scan(c("MXS", a, b), c("K3", a, b), c("GS", a, b), A.min, A.max)

        def wait(j):
            if t and j == "B" and PY_EARLY:
                mm([(c("PY", 512), ID, c(Y, 512, NV), True, False)])
            for x in fills.get(j, []):
                if x == "G":
                    ghosts0()
                elif str(x)[0] in "xX":
                    greatest(x)
                elif x in EARLY:
                    if turns:
                        a, b = EARLY[x]
                        tt(c("YT", a, b), c("PY", a, b), c("MB", a, b), A.max)
                else:
                    naming("v", at[0], at[0] + x)
                    at[0] += x

        def ring_search():
            x = 0
            for a, b in ring:
                ts(c("WR", x, x + b - a), c("PD", 16 + a, 16 + b), 32.0 * later - 8.0, A.is_ge)
                x += b - a
            wait("W")
            search("WR", "ER", NR, "ZR", K2, CL, False, wait, 40 - s0)

        if t == 0:
            ts(c("C0"), c("Y0", 896, NV), 0.0, A.is_ge, 2000.0, A.mult)
            ts(c("YA", 896, NV), c("Y0", 896, NV), 2.0, A.add)
            tt(c("C1"), c("C0"), c("DS"), A.min)
            cp(c("ZB", 16, 144, 16), c("B1", 0, 128, 16))
            tt(c("C", 0, 128), c("C1"), c("PR", 896, NV), A.max)
            fill(c("CJ"), float(Z0_))
            Y = "Y0"
        else:
            search_tables(NC, [(0, 64), (76, 92)])
            tt(ind(c("PH"), CL), c("FF"), c("FF"), A.add)
            wanted(c("W", 0, 64))
            rest = c("R0", 16 * ramp0, 16 * RAMP)
            search("W", "E", NC, "Z", 256, NL, True, lambda j: t == 1 and j == "C" and ramp0 < RAMP and scan(
                c("RA", 16 * ramp0, 16 * RAMP), rest, rest, A.add, A.add, ramp_low + STEP * ramp0))
            turn([("LG", NG * t)], "PG")
            act(c(Y, NV, DUMP), c("PG", 0, NG), F.Identity, GHOST, 1.0)
            if t == 1:
                ts(c("R2", 0, RAMP), c("RA", 0, 16 * RAMP, 16), 2.0, A.add)
            if LS_MODE == 0:
                cp(c("LS", 0, sn), ind(c("PR"), c("NL", 0, sn // 16)))
                cp(c("LS", sn, ns), ind(c("PR"), c("NL", sn // 16, 16)))
                ts(c("C", 0, sn), c("LS", 0, sn), 0.0, A.add)
                ts(c("C", sn, ns), c("LS", sn, ns), 0.0, A.add)
            elif LS_MODE == 1:
                cp(c("LS"), ind(c("PR"), NL))
                ts(c("C"), ind(c("PR"), NL), 0.0, A.add)
                tt(c("G", 0, 16 * V_ZERO), ind(c(Y), c("LS", sn, sn + V_ZERO)), c("RA", 0, 16 * V_ZERO), A.add)
            else:
                cp(c("LS", 0, sn), ind(c("PR"), c("NL", 0, sn // 16)))
                ts(c("C"), ind(c("PR"), NL), 0.0, A.add)
                cp(c("LS", sn, ns), ind(c("PR"), c("NL", sn // 16, 16)))
        op("v", [c("CT", 0, ns)], [c("C", 0, ns)], lambda: V.transpose(T.CT[:, 0:ns], T.C[:, 0:ns]))
        items = []
        for b in range(ns // 32):
            for h in (0, 1):
                for gg in (0, 1):
                    x = 16 - 16 * (gg - h)
                    items.append((c("PL", 2 * b + h, ns, kc), c("Z%d" % h, x, x + 128),
                                  c("CT", 32 * b + 16 * gg, 32 * b + 16 * gg + 16), gg == 0, gg == 1))
        mm(items)

        def gather_s():
            if sn:
                act(c("GS", 0, 16 * sn), ind(c(Y), c("LS", 0, sn)), F.Identity, 0.0, 1.0)

        def gather_v(a, b):
            if a < b:
                tt(c("G", 16 * a, 16 * b), ind(c(Y), c("LS", sn + a, sn + b)), c("RA", 16 * a, 16 * b), A.add)

        fl_at = None if defer else FL_AT[later]
        if t == 0:
            mm([(c("PG", 384, 385), B1, c("ONE", 0, 1), True, False), (c("PG", 384, 385), NU, c("ONE", 0, 1), False, True)])
            iota(c("CJ", 0, None, 2), [[1, NC]], 1)
            sel(c("P1"), c("ONE", 0, 128), [[16, 8], [-1, 16]], A.is_equal, -112, 1)
            sel(c("P2", 16, 128), c("ONE", 16, 128), [[16, 7], [-1, 16]], A.is_equal, -112, 1)
            sel(c("P2", 0, 16), c("ONE", 0, 16), [[-1, 16]], A.is_equal, 0, 1)
            ts(c("LS", 0, ns), c("C", 0, ns), 0.0, A.add)
            fill(c("H0"), 0.0)
            fill(c("WR", 40), 1.0)
            fill(c(Y, DUMP, DUMP + ns), -1.0)
            ts(c("L", 0, ns), c("PL", 0, ns), 0.0, A.add)
            ts(c("CC"), c("PG", 384, 385), -1.0, A.add)
            diagonal(Y, True, True)
            between = [lambda: act(c("AB"), block("BN", 0), F.Relu, TAG, -0.012), lambda: times(NI, ID, -1.0), lambda: times(c("IT"), ID, TAG),
                       lambda: times(c("BF"), B1, -32.0), lambda: times(c("DL", 0, K2), c("ONE", 0, K2), DELTA),
                       lambda: times(c("CX"), c("ONE", 0, 1), -0.9375), lambda: times(c("ER", 0, 1), c("ONE", 0, 1), 0.0),
                       lambda: times(c("ZR", Z0_, Z0_ + K2), c("ONE", 0, K2), 0.0)]

            def names0(a, b):
                for k in range(a, b, kc):
                    naming("s", k, min(k + kc, b))
                    if between:
                        between.pop()()

            def ghosts0():
                turn([("LG", 0)], "PG")
                ts(c(Y, NV, DUMP), c("PG", 0, NG), GHOST - 2.0, A.add)
                if T0_AT * kc < s_end:
                    gather_s()
                    names0(T0_AT * kc, s_end)
                times(c("YT", YT_G[0]), c(M, YT_G[0], DUMP), 1.0)
                if YT_G[0]:
                    narrow(c("YT", 0, YT_G[0]), c(M, 0, YT_G[0]))
                if T0_AT * kc >= s_end:
                    gather_s()
                gather_v(0, vn)

            names0(0, min(T0_AT * kc, s_end))
            setup = [lambda: ts(c("NE"), c("XI"), c("CC"), A.not_equal, BIG, A.mult),
                     lambda: ts(c("H0", 0, None, 2), c("XI", 0, None, 2), c("CC"), A.is_equal, BIG, A.mult),
                     lambda: ts(c("SG"), c("SF", 0, K2, 16), c("CC"), A.add),
                     lambda: fill(c("R0", 0, 16 * ramp0, 16), STEP / 2.0),
                     lambda: scan(c("RA", 0, 16 * ramp0), c("R0", 0, 16 * ramp0), c("R0", 0, 16 * ramp0), A.add, A.add, ramp_low)]
            for j, f in enumerate(setup):
                f()
                wait("L%d" % j)
            search_tables(NR, [(s0, s0 + 40), (100, 108)])
            if sn:
                iota(c("K2", 0, 16 * sn), [[0, sn], [-40, 16]], 32)
            iota(c("PR", DUMP, DUMP + K2), [[1, K2]], DUMP)
            if sn:
                iota(c("K3", 0, 16 * sn), [[0, sn], [40, 16]], -8)
            iota(c("CO", TW - K2), [[0, K2]], YW_ - 1)
            iota(c("MO", TW - K2), [[0, K2]], 0)
            ring_search()
            wait("Z")
            turn([("YT", NV), (MV, NV)], "PN")
            for a, b in ((512, 896), (0, 512)):
                mm([(c("PY", a, b), c("IT") if n == "YT" else ID, c(n, a, b), n == Y, n == "YT") for n in (Y, MV, "YT")])
            act(block("NM", t), c("PN", 0, NG), F.Sign, 0.0, 1.0)
            exchange("NM", "LN", t, "nt", "nn")
            act(c(YN, 0, 896), c("PY", 0, 896), F.Identity, 2.0, 1.0021)
            act(c(YN, NV, DUMP), c(Y, NV, DUMP), F.Identity, 2.0, 1.0)
            times(c("I32"), ID, 32.0)
            iota(c(YN, DUMP), [[0, 256]], 1)
            cp(c("PRL"), ind(c("PR", RING0), CL))
        else:
            gather_s()
            gather_v(V_ZERO if LS_MODE == 1 else 0, min(vn, V_FIRST))
            ts(c("L"), c("PL", 0, ns), 0.0, A.add)
            naming("s", 0, s_end if fl_at is None else fl_at * kc)
            gather_v(V_FIRST, vn)
            search_tables(NR, [(s0, s0 + 40), (100, 108)])
            clear(c("ZR", Z0_, Z0_ + K2))
            if not last:
                clear(c("Z", Z0_, Z0_ + 256))
            clear(c(MW, 0, DUMP))
            if YT_G[later] and turns and t == 1:
                narrow(c("YT", NV), c("MB", NV, DUMP))
                narrow(c("YT", 0, NV), c("MB", 0, NV))
            if not last:
                clear(c("M%d" % ((t + 1) % 2), 0, DUMP))
            else:
                clear(c("OF", 0, RING0))
                clear(c("OF", 896, NV))
                dma("q", "o_b", [], [c("OF", 0, RING0), c("OF", 896, NV)],
                    [(T.yf[:, 0:RING0], T.OF[:, 0:RING0]), (T.yf[:, 896:NV], T.OF[:, 896:NV])])
            if YT_G[later] and turns and t > 1:
                narrow(c("YT", NV), c("MB", NV, DUMP))
                narrow(c("YT", 0, NV), c("MB", 0, NV))
            wait("g")

        least = c("PG", 256, 256 + ns)
        if defer:
            for x in MINS[later]:
                if x == "N":
                    scan(c("MNS", 0, 16 * sn), c("K2", 0, 16 * sn), c("GS", 0, 16 * sn), A.max, A.min)
                elif x == "n":
                    scan(c("MN", 8 * vn - 1, -1, -1), c("G", 16 * vn - 1, -1, -2), c("G", 16 * vn - 2, -1, -2), A.min, A.min, 4000.0)
                elif x == "F":
                    ts(c("FL", 0, sn), c("MNS", 15, 16 * sn, 16), 2.0 * later, A.is_ge)
                elif x == "f":
                    tt(c("FL", sn, ns), c("MN", 0, 8 * vn, 8), c("R2", 0, vn) if t else c("RA", 0, 16 * vn, 16), A.is_ge)
                elif x == "c":
                    cp(c("COL"), ind(c("CO"), CL))
                elif x == "o":
                    cp(c("OI"), ind(c(Y, RING0), CL))
                elif x == "d":
                    ts(c("OD"), c("OI"), 1, A.bitwise_and)
                else:
                    wait(x)
            wait("s")
            if t:
                tt(ind(c(Y), NL), c("FL"), c("ONE"), A.add)
            else:
                tt(c(YN, 896, NV), c("FL", 0, ns), c("YA", 896, NV), A.add)
                Y = YN
        for x in "" if defer else SCANS[later] if sn else "nx":
            if x == "n":
                scan(c("MN", 8 * vn - 1, -1, -1), c("G", 16 * vn - 1, -1, -2), c("G", 16 * vn - 2, -1, -2), A.min, A.min, 4000.0)
                mm([(c("PG", 256 + sn, 256 + ns), ID, c("MN", 0, 8 * vn, 8), True, False),
                    (c("PG", 256 + sn, 256 + ns), NI, c("RA", 0, 16 * vn, 16), False, True)])
            elif x == "N":
                scan(c("MNS", 0, 16 * sn), c("K2", 0, 16 * sn), c("GS", 0, 16 * sn), A.max, A.min)
                mm([(c("PG", 256, 256 + sn), ID, c("MNS", 15, 16 * sn, 16), True, True)])
            elif x == "x":
                scan(c("MX", 0, 8 * vn), c("G", 0, 16 * vn, 2), c("G", 1, 16 * vn, 2), A.max, A.max, -4000.0)
                spread(sn, ns, c("MN", 0, 8 * vn, 8), c("MX", 7, 8 * vn, 8))
            else:
                scan(c("MXS", 0, 16 * sn), c("K3", 0, 16 * sn), c("GS", 0, 16 * sn), A.min, A.max)
                spread(0, sn, c("MNS", 15, 16 * sn, 16), c("MXS", 15, 16 * sn, 16))
            if fl_at is not None and x == [y for y in SCANS[later] if y in "nN"][-1]:
                act(c("FL", 0, ns), least, F.Relu, -96.0, 64.0)
                naming("s", fl_at * kc, s_end)
            wait(x)
        if fl_at is None and not defer:
            ts(c("FL", 0, ns), least, 2.0 * later, A.is_ge, 32.0, A.mult)
        if t == 0 and not defer:
            cp(c("COL"), ind(c("CO"), CL))
        if not defer:
            wait("r")
            tt(c("RES", 0, ns), c("PL", 256, 256 + ns), c("FL", 0, ns), A.min)
        if defer:
            pass
        elif t == 0:
            cp(c("OI"), ind(c(Y, RING0), CL))
            tt(c(YN, 896, NV), c("RES", 0, ns), c("YA", 896, NV), A.max)
            ts(c("OD"), c("OI"), 1, A.bitwise_and)
            Y = YN
        else:
            wait("s")
            tt(ind(c(Y), NL), c("RES"), c("ONE"), A.add)

        def dirty(a, b):
            if a < b:
                act(c("DG", 16 * a, 16 * b), ind(c(Y), c("PRL", a, b)), F.Relu, 4.0, -2.0)

        dv, d2, run = D_V[later]
        diagonal(Y, True, True)
        if t:
            mm([(c("PY", 0, 512), ID, c(Y, 0, 512), True, cut > 0)])
            wait("A")
            ring_search()
            if not PY_EARLY:
                mm([(c("PY", 512), ID, c(Y, 512, NV), True, False)])
            act(c("NN"), c(M, NV, DUMP), F.Identity, 0.0, 1.0)
            wait("C2")
            if defer and RES_ON == "e":
                spreads()
            cp(c("PRL"), ind(c("PR", RING0), CL))
            wait("D0")
            act(c("SN"), c("PD", 0, 64), F.Sign, -24.0, 1.0, c("CN"))
            if defer and RES_ON == "e":
                act(c("RES"), c("PL", 256, 512), F.Relu, -31.0, 1.0)
            if odd_s:
                act(c("O1"), ind(c(Y, RING0), CL), F.Identity, 0.0, 1.0)
                act(c("OM"), ind(c("MF"), CL), F.Identity, 0.0, 1.0)
                act(c("O2"), c("O1"), F.Identity, 127.75, 0.5)
                cp(c("COL"), ind(c("CO"), CL))
            else:
                cp(c("OI"), ind(c(Y, RING0), CL))
                cp(c("COL"), ind(c("CO"), CL))
                ts(c("OD"), c("OI"), 1, A.bitwise_and)
        if not (defer and t):
            act(c("OC"), ind(c(Y, RING0), CL), F.Identity, 0.0, 1.0)
        dirty(dv, d2)
        wait("D")
        if t == 0:
            act(c("SN"), c("PD", 0, 64), F.Sign, -24.0, 1.0, c("CN"))
        elif cut:
            mm([(c("PY", 512), ID, c("YT", 512, NV), False, False), (c("PY", 0, 512), ID, c("YT", 0, 512), True, False),
                (c("PY", cut, 512), ID, c(Y, cut, 512), False, False)])
        elif turns:
            mm([(c("PY", a, a + 512), c("IT"), c("YT", a, a + 512), False, False) for a in (512, 0)])
        if t:
            if TURN_FIRST:
                turn([(x, NV) for x in ["YT"] * min(turns, 1) + [MV]] + [("NN", 0)], "PN")
            mm([(c("PY", a, a + 512), ID, c(MV, a, a + 512), False, True) for a in (512, 0)], True)
            if not TURN_FIRST:
                turn([(x, NV) for x in ["YT"] * min(turns, 1) + [MV]] + [("NN", 0)], "PN")
            act(block("NM", t), c("PN", 0, NG), F.Sign, 0.0, 1.0)
            exchange("NM", "LN", t, "nt", "nn")
        if t == 0:
            clear(c(MW, 0, DUMP))
            iota(c("CF", 0, None, 2), [[0, K2]], 8192)
            iota(c("PR", DUMP + K2), [[1, 256 - K2]], DUMP + K2)
            clear(c("Z", Z0_, Z0_ + 256))
            clear(c("PH", 0, RINGN))
            clear(c("M1", 0, DUMP))
        elif not last:
            clear(c("MB", 0, DUMP))
        if defer and t and RES_ON != "e":
            spreads()
        left = c("PS", 480, 481)
        mm([(left, c("BF"), c("CX"), True, False), (left, c("BF"), c("CN"), False, True)])
        def dirty_sums(a, b):
            o = c("PS", a, b)
            more = [(o, c(l), c(n, a, b), n == "O1", False) for l, n in (("I64", "O1"), ("I64", "OM"), ("IN", "O2"))] if odd_s else []
            mm(more + sums(o, "DG", a, b, ID, not odd_s))

        late = D_LATE if t else 0
        if late < dv:
            ts(c("DG", 16 * late, 16 * dv), ind(c(Y), c("PRL", late, dv)), 2.0, A.is_lt)
        dirty(d2, run)
        if not late:
            dirty_sums(0, run)
        dirty(max(d2, run), K2)
        if defer and t and RES_ON == "s":
            act(c("RES"), c("PL", 256, 512), F.Relu, -31.0, 1.0)
        wait("E")
        if t:
            tt(c(YN, 0, NV), c("PY"), c(M, 0, NV), A.max)
        if late:
            ts(c("DG", 0, 16 * late), ind(c(Y), c("PRL", 0, late)), 2.0, A.is_lt)
            dirty_sums(0, run)
        if not odd_s:
            tt(c("OM"), ind(c("MO"), CL), c("OD"), A.mult)
        if defer and RES_ON == "v":
            ts(c("RES"), c("PL", 256, 512), -31.0, A.add, 0.0, A.max)
        if last:
            mm([(c("PY", a, b), l, c(n, x + a, x + b), n == "PH", n != "PH")
                for a, b in ((0, 512), (512, RINGN)) for l, n, x in ((ID, "PH", 0), (NI, YN, RING0))])
        dirty_sums(run, K2)
        held = c("PK", 256, 256 + 2 * K2, 2)
        if not (defer and t):
            mm([(c("PK", 257, 256 + 2 * K2, 2), ID, c("OC"), True, True)])
        for a, x, b in H_V[later]:
            act(c("HG", 16 * x, 16 * b), ind(c(YN), c("COL", x, b)), F.Silu, 318.75, -320.0)
            ts(c("HG", 16 * a, 16 * x), ind(c(YN), c("COL", a, x)), 1.0, A.is_equal, -0.25, A.mult)
            o = c("PK", 256 + 2 * a, 256 + 2 * b, 2)
            mm([(o, ID, c("ONE", 0, b - a), True, False)] + sums(o, "HG", a, b, IH, False))
        if odd_s:
            ts(c("FF"), c("PS", 0, K2), 128.0 - 16384.0, A.is_gt)
        else:
            tt(c("FF"), c("PS", 0, K2), c("OM"), A.min)
        mm([(c("PG", 256, 256 + K2), B1, c("FF"), True, True)])
        if defer and t:
            tt(ind(c(YN), NL), c("RES"), c("ONE"), A.add)
            act(c("OC"), ind(c(YN, RING0), CL), F.Identity, 0.0, 1.0)
        elif defer:
            greatest("x")
            greatest("X")
            spreads()
            act(c("RES", 0, ns), c("PL", 256, 256 + ns), F.Relu, -31.0, 1.0)
        if last:
            act(c("OF", RING0, 896), c("PY", 0, RINGN), F.Relu, -0.001, 1.0)
        act(c("A8"), c("PG", 256, 256 + K2), F.Abs, -8.0, 1.0)
        act(c("CD"), c("A8"), F.Silu, -1600.006, 200.0)
        if t == 0:
            times(c("YA", DUMP), c("ONE"), 1.0)
            times(c("YA", NV, DUMP), c("ONE", 0, NG), GHOST)
            times(c("DL", K2), c("ONE", K2), DELTA)
            if ODD_S:
                times(c("I64"), ID, 64.0)
                times(c("IN"), ID, -128.0)

        def values_out(j):
            for x in OUT_AT.get(j, "") if last else "":
                if x == "r":
                    ts(c("OY", RING0, 896), c(YN, RING0, 896), -2.0, A.add, -1.0, A.max)
                else:
                    a, b = (0, RING0) if x == "a" else (896, NV)
                    ts(c("Y0", a, b), c(YN, a, b), -2.0, A.add, -1.0, A.max)
                    dma("q", "o_" + x, [], [c("Y0", a, b)], [(T.yy[:, a:b], T.Y0[:, a:b])])

        def notices(j):
            values_out(j)
            if j in NOTES:
                a, b = NOTES[j]
                tt(ind(c(MW, 0, NV), c("BD", a // 16, b // 16)), c("LN", NG * t + a, NG * t + b), c("AB", a, b), A.mult)
                if j == max(NOTES):
                    diagonal(MW, True, False, last)

        if t == 0:
            fill(c("W", 64), 1.0)
            fill(c("E", 0, 1), 0.0)
            if ODD_S:
                cp(c("MF", 0, RINGN), c("MO", 0, RINGN))
                fill(c("MF", TW - K2), 0.0)
        notices(0)
        ts(c("FR"), held, 2.0, A.is_lt, 32.0, A.mult)
        if defer and t:
            mm([(c("PK", 257, 256 + 2 * K2, 2), ID, c("OC"), True, True)])
        notices(1)
        if last:
            fill(c("OM"), -2.0)
        scan(c("CF", 1, None, 2), c("FR"), c("FR"), A.add, A.add, left)
        notices(2)
        scan(c("KO"), c("CF"), c("PK", 256, 256 + 2 * K2), A.max, A.min)
        notices(3)
        if defer and t == 0:
            tt(c(YN, 896, NV), c("RES", 0, ns), c("YA", 896, NV), A.add)
        if last:
            ts(c("FR"), KO, 2.0, A.is_lt)
            for x in TAIL:
                ring_out(x)
        tt(ind(c(YN, RING0), CL), KO, c("CD"), A.add)
        diagonal(YN, False, True, last)

        if not last:
            border(YN, t + 1, -GHOST)
            if t == 0 and ramp0 < RAMP:
                times(c("R0", 16 * ramp0, 16 * RAMP), c("R0", 0, 16 * (RAMP - ramp0)), 1.0)
            if t == 0:
                clear(c("MB", 0, DUMP))
                iota(c("K2", 16 * sn, 16 * S_SLOTS[1]), [[0, S_SLOTS[1] - sn], [-40, 16]], 32)
                iota(c("K3", 16 * sn, 16 * S_SLOTS[1]), [[0, S_SLOTS[1] - sn], [40, 16]], -8)

    for x in "yf":
        if x not in TAIL:
            ring_out(x)
    wanted(c("OW"))
    dma("q", "o_w", [], [c("OW")], [(T.yw[:, :], T.OW[:, :])])
    g.wait_ge(T.sem.sent, (sent[0] - 1) * sum(ENG))
    for sem, n in list(count.items()) + list(dmas.items()):
        need("q", (sem, n))
